import numpy as np, ml_dtypes
CORES = [23,119,17,113]
N = 4
import mx_ref
BF = ml_dtypes.bfloat16
def gcols(t, e):
    v = np.concatenate([t.reshape(8, 16, -1, 4), np.zeros((8, 16, 1, 4), BF)], axis=2)
    return np.ascontiguousarray(np.stack([v[g][:, e[g]] for g in range(8)])).reshape(128, -1)
def tile(rs):
    return np.stack(rs, axis=2).reshape(128, -1).astype(BF)
def pick(q, e):
    c = np.concatenate([q[0].reshape(128, -1, 4), np.zeros((128, 1, 4), np.uint8)], axis=1); s = np.concatenate([q[1], np.ones((16, 1), np.uint8)], axis=1)
    return (np.ascontiguousarray(c[:, e].reshape(128, -1)), np.ascontiguousarray(s[:, e]))
def join(*qs):
    return (np.concatenate([q[0] for q in qs], axis=1), np.concatenate([q[1] for q in qs], axis=1))
def put(q, e, v):
    c, s = q[0].reshape(128, -1, 4).copy(), q[1].copy(); c[:, e] = v[0].reshape(128, -1, 4); s[:, e] = v[1]
    return (c.reshape(128, -1), s)
def pk(c, s):
    return (np.ascontiguousarray(c), mx_ref.live(s))
def emit(q):
    return q[0], q[1]
def packed(v, rng):
    q = [mx_ref.quantize(np.ascontiguousarray(v[r])) for r in range(N)]
    return np.stack([a for a, b in q]), np.stack([mx_ref.plane(b, rng) for a, b in q])
def values_of_codes():
    e, c = np.zeros((128, 128, 4), np.float32), np.zeros((128, 2, 4), np.uint8)
    e[np.arange(128), np.arange(128), 0] = 1
    c[:127, :, 0] = np.arange(256).reshape(2, 128).T[:127]
    return mx_ref.matmul(mx_ref.quantize(e.reshape(128, 512).astype(BF)), (c.reshape(128, 8), np.full((16, 2), 127, np.uint8))).T.reshape(-1).astype(np.float64)
CODE_VALUE, SCALE_VALUE = values_of_codes(), 2.0 ** (np.arange(256) - 127.0)
def decode(q):
    return (CODE_VALUE[q[0]].reshape(16, 8, -1, 4) * SCALE_VALUE[q[1]][:, None, :, None] + 0.0).reshape(128, -1).astype(np.float32)
def f(rng, *shape):
    return mx_ref.flush((rng.standard_normal(shape, dtype=np.float32) * np.exp2(rng.integers(-2, 3, shape[:-1] + (1,)))).astype(BF))
def wide(rng, *shape, cols=0):
    v = rng.standard_normal(shape, dtype=np.float32) * np.exp2(rng.integers(-12, 13, shape)).astype(np.float32)
    if cols: v *= np.repeat(np.exp2(rng.integers(-cols, cols + 1, shape[:-2] + (1, shape[-1] // 4))) * (rng.random(shape[:-2] + (1, shape[-1] // 4)) > 0.0625), 4, axis=-1).astype(np.float32)
    return mx_ref.flush(v.astype(BF))
C, B, K, R = 320, 20, 128, 3
def numbers_of(rng):
    return {"x": np.array(f(rng, N, 128, 4 * C)), "u": np.array(f(rng, N, 128, 512)), "v": np.array(f(rng, N, 128, 512))}
def layers(rng):
    return np.array(f(rng, N, 128, 2048)).reshape(N, 8, 16, 4, 8, 16, 4)
def weights(rng, w):
    c, p = packed(np.ascontiguousarray(w).reshape(N, 128, 2048), rng)
    return {"wc": c, "ws": p}
def lone(u, k, k2=0.0):
    a = u.reshape(N, 128, 128, 4)
    a[:, :, ::16] = 0
    for h in range(0, 128, 16):
        a[:, h, h, 0] = np.asarray(k, np.float32).astype(BF)
        a[:, h + 1, h, 0] = np.asarray(k2, np.float32).astype(BF)
    return a.reshape(N, 128, 512)
def setup_inputs(rng):
    return {**numbers_of(rng), **weights(rng, layers(rng))}
def setup_inputs_ties(rng):
    d = numbers_of(rng)
    m = C // B
    k = (rng.permutation(m) % 5)[:, None]
    one = 1 << rng.integers(0, 8, (N // 2, 2, m, B))
    two = one | (1 << rng.integers(0, 8, one.shape))
    w = np.where(k == 0, one * rng.integers(0, 2, one.shape), np.where(k == 3, two, 0))
    each = 1 << (np.arange(B) % 8)
    w[:, 0] += np.where(k == 2, each, 0)
    w[:, 1] += np.where(k == 4, each, 0)
    w = (w ^ rng.integers(0, 256, 4)[rng.integers(0, 4, (N // 2, 1, m, 1))]).reshape(N, 1, C)
    x = np.zeros((N, 8, 16, C, 4), np.float32)
    x[:, :, 0, :, 0] = ((w >> np.arange(8)[:, None]) & 1) * 2.0 - 1.0
    z = (N, 8, 8, C, 4)
    x[:, :, 8:] = (1.0 + (2 * rng.integers(0, 64, z) + 1) * 2.0 ** -7) * np.exp2(-rng.integers(2, 9, z)) * (rng.integers(0, 2, z) * 2.0 - 1.0)
    x[:, :, 8, :, 0] = 126.0 * (rng.integers(0, 2, (N, 8, C)) * 2.0 - 1.0)
    a = layers(rng)
    a[:, :, :, :, :, :8] = 0
    a[:, :, :, :, rng.permutation(8)[:4]] = 0
    return {"x": x.reshape(N, 128, 4 * C).astype(BF), "u": lone(d["u"], 1.0), "v": d["v"], **weights(rng, a)}
def setup_inputs_near(rng):
    d = numbers_of(rng)
    x = d["x"].reshape(N, 8, 16, C, 4)
    o = np.repeat(rng.permutation(N // 2) % 2, 2)
    small = (o == 0)[:, None, None]
    s = np.where(small, rng.choice([1.125, 2.0, -40.0, -40.0], (N, 8, C)) * 2.0 ** -30, rng.integers(-1, 2, (N, 8, C)))
    less = np.where(small, -1.25 * 2.0 ** -30, np.zeros((N, 8, C)))
    for r in range(N):
        for g in rng.permutation(8)[:4]:
            c = rng.integers(C)
            s[r, g, c] = 2.0 ** 29
            less[r, g, c] = 2.0 ** 29
    x[:, :, :8] = 0
    x[:, :, 0, :, 0] = s.astype(np.float32).astype(BF)
    x[:, :, 1, :, 0] = less.astype(np.float32).astype(BF)
    w = layers(rng)
    w[:, :, :8] = 0
    w[:, :, :, :, :, :8] = 0
    return {"x": x.reshape(N, 128, 4 * C), "u": lone(d["u"], np.where(o == 0, 1.125 * 2.0 ** -30, 1.0), np.where(o == 0, 2.0 ** -30, 1.0)), "v": d["v"], **weights(rng, w)}
def setup_inputs_late(rng):
    d = numbers_of(rng)
    x = d["x"].reshape(N, 8, 16, C, 4)
    p = rng.permutation(N // 2)
    c = rng.choice([-1.0, 1.0]) * (1.0 - 2.0 * (p // 2 % 2))
    s = np.stack([c, np.where(p % 2 == 0, c, -c)], axis=1).reshape(N)
    x[:, :, 0] = s.astype(np.float32).astype(BF)[:, None, None, None]
    z = (N, 8, C, 4)
    a = (1.0 + (2 * rng.integers(0, 64, z) + 1) * 2.0 ** -7) * np.exp2(-rng.integers(13, 15, z))
    a[:, 0, :, 0] = 1.96875
    x[:, 7, 8:] = (a * (rng.integers(0, 2, z) * 2.0 - 1.0)).astype(np.float32).astype(BF)
    x[:, 6, 8:] = 0
    w = layers(rng)
    w[:, :, :, :, 6:, 8:] = 0
    for i in range(8, 16):
        for b in range(4): w[:, 7, i, b, 6, i, b] = 32
    w[:, 7, 8, 0, 6, 8, 0] = 0
    return {"x": x.reshape(N, 128, 4 * C), "u": lone(d["u"], 1.0), "v": d["v"], **weights(rng, w)}
def setup_inputs_ends(rng):
    d = numbers_of(rng)
    x = np.zeros((N, 8, 16, C, 4), np.float32)
    u = d["u"].reshape(N, 8, 16, 128, 4)
    u[:, :, :, ::16] = 0
    w = np.zeros((N, 128, 4, 128, 4), np.float32)
    i = np.arange(128)
    o = rng.permutation(N // 2) % 2
    for p in range(N // 2):
        e = slice(2 * p, 2 * p + 2)
        k = 2.0 ** 30 if o[p] == 0 else 2.0 ** -30
        for g in range(8): u[e, g, :, 16 * g] = k
        if o[p] == 0:
            c = rng.choice([-1.0, 1.0], (C // B, 1)) * np.ones((1, 8))
            h = np.argsort(rng.random(c.shape), axis=1)[:, :2]
            np.put_along_axis(c, h, -c[:, :2], axis=1)
            m = rng.permutation(C // B)[:2]
            c[m[0]], c[m[1]] = 1.0, -1.0
            s = 0.75 + 0.25 * rng.random((2, 8, 16, C, 4))
            for a in m: s[:, :, :, B * a:B * a + B] = 1.0
            x[e] = 2.0 ** 30 * s * np.repeat(c.T, B, axis=1)[:, None, :, None]
            for g in rng.permutation(8)[:4]: u[e, :, :, 16 * g] = k
            d["v"][e] = (2.0 ** 30 * rng.choice([-1.0, 1.0], (2, 128, 512))).astype(np.float32).astype(BF)
            for b in range(4): w[e, i, b, i, b] = -1
        else:
            x[e] = 2.0 ** -30
            for g in range(8): x[2 * p + 1, g][:, np.arange(C) % B % 8 == g] = -7.0 * 2.0 ** -30
    d["v"] = (np.where(d["v"] < 0, -1.0, 1.0) * np.where(rng.permutation(N) % 2, 2.0 ** -30, 2.0 ** 30)[:, None, None]).astype(np.float32).astype(BF)
    return {"x": x.reshape(N, 128, 4 * C).astype(BF), "u": u.reshape(N, 128, 512), "v": d["v"], **weights(rng, w.astype(BF))}
def setup_inputs_spread(rng):
    d = setup_inputs(rng)
    d["x"] = wide(rng, N, 128, 4 * C, cols=6)
    return d
def check_inputs(d):
    b = []
    for k in ("x", "u", "v"):
        a = np.abs(d[k].astype(np.float32))
        if not (np.isfinite(a).all() and ((a == 0) | (a >= 2.0 ** -30) & (a <= 2.0 ** 30)).all()): b.append("a value of " + k)
    none, least, most = [emit(mx_ref.quantize(np.full((128, 16), k, np.float32).astype(BF)))[1][0, 0] for k in (0.0, 2.0 ** -30, 2.0 ** 30)]
    for r in range(N):
        if ((d["wc"][r] == 0x7F) | (d["wc"][r] == 0xFF)).any(): b.append("wc: a code that is no number")
        s = mx_ref.live(d["ws"][r])
        if ((s != none) & ((s < least) | (s > most))).any(): b.append("ws: a scale out of range")
    return b
def reference(x, u, v, wc, ws):
    qu = [mx_ref.quantize(u[r]) for r in range(N)]
    lay = [pk(wc[r], ws[r]) for r in range(N)]
    now = [x[r] for r in range(N)]
    mate = np.arange(N) ^ 1
    after = (np.arange(C)[:, None] + np.arange(1, C)) % C
    for t in range(R):
        q = [mx_ref.quantize(now[r]) for r in range(N)]
        own = [decode(q[r]).astype(BF) for r in range(N)]
        word = np.stack([np.packbits(mx_ref.matmul(qu[r], q[r])[::16] > 0, axis=0, bitorder="little")[0] for r in range(N)])
        theirs = word[:, :, None] ^ np.repeat(word[mate].reshape(N, -1, B), B, axis=1)
        ours = word[:, :, None] ^ word[:, after]
        care = np.full((N, C), 255, np.uint8)
        a, kept = np.zeros((N, 8, C), np.int64), np.zeros((N, 8, C), np.int64)
        for k in range(8):
            g = (3 * t + k) % 8
            bit = np.uint8(1 << g)
            keep = np.any((theirs & care[:, :, None]) == bit, axis=2)
            hit = (ours & care[:, :, None]) == bit
            first = after[np.arange(C), np.argmax(hit, axis=2)]
            a[:, g] = np.where(~keep & np.any(hit, axis=2), first, np.arange(C))
            kept[:, g] = keep
            care = np.where(keep, care, care & np.uint8(255 - (1 << g)))
        l = np.argsort(kept, axis=2, kind="stable")[:, :, :K]
        z = [((own[r].astype(np.float32) + gcols(own[r], a[r]).astype(np.float32)) * np.float32(0.5)).astype(BF) for r in range(N)]
        sent = [mx_ref.quantize(gcols(z[r], l[r])) for r in range(N)]
        now = []
        for r in range(N):
            came = sent[mate[r]]
            held = decode(came)
            made = tile([mx_ref.matmul(pick(lay[r], np.arange(128 * b, 128 * b + 128)), came) * np.float32(0.03125) + held[:, b::4] for b in range(4)]).reshape(8, 16, K, 4)
            new = z[r].reshape(8, 16, C, 4).copy()
            for g in range(8): new[g][:, l[r, g]] = made[g]
            now.append(new.reshape(128, 4 * C))
    y, al = np.zeros((N, 128, C), np.float32), np.zeros((N, 8, C + K), np.float32)
    oc, osc = np.zeros((N, 128, 4 * C), np.uint8), np.zeros((N, 16, C), np.uint8)
    for r in range(N):
        q = mx_ref.quantize(now[r])
        y[r] = mx_ref.matmul(mx_ref.quantize(v[r]), q)
        al[r] = np.concatenate([a[r], l[r]], axis=1)
        oc[r], osc[r] = emit(q)
    return {"y": y, "al": al, "oc": oc, "osc": osc}

@@ -1,0 +1,452 @@
+from concourse.bass import DstId, RemoteDMATransfer
+from concourse.mybir import dt, AluOpType, AxisListType, ActivationFunctionType
+
+C, K, R = 320, 128, 3
+F8, F32, BF, I32, U16, U8 = "float8_e4m3fn_x4", "float32", "bfloat16", "int32", "uint16", "uint8"
+
+
+def _sb(n, d):
+    return ("sbuf", [128, n], d)
+
+
+SCRATCH = {
+    "ps": ("psum", [128, 4096], F32),
+    "x0": _sb(1280, BF), "xs": _sb(1280, BF), "qx": _sb(C, F8), "qxs": _sb(C, U8),
+    "ut": _sb(512, BF), "uq": _sb(128, F8), "uqs": _sb(128, U8),
+    "vt": _sb(512, BF), "vq": _sb(128, F8), "vqs": _sb(128, U8),
+    "wq": _sb(512, F8), "wqs": _sb(512, U8),
+    "dg": _sb(516, BF), "dh": _sb(516, BF), "dk": _sb(516, BF),
+    "eh": _sb(512, F8), "ehs": _sb(512, U8), "ek": _sb(512, F8), "eks": _sb(512, U8),
+    "cwt": _sb(512, BF), "cw": _sb(768, F8), "cws": _sb(768, U8),
+    "ip": _sb(4, I32), "ir": _sb(C, I32), "iw": _sb(C, I32), "io8": _sb(8, I32), "i4": _sb(4, I32), "ia": _sb(16, I32),
+    "kf": _sb(96, F32), "ki": _sb(32, I32), "jrow": _sb(C, F32), "wmask": _sb(C, F32), "seg": _sb(C, F32),
+    "ones": _sb(C, F32), "pw4": _sb(16, F32), "pw2": _sb(16, F32), "tmp8": _sb(16, F32), "oneh": _sb(8, F32),
+    "sl": _sb(12, U16), "mg": _sb(176, F32), "phi": _sb(960, F32), "phit": _sb(960, F32), "j24": _sb(24, F32),
+    "j16": _sb(20, F32), "code": _sb(24, F32), "res": _sb(60, F32),
+    "bt": _sb(1280, BF), "bq": _sb(C, F8), "bqs": _sb(C, U8),
+    "w4": _sb(C, F32), "gw": _sb(176, F32), "gm": _sb(176, F32), "ms": _sb(60, F32), "msg": _sb(60, U16), "pw": _sb(60, U16),
+    "wm": _sb(C, F32), "wsc": _sb(C, F32), "wl": _sb(20, U16),
+    "wj": _sb(3, F32), "wji": _sb(3, I32), "ob": _sb(24, I32), "u0": _sb(24, F32), "u1": _sb(24, F32), "sg": _sb(24, F32),
+    "obb": _sb(24, F32), "ct": _sb(768, BF), "pt": _sb(768, BF), "n0": _sb(960, F32), "nn": _sb(960, F32),
+    "sm": _sb(60, I32), "vi": _sb(60, I32), "dd": _sb(480, I32), "vv": _sb(60, F32), "vz": _sb(60, F32), "sc": _sb(60, F32),
+    "kl": _sb(60, F32), "keep": _sb(24, F32), "pks": _sb(24, F32), "pb": _sb(24, F32), "base": _sb(8, F32),
+    "zz": _sb(7 * 960, BF), "zv": _sb(960, F32), "so": _sb(480, BF), "mn": _sb(24, F32), "ac": _sb(24 * 8, F32),
+    "kg": _sb(32, F32), "kt": _sb(32, F32), "ag": _sb(32, F32), "at": _sb(32, F32), "uk": _sb(32, F32), "ua": _sb(32, F32),
+    "us": _sb(32, F32), "uto": _sb(32, F32), "ust": _sb(32, F32), "utt": _sb(32, F32), "kw": _sb(32, F32), "pq": _sb(160, F32),
+    "poff": _sb(20, U16), "selo": _sb(20, U16), "lw": _sb(C, F32), "lm": _sb(128, F32), "ls": _sb(128, F32), "loff": _sb(8, U16),
+    "aw": _sb(32, F32), "aoff": _sb(20, U16),
+    "fb": _sb(1280, BF), "fc": _sb(1280, BF), "zt": _sb(4 * 448, BF), "et": _sb(512, BF), "qe": _sb(128, F8), "qes": _sb(128, U8),
+    "qa": _sb(128, F8), "qas": _sb(128, U8), "yo": _sb(C, F32),
+}
+SEMAPHORES = ["cv", "cs", "ct", "cg", "dx", "du", "dv", "dw", "dk", "da", "do", "rw", "re", "rl"]
+
+
+def rank_program(g, core, T, topo):
+    rank = T.rank_of(core)
+    if rank is None:
+        return
+    A, AF, X = AluOpType, ActivationFunctionType, AxisListType.X
+    partner = T.cores[rank ^ 1]
+    rid, pid = topo.addr(partner)[:2]
+    mask, neng = topo.mask(core, partner), len(topo.engines(core, partner))
+    codv = T["code"]
+    eng = {"v": g.vector, "s": g.scalar, "t": g.tensor, "g": g, "y": g.sync}
+    own = {"v": "cv", "s": "cs", "t": "ct", "g": "cg"}
+    cnt = {s: 0 for s in SEMAPHORES}
+    seen = {q: {} for q in eng}
+    wr, rd = {}, {}
+
+    def need(q, tok):
+        v = cnt[tok[1]] if tok[2] is None else tok[2]
+        if seen[q].get(tok[1], 0) < v:
+            eng[q].wait_ge(T.sem[tok[1]], v)
+            seen[q][tok[1]] = v
+
+    def waits(q, reads, writes, waw=True):
+        for k in reads:
+            for tok in wr.get(k, []):
+                need(q, tok)
+            if k[:2] == "ps":
+                for tok in rd.get(k, []):
+                    if tok[0] != q:
+                        need(q, tok)
+        for k in writes:
+            for tok in wr.get(k, []):
+                if waw or tok[0] != q:
+                    need(q, tok)
+            for tok in rd.get(k, []):
+                need(q, tok)
+
+    def note(tok, reads, writes):
+        for k in reads:
+            rd.setdefault(k, []).append(tok)
+        for k in writes:
+            wr[k] = [tok]
+            rd[k] = []
+
+    def op(q, call, args, reads, writes, kw=None, waw=True):
+        waits(q, reads, writes, waw)
+        s = own[q]
+        call(*args, **(kw or {})).then_inc(T.sem[s], 1)
+        cnt[s] += 1
+        note((q, s, cnt[s]), reads, writes)
+
+    def dmas(sem, items, reads, writes):
+        for q in sorted(set(i[0] for i in items)):
+            waits(q, reads, writes)
+        for q, o, i in items:
+            eng[q].dma_start(o, i).then_inc(T.sem[sem], 16)
+            cnt[sem] += 16
+        note(("dma", sem, None), reads, writes)
+
+    vec, sca = g.vector, g.scalar
+
+    def ts(o, i, s1, o1, s2, o2, reads, writes):
+        if o2 is None:
+            op("v", vec.tensor_scalar, (o, i, s1, None, o1), reads, writes)
+        else:
+            op("v", vec.tensor_scalar, (o, i, s1, s2, o1, o2), reads, writes)
+
+    def tt(o, a, b, f, reads, writes):
+        op("v", vec.tensor_tensor, (o, a, b, f), reads, writes)
+
+    def cp(o, i, reads, writes):
+        op("v", vec.tensor_copy, (o, i), reads, writes)
+
+    def act(o, i, f, reads, writes, **kw):
+        op("s", sca.activation, (o, i, f), reads, writes, kw)
+
+    def fill(o, c, w):
+        op("v", vec.memset, (o, c), [], w)
+
+    def scan(o, a, b, init, f, h, reads, writes):
+        op("v", vec.tensor_tensor_scan, (o, a, b, init, f, h), reads, writes)
+
+    def quant(q, s, t, reads, writes):
+        op("v", vec.quantize_mx, (q, s, t), reads, writes)
+
+    def mm(bank, n, l, ls, r, rs, reads, start=True, stop=True):
+        op("t", g.tensor.matmul_mx, (T.ps[:, 512 * bank:512 * bank + n], l, ls, r, rs, start, stop), reads, ["ps%d" % bank], waw=start)
+
+    dmas("dx", [("y", T.x0[:, 0:640], T.x[:, 0:640]), ("s", T.x0[:, 640:1280], T.x[:, 640:1280])], [], ["x"])
+    dmas("du", [("y", T.ut[:], T.u[:, :])], [], ["ut"])
+    dmas("dw", [("y", T.wq[:, 0:512].bitcast(dt.uint8), T.wc[:, 0:2048]), ("y", T.wqs[:, 0:512], T.ws[:, 0:512])], [], ["w"])
+    dmas("dv", [("y", T.vt[:], T.v[:, :])], [], ["vt"])
+
+    def iota(o, pat, base, cm, w):
+        op("g", g.iota, (o, pat, base, cm), [], w)
+    iota(T.ip[:, 0:1], [[1, 1]], 0, 1, ["ip"])
+    iota(T.io8[:, :], [[-16, 8]], 0, 1, ["io8"])
+    iota(T.iw[:, :], [[1, C]], 128, -1, ["iw"])
+    iota(T.ir[:, :], [[1, C]], 0, 0, ["ir"])
+    iota(T.i4[:, :], [[16, 4]], 0, 0, ["i4"])
+    fill(T.ones[:, :], 1.0, ["ones"])
+    fill(T.dg[:, :], 0.5, ["dg"])
+    op("g", g.affine_select, (T.dh[:, :], T.dg[:, :], [[-1, 516]], A.is_equal, 0.0, 3, 4), ["dg"], ["dh"])
+    fill(T.bt[:, :], 0.0, ["bt"])
+    fill(T.cwt[:, :], 0.0, ["cwt"])
+    fill(T.tmp8[:, 8:16], 0.0, ["t8b"])
+    for base, buf in ((4.0, T.pw4), (2.0, T.pw2)):
+        fill(T.tmp8[:, 0:8], base, ["t8"])
+        scan(buf[:, 0:8], T.tmp8[:, 0:8], T.tmp8[:, 8:16], 1.0 / base, A.mult, A.add, ["t8", "t8b"], ["pw"])
+        cp(buf[:, 8:16], buf[:, 0:8], ["pw"], ["pw"])
+    ts(T.oneh[:, :], T.io8[:, :], 0.0, A.is_equal, None, None, ["io8"], ["oneh"])
+
+    def weights(t):
+        s = (-3 * t) % 8
+        for h, buf in enumerate((T.pw4, T.pw2)):
+            tt(T.tmp8[:, 0:8], T.oneh[:, :], buf[:, s:s + 8], A.mult, ["oneh", "pw"], ["t8"])
+            op("v", vec.tensor_reduce, (T.kf[:, 90:91], T.tmp8[:, 0:8], X, A.add), ["t8"], ["wcol"])
+            ts(T.cwt[:, 0:512:4], T.ones[:, 0:128], T.kf[:, 90:91], A.mult, None, None, ["ones", "wcol"], ["cwt"])
+            o = 128 * (2 * t + h)
+            quant(T.cw[:, o:o + 128], T.cws[:, o:o + 128], T.cwt[:, :], ["cwt"], ["cw%d" % (2 * t + h)])
+    weights(0)
+    quant(T.uq[:, :], T.uqs[:, :], T.ut[:, :], ["ut"], ["uq"])
+    quant(T.qx[:, :], T.qxs[:, :], T.x0[:, :], ["x"], ["qx"])
+
+    kf, k = T.kf, ["kf"]
+    for c, (m, sh) in enumerate(((15, 0), (31, 0), (1, 4), (3, 5))):
+        op("v", vec.tensor_scalar, (T.ki[:, c:c + 1], T.ip[:, 0:1], sh, m, A.logical_shift_right, A.bitwise_and), ["ip"], ["ki"])
+    cp(kf[:, 3:4], T.ki[:, 0:1], ["ki"], k)
+    ts(kf[:, 4:5], T.ki[:, 3:4], 3.0, A.is_equal, -64.0, A.mult, ["ki"], k)
+    cp(kf[:, 13:14], T.ki[:, 1:2], ["ki"], k)
+    ts(kf[:, 14:15], T.ki[:, 2:3], 16.0, A.mult, None, None, ["ki"], k)
+    ts(kf[:, 0:1], T.ki[:, 3:4], 96.0, A.mult, kf[:, 13:14], A.add, ["ki", "kf"], k)
+    ts(kf[:, 5:6], T.ki[:, 3:4], 96.0, A.mult, kf[:, 14:15], A.add, ["ki", "kf"], k)
+    for t in (1, 2):
+        ts(kf[:, t:t + 1], kf[:, 0:1], 32.0 * t, A.add, kf[:, 4:5], A.add, k, k)
+
+    def floor20(o, i, n):
+        ts(kf[:, 80:80 + n], i, 0.05, A.mult, -0.475, A.add, k, ["fl"])
+        cp(T.ki[:, 16:16 + n], kf[:, 80:80 + n], ["fl"], ["fli"])
+        cp(o, T.ki[:, 16:16 + n], ["fli"], k)
+    ts(kf[:, 16:19], kf[:, 0:3], kf[:, 3:4], A.subtract, None, None, k, k)
+    floor20(kf[:, 20:23], kf[:, 16:19], 3)
+    floor20(kf[:, 24:27], kf[:, 0:3], 3)
+    tt(kf[:, 6:9], kf[:, 20:23], kf[:, 24:27], A.is_equal, k, k)
+    ts(kf[:, 9:12], kf[:, 6:9], -1.0, A.mult, 1.0, A.add, k, k)
+    ts(kf[:, 28:32], T.i4[:, :], kf[:, 3:4], A.add, None, None, ["i4", "kf"], k)
+    floor20(kf[:, 32:36], kf[:, 28:32], 4)
+    ts(kf[:, 32:36], kf[:, 32:36], 2.0, A.min, None, None, k, k)
+    ts(kf[:, 36:40], kf[:, 32:36], -20.0, A.mult, None, None, k, k)
+    tt(kf[:, 36:40], kf[:, 36:40], kf[:, 28:32], A.add, k, k)
+    ts(kf[:, 40:44], kf[:, 32:36], 32.0, A.mult, kf[:, 5:6], A.add, k, k)
+    ts(kf[:, 44:48], kf[:, 32:36], 1.0, A.is_ge, kf[:, 4:5], A.mult, k, k)
+    tt(kf[:, 40:44], kf[:, 40:44], kf[:, 44:48], A.add, k, k)
+    floor20(kf[:, 48:52], kf[:, 40:44], 4)
+    ts(kf[:, 52:56], kf[:, 48:52], 1.0, A.add, 15.0, A.min, k, k)
+    for o in (48, 52):
+        ts(kf[:, o:o + 4], kf[:, o:o + 4], 20.0, A.mult, None, None, k, k)
+        tt(kf[:, o:o + 4], kf[:, o:o + 4], kf[:, 36:40], A.add, k, k)
+        ts(kf[:, o:o + 4], kf[:, o:o + 4], 319.0, A.min, None, None, k, k)
+    cp(T.sl[:, 0:3], kf[:, 0:3], k, ["sl"])
+    cp(T.sl[:, 3:11], kf[:, 48:56], k, ["sl"])
+    op("v", vec.tensor_scalar, (T.iw[:, :], T.iw[:, :], 15, None, A.bitwise_and), ["iw"], ["iw"])
+    ts(T.wmask[:, :], T.iw[:, :], 0.0, A.is_equal, None, None, ["iw"], ["wmask"])
+    fill(T.mg[:, :], 0.0, ["mg"])
+    cp(T.mg[:, 0:48], T.wmask[:, 0:48], ["wmask"], ["mg"])
+    for t in range(3):
+        ts(T.mg[:, 48 + 20 * t:68 + 20 * t], T.ones[:, 0:20], kf[:, 6 + t:7 + t], A.mult, None, None, ["ones", "kf"], ["mg"])
+        ts(T.mg[:, 112 + 20 * t:132 + 20 * t], T.ones[:, 0:20], kf[:, 9 + t:10 + t], A.mult, None, None, ["ones", "kf"], ["mg"])
+
+    def more_constants():
+        cp(T.jrow[:, :], T.ir[:, :], ["ir"], ["jrow"])
+        op("v", vec.tensor_scalar, (T.iw[:, :], T.ir[:, :], 15, None, A.bitwise_and), ["ir"], ["iw"])
+        ts(T.seg[:, :], T.iw[:, :], 0.0, A.not_equal, None, None, ["iw"], ["seg"])
+        for i in range(8):
+            fill(codv[:, 3 * i:3 * i + 3], 1024.0 * (i + 1), ["code"])
+        fill(T.res[:, :], 0.0, ["res"])
+        for t in range(3):
+            fill(T.res[:, 20 * t:20 * t + 1], 2.0, ["res"])
+            fill(T.ct[:, 256 * t:256 * t + 1], 0.0, ["ct%d" % t])
+            fill(T.pt[:, 256 * t:256 * t + 1], 0.0, ["pt%d" % t])
+            s = slice(320 * t, 320 * t + 320)
+            ts(T.phi[:, s], T.jrow[:, :], kf[:, t:t + 1], A.subtract, None, None, ["jrow", "kf"], ["phi"])
+        ts(T.phit[:, :], T.phi[:, :], 0.0, A.is_lt, 320.0, A.mult, ["phi"], ["phit"])
+        tt(T.phi[:, :], T.phi[:, :], T.phit[:, :], A.add, ["phi", "phit"], ["phi"])
+        ts(T.phit[:, :], T.phi[:, :], 2.0, A.mult, -256.0, A.add, ["phi"], ["phit"])
+        tt(T.phi[:, :], T.phi[:, :], T.phit[:, :], A.max, ["phi", "phit"], ["phi"])
+        for b in range(4):
+            quant(T.eh[:, 128 * b:128 * b + 128], T.ehs[:, 128 * b:128 * b + 128], T.dh[:, 3 - b:515 - b], ["dh"], ["eh"])
+
+    def later_constants():
+        for i in range(8):
+            cp(T.j24[:, 3 * i:3 * i + 3], kf[:, 0:3], k, ["j24"])
+        ts(T.j16[:, :], T.ir[:, 0:20], 16.0, A.mult, kf[:, 3:4], A.add, ["ir", "kf"], ["j16"])
+        for n in ("kg", "ag", "uk", "ua"):
+            fill(T[n][:, :], 0.0, [n])
+        ts(T.dk[:, :], T.dh[:, :], 64.0, A.mult, None, None, ["dh"], ["dk"])
+        for b in range(4):
+            quant(T.ek[:, 128 * b:128 * b + 128], T.eks[:, 128 * b:128 * b + 128], T.dk[:, 3 - b:515 - b], ["dk"], ["ek"])
+        quant(T.vq[:, :], T.vqs[:, :], T.vt[:, :], ["vt"], ["vq"])
+        weights(1)
+        weights(2)
+
+    def to_wrapped(src, dst, sem, queues, key_in, key_out):
+        items = []
+        for a in range(4):
+            n = 3 if a < 3 else 1
+            for gr in range(8):
+                G, h = divmod(gr, 2)
+                items.append((queues[len(items) % len(queues)],
+                              dst[32 * G + 6 * a:32 * G + 6 * a + 2 * n, 16 * h:16 * h + 16],
+                              src[32 * a + 3 * gr:32 * a + 3 * gr + n, 0:32]))
+        dmas(sem, items, [key_in], [key_out])
+
+    for t in range(R):
+        rot = (3 * t) % 8
+
+        def by_group(fn):
+            n = 8 - rot
+            fn(slice(3 * rot, 24), slice(0, 3 * n))
+            if rot:
+                fn(slice(0, 3 * rot), slice(3 * n, 24))
+        mm(0, C, T.uq[:, :], T.uqs[:, :], T.qx[:, :], T.qxs[:, :], ["uq", "qx"])
+        ts(T.bt[:, 0:1280:4], T.ps[:, 0:C], 0.0, A.is_gt, None, None, ["ps0"], ["bt"])
+        quant(T.bq[:, :], T.bqs[:, :], T.bt[:, :], ["bt"], ["bq"])
+        for h in range(2):
+            o = 128 * (2 * t + h)
+            mm(1 + h, C, T.cw[:, o:o + 128], T.cws[:, o:o + 128], T.bq[:, :], T.bqs[:, :], ["cw%d" % (2 * t + h), "bq"])
+        act(T.w4[:, :], T.ps[:, 512:512 + C], AF.Copy, ["ps1"], ["w4"])
+        cp(T.gw[:, :], T.w4[:, 0:C].indirect(T.sl[:, 0:11]), ["w4", "sl"], ["gw"])
+        tt(T.gm[:, :], T.gw[:, :], T.mg[:, :], A.mult, ["gw", "mg"], ["gm"])
+        tt(T.ms[:, :], T.gm[:, 48:108], T.gm[:, 112:172], A.add, ["gm"], ["ms"])
+        cp(T.msg[:, :], T.ms[:, :], ["ms"], ["msg"])
+        waits("g", ["msg"], [])
+        g.remote_dma(T.pw[:, 0:60], T.msg[:, 0:60], T.sem["rw"], T.sem["rl"], pid, rid, mask)
+        cnt["rl"] += neng
+        cnt["rw"] += neng
+        note(("dma", "rl", None), ["msg"], [])
+        if t == 0:
+            more_constants()
+        for b in range(4):
+            mm(4 + b, C, T.eh[:, 128 * b:128 * b + 128], T.ehs[:, 128 * b:128 * b + 128], T.qx[:, :], T.qxs[:, :], ["eh", "qx"])
+            act(T.fb[:, 320 * b:320 * b + 320], T.ps[:, 512 * (4 + b):512 * (4 + b) + C], AF.Copy, ["ps%d" % (4 + b)], ["fb%d" % b])
+            act(T.fc[:, 320 * b:320 * b + 320], T.ps[:, 512 * (4 + b):512 * (4 + b) + C], AF.Copy, ["ps%d" % (4 + b)], ["fc%d" % b])
+        for c in range(3):
+            op("v", vec.tensor_reduce, (T.wj[:, c:c + 1], T.gm[:, 16 * c:16 * c + 16], X, A.add), ["gm"], ["wj"], waw=False)
+        cp(T.wji[:, :], T.wj[:, :], ["wj"], ["wji"])
+        for i in range(8):
+            op("v", vec.tensor_scalar, (T.ob[:, 3 * i:3 * i + 3], T.wji[:, :], 2 * i, 1, A.logical_shift_right, A.bitwise_and), ["wji"], ["ob"], waw=False)
+        tt(T.u0[:, :], T.ob[:, :], codv[:, :], A.mult, ["ob", "code"], ["u0"])
+        tt(T.u1[:, :], codv[:, :], T.u0[:, :], A.subtract, ["u0", "code"], ["u1"])
+        ts(T.sg[:, :], T.ob[:, :], -32768.0, A.mult, 16384.0, A.add, ["ob"], ["sg"])
+        ts(T.obb[:, :], T.ob[:, :], 16384.0, A.mult, None, None, ["ob"], ["obb"])
+        tt(T.wm[:, :], T.ps[:, 1024:1024 + C], T.wmask[:, :], A.mult, ["ps2", "wmask"], ["wm"])
+        scan(T.wsc[:, :], T.seg[:, :], T.wm[:, :], 0.0, A.mult, A.add, ["seg", "wm"], ["wsc"])
+        cp(T.wl[:, :], T.wsc[:, 15:C:16], ["wsc"], ["wl"])
+        for i in range(8):
+            n = 1 << i
+            for c in range(3):
+                lo, hi = slice(256 * c, 256 * c + n), slice(256 * c + n, 256 * c + 2 * n)
+                col = slice(3 * i + c, 3 * i + c + 1)
+                ts(T.ct[:, hi], T.ct[:, lo], T.u1[:, col], A.max, None, None, ["ct%d" % c, "ct%dh" % c, "u1"], ["ct%dh" % c])
+            for c in range(3):
+                lo = slice(256 * c, 256 * c + n)
+                col = slice(3 * i + c, 3 * i + c + 1)
+                ts(T.ct[:, lo], T.ct[:, lo], T.u0[:, col], A.max, None, None, ["ct%d" % c, "ct%dh" % c, "u0"], ["ct%d" % c])
+        for c in range(3):
+            s = slice(320 * c, 320 * c + 320)
+            tt(T.n0[:, s], T.ct[:, 256 * c:256 * c + 256].indirect(T.wl[:, 0:20]), T.phi[:, s], A.add,
+               ["ct%d" % c, "ct%dh" % c, "wl", "phi"], ["n0%d" % c])
+            if t < R - 1:
+                fill(T.ct[:, 256 * c:256 * c + 1], 0.0, ["ct%d" % c])
+        if t == 0:
+            later_constants()
+        note(("dma", "rw", cnt["rw"]), [], ["pw"])
+        for c in range(3):
+            ts(T.sm[:, 20 * c:20 * c + 20], T.pw[:, 20 * c:20 * c + 20], T.wj[:, c:c + 1], A.add, None, None, ["pw", "wj"], ["sm%d" % c])
+        op("v", vec.tensor_scalar, (T.vi[:, :], T.sm[:, :], 0x5555, None, A.bitwise_and), ["sm0", "sm1", "sm2"], ["vi"])
+        ts(T.vz[:, :], T.vi[:, :], 0.0, A.is_equal, None, None, ["vi"], ["vz"])
+        ts(T.vv[:, :], T.vi[:, :], 2.0 ** -15, A.mult, None, None, ["vi"], ["vv"])
+        for i in range(8):
+            op("v", vec.tensor_scalar, (T.dd[:, 60 * i:60 * i + 60], T.vi[:, :], 4 ** i, None, A.bitwise_and), ["vi"], ["dd%d" % i])
+        tt(T.vv[:, :], T.vv[:, :], T.vz[:, :], A.max, ["vv", "vz"], ["vv"])
+        for i in range(8):
+            scan(T.sc[:, :], T.res[:, :], T.vv[:, :], 2.0, A.max, A.min, ["res", "vv"], ["sc"])
+            if i < 7:
+                for c in range(3):
+                    m = T.sc[:, 20 * c + 19:20 * c + 20]
+                    ts(T.kl[:, 20 * c:20 * c + 20], T.dd[:, 60 * i + 20 * c:60 * i + 20 * c + 20], 2.0 ** -14, A.mult, m, A.is_gt,
+                       ["dd%d" % i, "sc"], ["kl%d" % c])
+            c3 = slice(3 * i, 3 * i + 3)
+            ts(T.keep[:, c3], T.sc[:, 19:60:20], 2.0 ** -14 * 4 ** i, A.is_lt, None, None, ["sc"], ["keep%d" % i])
+            if i < 7:
+                tt(T.vv[:, :], T.vv[:, :], T.kl[:, :], A.max, ["vv", "kl0", "kl1", "kl2"], ["vv"])
+            tt(T.pks[:, c3], T.keep[:, c3], T.sg[:, c3], A.mult, ["keep%d" % i, "sg"], ["pks%d" % i])
+            n = 1 << i
+            if i < 7:
+                for c in range(3):
+                    act(T.pt[:, 256 * c + n:256 * c + 2 * n], T.pt[:, 256 * c:256 * c + n], AF.Identity, ["pt%d" % c, "pks%d" % i], ["pt%d" % c],
+                        bias=T.pks[:, 3 * i + c:3 * i + c + 1])
+        keeps = ["keep%d" % i for i in range(8)]
+        tt(T.pb[:, :], T.keep[:, :], T.obb[:, :], A.mult, keeps + ["obb"], ["pb"])
+        for c in range(3):
+            op("v", vec.tensor_reduce, (T.base[:, c:c + 1], T.pb[:, c:24:3], X, A.add), ["pb"], ["base"], waw=False)
+        tt(T.base[:, 3:6], T.base[:, 0:3], T.pks[:, 21:24], A.add, ["base", "pks7"], ["base2"])
+        for c in range(3):
+            lo, hi = slice(256 * c, 256 * c + 128), slice(256 * c + 128, 256 * c + 256)
+            act(T.pt[:, hi], T.pt[:, lo], AF.Identity, ["pt%d" % c, "base2"], ["pt%dh" % c], bias=T.base[:, 3 + c:4 + c])
+            act(T.pt[:, lo], T.pt[:, lo], AF.Identity, ["pt%d" % c, "base"], ["pt%d" % c], bias=T.base[:, c:c + 1])
+        by_group(lambda o, i: cp(T.kg[:, o], T.keep[:, i], keeps, ["kg"]))
+        op("v", vec.transpose, (T.kt[:, :], T.kg[:, :]), ["kg"], ["kt"])
+        to_wrapped(T.kt, T.uk, "dk", ["y"], "kt", "uk")
+        for c in range(3):
+            s = slice(320 * c, 320 * c + 320)
+            tt(T.nn[:, s], T.pt[:, 256 * c:256 * c + 256].indirect(T.wl[:, 0:20]), T.n0[:, s], A.add,
+               ["pt%d" % c, "pt%dh" % c, "wl", "n0%d" % c], ["nn%d" % c])
+        nns = ["nn0", "nn1", "nn2"]
+        if t < R - 1:
+            for c in range(3):
+                fill(T.pt[:, 256 * c:256 * c + 1], 0.0, ["pt%d" % c])
+        for i in range(7):
+            act(T.zz[:, 960 * i:960 * i + 960], T.nn[:, :], AF.Abs, nns, ["zz%d" % i], bias=-1024.0 * (i + 1))
+        ts(T.zv[:, :], T.nn[:, :], -8192.0, A.add, None, None, nns, ["zv"])
+        for c in range(3):
+            op("v", vec.tensor_reduce, (T.mn[:, 21 + c:22 + c], T.zv[:, 320 * c:320 * c + 320], X, A.min), ["zv"], ["mn"],
+               {"apply_absolute_value": True}, waw=False)
+
+        def firsts(i):
+            for c in range(3):
+                o = 960 * i + 320 * c
+                scan(T.so[:, 160 * c:160 * c + 160], T.zz[:, o:o + 160], T.zz[:, o + 160:o + 320], 65536.0, A.min, A.min, ["zz%d" % i], ["so%d" % c])
+            cp(T.mn[:, 3 * i:3 * i + 3], T.so[:, 159:480:160], ["so0", "so1", "so2"], ["mn"])
+        for i in range(5):
+            firsts(i)
+        scan(T.us[:, :], T.seg[:, 0:32], T.uk[:, :], 0.0, A.mult, A.add, ["seg", "uk"], ["us"])
+        for h in range(2):
+            ts(T.uto[:, 16 * h:16 * h + 16], T.ones[:, 0:16], T.us[:, 16 * h + 15:16 * h + 16], A.mult, None, None, ["ones", "us"], ["uto%d" % h])
+        op("v", vec.transpose, (T.ust[:, :], T.us[:, :]), ["us"], ["ust"])
+        op("v", vec.transpose, (T.utt[:, :], T.uto[:, :]), ["uto0", "uto1"], ["utt"])
+        op("v", vec.transpose, (T.kw[:, :], T.uk[:, :]), ["uk"], ["kw"])
+        pq, q = T.pq, ["pq"]
+        scan(pq[:, 0:20], T.ones[:, 0:20], T.utt[:, 0:20], 0.0, A.mult, A.add, ["ones", "utt"], q)
+        tt(pq[:, 20:40], T.ust[:, 0:20], T.utt[:, 0:20], A.subtract, ["ust", "utt"], ["pq1"])
+        tt(pq[:, 20:40], pq[:, 20:40], pq[:, 0:20], A.add, q + ["pq1"], ["pq1"])
+        ts(pq[:, 40:41], pq[:, 19:20], -1.0, A.mult, 319.0, A.add, q, ["pq2"])
+        tt(pq[:, 60:80], T.j16[:, :], pq[:, 20:40], A.subtract, ["j16", "pq1"], ["pq3"])
+        ts(pq[:, 80:100], pq[:, 20:40], pq[:, 40:41], A.add, None, None, ["pq1", "pq2"], ["pq4"])
+        tt(pq[:, 80:100], pq[:, 80:100], pq[:, 60:80], A.subtract, ["pq3", "pq4"], ["pq4"])
+        tt(pq[:, 80:100], pq[:, 80:100], T.kw[:, 0:20], A.mult, ["pq4", "kw"], ["pq4"])
+        tt(pq[:, 60:80], pq[:, 60:80], pq[:, 80:100], A.add, ["pq3", "pq4"], ["pq3"])
+        cp(T.poff[:, :], pq[:, 60:80], ["pq3"], ["poff"])
+        op("v", vec.tensor_copy, (T.lw[:, 0:C].indirect(T.poff[:, 0:20]), T.jrow[:, :]), ["poff", "jrow"], ["lw"])
+        ts(pq[:, 100:120], pq[:, 60:80], 128.0, A.is_lt, None, None, ["pq3"], ["pq5"])
+        ts(pq[:, 60:80], pq[:, 60:80], 320.0, A.add, None, None, ["pq3"], ["pq3"])
+        tt(pq[:, 60:80], pq[:, 60:80], T.j16[:, :], A.subtract, ["pq3", "j16"], ["pq3"])
+        tt(pq[:, 60:80], pq[:, 60:80], pq[:, 100:120], A.mult, ["pq3", "pq5"], ["pq3"])
+        tt(pq[:, 60:80], pq[:, 60:80], T.j16[:, :], A.add, ["pq3", "j16"], ["pq3"])
+        cp(T.selo[:, :], pq[:, 60:80], ["pq3"], ["selo"])
+        tt(T.lm[:, :], T.lw[:, 0:128], T.wmask[:, 0:128], A.mult, ["lw", "wmask"], ["lm"])
+        scan(T.ls[:, :], T.seg[:, 0:128], T.lm[:, :], 0.0, A.mult, A.add, ["seg", "lm"], ["ls"])
+        cp(T.loff[:, :], T.ls[:, 15:128:16], ["ls"], ["loff"])
+        for i in range(5, 7):
+            firsts(i)
+        ac = T.ac
+        ts(ac[:, 0:24], T.mn[:, :], 0.5, A.mult, 128.0, A.add, ["mn"], ["ac0"])
+        ts(ac[:, 24:48], T.mn[:, :], 500.0, A.is_lt, None, None, ["mn"], ["ac1"])
+        tt(ac[:, 0:24], ac[:, 0:24], T.mn[:, :], A.min, ["ac0", "mn"], ["ac0"])
+        tt(ac[:, 24:48], ac[:, 24:48], T.keep[:, :], A.is_gt, ["ac1"] + keeps, ["ac1"])
+        tt(ac[:, 0:24], ac[:, 0:24], ac[:, 24:48], A.mult, ["ac0", "ac1"], ["ac0"])
+        tt(ac[:, 0:24], ac[:, 0:24], T.j24[:, :], A.add, ["ac0", "j24"], ["ac0"])
+        ts(ac[:, 24:48], ac[:, 0:24], 320.0, A.is_ge, -320.0, A.mult, ["ac0"], ["ac1"])
+        by_group(lambda o, i: tt(T.ag[:, o], ac[:, i], ac[:, 24 + i.start:24 + i.stop], A.add, ["ac0", "ac1"], ["ag"]))
+        op("v", vec.transpose, (T.at[:, :], T.ag[:, :]), ["ag"], ["at"])
+        to_wrapped(T.at, T.ua, "da", ["y", "s"], "at", "ua")
+        if t == R - 1:
+            dmas("do", [("y", T.al[:, 96 * a:96 * a + 96], T.at[32 * a:32 * a + 24, 0:32]) for a in range(3)]
+                 + [("y", T.al[:, 288:320], T.at[96:120:3, 0:32]), ("y", T.al[:, 320:448], T.lw[0:128:16, 0:128])], ["at", "lw"], ["al"])
+        op("v", vec.transpose, (T.aw[:, :], T.ua[:, :]), ["ua"], ["aw"])
+        cp(T.aoff[:, :], T.aw[:, 0:20], ["aw"], ["aoff"])
+        for b in range(4):
+            f = slice(320 * b, 320 * b + 320)
+            tt(T.zt[:, 448 * b:448 * b + 320], T.fb[:, f].indirect(T.aoff[:, 0:20]), T.fc[:, f], A.add, ["fb%d" % b, "fc%d" % b, "aoff"], ["zt%d" % b])
+            act(T.et[:, b:512:4], T.zt[:, 448 * b:448 * b + 320].indirect(T.loff[:, 0:8]), AF.Copy, ["zt%d" % b, "loff"], ["et%d" % b])
+        quant(T.qe[:, :], T.qes[:, :], T.et[:, :], ["et%d" % b for b in range(4)], ["qe"])
+        waits("g", ["qe"], [])
+        g.remote_dma(T.qa[:, 0:128].bitcast(dt.uint8), T.qe[:, 0:128].bitcast(dt.uint8), T.sem["re"], T.sem["rl"], pid, rid, mask)
+        g.remote_dma(T.qas[:, 0:128], T.qes[:, 0:128], T.sem["re"], T.sem["rl"], pid, rid, mask)
+        cnt["rl"] += 2 * neng
+        cnt["re"] += 2 * neng
+        note(("dma", "rl", None), ["qe"], [])
+        note(("dma", "re", cnt["re"]), [], ["qa"])
+        for b in range(4):
+            w = slice(128 * b, 128 * b + 128)
+            mm(4 + b, 128, T.wq[:, w], T.wqs[:, w], T.qa[:, :], T.qas[:, :], ["w", "qa"], True, False)
+            mm(4 + b, 128, T.ek[:, w], T.eks[:, w], T.qa[:, :], T.qas[:, :], ["ek", "qa"], False, True)
+            o, i = T.zt[:, 448 * b + 320:448 * b + 448], T.ps[:, 512 * (4 + b):512 * (4 + b) + 128]
+            n, win = T.xs[:, b:1280:4], T.zt[:, 448 * b:448 * b + 448].indirect(T.selo[:, 0:20])
+            if b % 2 == 0:
+                act(o, i, AF.Copy, ["ps%d" % (4 + b)], ["tm%d" % b], scale=0.03125)
+                act(n, win, AF.Copy, ["zt%d" % b, "tm%d" % b, "selo"], ["xs%d" % b])
+            else:
+                ts(o, i, 0.03125, A.mult, None, None, ["ps%d" % (4 + b)], ["tm%d" % b])
+                cp(n, win, ["zt%d" % b, "tm%d" % b, "selo"], ["xs%d" % b])
+        quant(T.qx[:, :], T.qxs[:, :], T.xs[:, :], ["xs%d" % b for b in range(4)], ["qx"])
+    dmas("do", [("y", T.oc[:, :], T.qx[:, 0:C].bitcast(dt.uint8))] + [("s", T.osc[4 * i:4 * i + 4, :], T.qxs[32 * i:32 * i + 4, 0:C]) for i in range(4)], ["qx"], ["oc"])
+    mm(0, C, T.vq[:, :], T.vqs[:, :], T.qx[:, :], T.qxs[:, :], ["vq", "qx"])
+    act(T.yo[:, :], T.ps[:, 0:C], AF.Copy, ["ps0"], ["yo"])
+    dmas("do", [("y", T.y[:, :], T.yo[:, :])], ["yo"], ["y"])
+    for s in ("do", "cv", "cs", "ct", "cg", "dx", "du", "dv", "dw", "dk", "da", "rw", "re", "rl"):
+        if seen["y"].get(s, 0) < cnt[s]:
+            need("y", ("end", s, cnt[s]))

@@ -18,27 +18,28 @@ SCRATCH = {
     "dg": _sb(516, BF), "dh": _sb(516, BF), "dk": _sb(516, BF),
     "eh": _sb(512, F8), "ehs": _sb(512, U8), "ek": _sb(512, F8), "eks": _sb(512, U8),
     "cwt": _sb(512, BF), "cw": _sb(768, F8), "cws": _sb(768, U8),
-    "ip": _sb(4, I32), "ir": _sb(C, I32), "iw": _sb(C, I32), "io8": _sb(8, I32), "i4": _sb(4, I32), "ia": _sb(16, I32),
+    "ip": _sb(4, I32), "ir": _sb(C, I32), "iw": _sb(C, I32), "io8": _sb(8, I32), "i4": _sb(4, I32),
     "kf": _sb(96, F32), "ki": _sb(32, I32), "jrow": _sb(C, F32), "wmask": _sb(C, F32), "seg": _sb(C, F32),
-    "ones": _sb(C, F32), "pw4": _sb(16, F32), "pw2": _sb(16, F32), "tmp8": _sb(16, F32), "oneh": _sb(8, F32),
-    "sl": _sb(12, U16), "mg": _sb(176, F32), "phi": _sb(960, F32), "phit": _sb(960, F32), "j24": _sb(24, F32),
-    "j16": _sb(20, F32), "code": _sb(24, F32), "res": _sb(60, F32),
+    "ones": _sb(128, F32), "pw4": _sb(16, F32), "pw2": _sb(16, F32), "tmp8": _sb(16, F32), "oneh": _sb(8, F32),
+    "sl": _sb(12, U16), "mg": _sb(176, F32), "phi0": _sb(C, F32), "phit": _sb(C, F32), "phi": _sb(960, F32), "j24": _sb(24, F32),
+    "j16": _sb(20, F32), "codv": _sb(24, F32), "res": _sb(60, F32),
     "bt": _sb(1280, BF), "bq": _sb(C, F8), "bqs": _sb(C, U8),
     "w4": _sb(C, F32), "gw": _sb(176, F32), "gm": _sb(176, F32), "ms": _sb(60, F32), "msg": _sb(60, U16), "pw": _sb(60, U16),
     "wm": _sb(C, F32), "wsc": _sb(C, F32), "wl": _sb(20, U16),
-    "wj": _sb(3, F32), "wji": _sb(3, I32), "ob": _sb(24, I32), "u0": _sb(24, F32), "u1": _sb(24, F32), "sg": _sb(24, F32),
+    "wj": _sb(3, F32), "wji": _sb(3, I32), "ob": _sb(24, I32), "obf": _sb(24, F32), "nb": _sb(24, F32),
+    "u0": _sb(24, F32), "u1": _sb(24, F32), "sg": _sb(24, F32),
     "obb": _sb(24, F32), "ct": _sb(768, BF), "pt": _sb(768, BF), "n0": _sb(960, F32), "nn": _sb(960, F32),
     "sm": _sb(60, I32), "vi": _sb(60, I32), "dd": _sb(480, I32), "vv": _sb(60, F32), "vz": _sb(60, F32), "sc": _sb(60, F32),
     "kl": _sb(60, F32), "keep": _sb(24, F32), "pks": _sb(24, F32), "pb": _sb(24, F32), "base": _sb(8, F32),
-    "zz": _sb(7 * 960, BF), "zv": _sb(960, F32), "so": _sb(480, BF), "mn": _sb(24, F32), "ac": _sb(24 * 8, F32),
+    "zz": _sb(6 * 960, BF), "zv": _sb(960, F32), "so": _sb(480, BF), "s0": _sb(480, F32), "mn": _sb(24, F32), "ac": _sb(48, F32),
     "kg": _sb(32, F32), "kt": _sb(32, F32), "ag": _sb(32, F32), "at": _sb(32, F32), "uk": _sb(32, F32), "ua": _sb(32, F32),
     "us": _sb(32, F32), "uto": _sb(32, F32), "ust": _sb(32, F32), "utt": _sb(32, F32), "kw": _sb(32, F32), "pq": _sb(160, F32),
     "poff": _sb(20, U16), "selo": _sb(20, U16), "lw": _sb(C, F32), "lm": _sb(128, F32), "ls": _sb(128, F32), "loff": _sb(8, U16),
     "aw": _sb(32, F32), "aoff": _sb(20, U16),
-    "fb": _sb(1280, BF), "fc": _sb(1280, BF), "zt": _sb(4 * 448, BF), "et": _sb(512, BF), "qe": _sb(128, F8), "qes": _sb(128, U8),
-    "qa": _sb(128, F8), "qas": _sb(128, U8), "yo": _sb(C, F32),
+    "fb": _sb(1280, BF), "fc": _sb(640, BF), "zg": _sb(640, F32), "zt": _sb(4 * 448, BF), "et": _sb(512, BF),
+    "qe": _sb(128, F8), "qes": _sb(128, U8), "qa": _sb(128, F8), "qas": _sb(128, U8), "yo": _sb(C, F32),
 }
-SEMAPHORES = ["cv", "cs", "ct", "cg", "dx", "du", "dv", "dw", "dk", "da", "do", "rw", "re", "rl"]
+SEMAPHORES = ["cv", "cs", "ct", "cg", "dx", "du", "dv", "dw", "dk", "da", "do", "dp", "rw", "re", "rl"]
 
 
 def rank_program(g, core, T, topo):
@@ -49,7 +50,6 @@ def rank_program(g, core, T, topo):
     partner = T.cores[rank ^ 1]
     rid, pid = topo.addr(partner)[:2]
     mask, neng = topo.mask(core, partner), len(topo.engines(core, partner))
-    codv = T["code"]
     eng = {"v": g.vector, "s": g.scalar, "t": g.tensor, "g": g, "y": g.sync}
     own = {"v": "cv", "s": "cs", "t": "ct", "g": "cg"}
     cnt = {s: 0 for s in SEMAPHORES}
@@ -101,11 +101,11 @@ def rank_program(g, core, T, topo):
 
     vec, sca = g.vector, g.scalar
 
-    def ts(o, i, s1, o1, s2, o2, reads, writes):
+    def ts(o, i, s1, o1, s2, o2, reads, writes, waw=True):
         if o2 is None:
-            op("v", vec.tensor_scalar, (o, i, s1, None, o1), reads, writes)
+            op("v", vec.tensor_scalar, (o, i, s1, None, o1), reads, writes, None, waw)
         else:
-            op("v", vec.tensor_scalar, (o, i, s1, s2, o1, o2), reads, writes)
+            op("v", vec.tensor_scalar, (o, i, s1, s2, o1, o2), reads, writes, None, waw)
 
     def tt(o, a, b, f, reads, writes):
         op("v", vec.tensor_tensor, (o, a, b, f), reads, writes)
@@ -128,28 +128,31 @@ def rank_program(g, core, T, topo):
     def mm(bank, n, l, ls, r, rs, reads, start=True, stop=True):
         op("t", g.tensor.matmul_mx, (T.ps[:, 512 * bank:512 * bank + n], l, ls, r, rs, start, stop), reads, ["ps%d" % bank], waw=start)
 
+    def iota(o, pat, base, cm, w, **kw):
+        op("g", g.iota, (o, pat, base, cm), [], w, kw)
+
     dmas("dx", [("y", T.x0[:, 0:640], T.x[:, 0:640]), ("s", T.x0[:, 640:1280], T.x[:, 640:1280])], [], ["x"])
-    dmas("du", [("y", T.ut[:], T.u[:, :])], [], ["ut"])
+    dmas("du", [("s", T.ut[:], T.u[:, :])], [], ["ut"])
     dmas("dw", [("y", T.wq[:, 0:512].bitcast(dt.uint8), T.wc[:, 0:2048]), ("y", T.wqs[:, 0:512], T.ws[:, 0:512])], [], ["w"])
     dmas("dv", [("y", T.vt[:], T.v[:, :])], [], ["vt"])
 
-    def iota(o, pat, base, cm, w):
-        op("g", g.iota, (o, pat, base, cm), [], w)
     iota(T.ip[:, 0:1], [[1, 1]], 0, 1, ["ip"])
     iota(T.io8[:, :], [[-16, 8]], 0, 1, ["io8"])
-    iota(T.iw[:, :], [[1, C]], 128, -1, ["iw"])
-    iota(T.ir[:, :], [[1, C]], 0, 0, ["ir"])
     iota(T.i4[:, :], [[16, 4]], 0, 0, ["i4"])
+    iota(T.iw[:, :], [[1, C]], 128, -1, ["iw"])
     fill(T.ones[:, :], 1.0, ["ones"])
-    fill(T.dg[:, :], 0.5, ["dg"])
-    op("g", g.affine_select, (T.dh[:, :], T.dg[:, :], [[-1, 516]], A.is_equal, 0.0, 3, 4), ["dg"], ["dh"])
-    fill(T.bt[:, :], 0.0, ["bt"])
-    fill(T.cwt[:, :], 0.0, ["cwt"])
     fill(T.tmp8[:, 8:16], 0.0, ["t8b"])
     for base, buf in ((4.0, T.pw4), (2.0, T.pw2)):
         fill(T.tmp8[:, 0:8], base, ["t8"])
         scan(buf[:, 0:8], T.tmp8[:, 0:8], T.tmp8[:, 8:16], 1.0 / base, A.mult, A.add, ["t8", "t8b"], ["pw"])
         cp(buf[:, 8:16], buf[:, 0:8], ["pw"], ["pw"])
+    fill(T.cwt[:, :], 0.0, ["cwt"])
+    fill(T.bt[:, :], 0.0, ["bt"])
+    fill(T.dg[:, :], 0.5, ["dg"])
+    op("g", g.affine_select, (T.dh[:, :], T.dg[:, :], [[-1, 516]], A.is_equal, 0.0, 3, 4), ["dg"], ["dh"])
+    iota(T.phi0[0:32, :], [[1, C]], 0, -1, ["phi0"], allow_small_or_imprecise_dtypes=True)
+    iota(T.ir[:, :], [[1, C]], 0, 0, ["ir"])
+    iota(T.jrow[:, :], [[1, C]], 0, 0, ["jrow"], allow_small_or_imprecise_dtypes=True)
     ts(T.oneh[:, :], T.io8[:, :], 0.0, A.is_equal, None, None, ["io8"], ["oneh"])
 
     def weights(t):
@@ -161,96 +164,103 @@ def rank_program(g, core, T, topo):
             o = 128 * (2 * t + h)
             quant(T.cw[:, o:o + 128], T.cws[:, o:o + 128], T.cwt[:, :], ["cwt"], ["cw%d" % (2 * t + h)])
     weights(0)
+
+    kf, k, ki = T.kf, ["kf"], ["ki"]
+    fill(kf[:, 0:12], 0.0, k)
+    op("v", vec.tensor_scalar, (T.ki[:, 0:1], T.ip[:, 0:1], 15, None, A.bitwise_and), ["ip"], ki)
+    op("v", vec.tensor_scalar, (T.ki[:, 1:2], T.ip[:, 0:1], 63, None, A.bitwise_and), ["ip"], ki, waw=False)
+    cp(kf[:, 13:14], T.ki[:, 0:1], ki, ["p16"])
+    cp(kf[:, 0:1], T.ip[:, 0:1], ["ip"], k)
+    ts(kf[:, 1:2], T.ip[:, 0:1], 128.0, A.add, None, None, ["ip"], k, False)
+    ts(kf[:, 2:3], T.ki[:, 1:2], 256.0, A.add, None, None, ki, k, False)
+    ts(kf[:, 8:12], T.i4[:, :], kf[:, 13:14], A.add, None, None, ["i4", "p16"], k, False)
+    ts(kf[:, 4:7], kf[:, 0:3], kf[:, 13:14], A.subtract, None, None, k + ["p16"], k)
+
+    def floor20(o, i, n):
+        ts(kf[:, 72:72 + n], i, 0.05, A.mult, -0.475, A.add, k, ["fl"])
+        cp(T.ki[:, 16:16 + n], kf[:, 72:72 + n], ["fl"], ["fli"])
+        cp(o, T.ki[:, 16:16 + n], ["fli"], k)
+    floor20(kf[:, 16:28], kf[:, 0:12], 12)
+    tt(kf[:, 28:31], kf[:, 16:19], kf[:, 20:23], A.is_equal, k, ["ma"])
+    ts(kf[:, 31:34], kf[:, 28:31], -1.0, A.mult, 1.0, A.add, ["ma"], ["mb"])
+    ts(kf[:, 24:28], kf[:, 24:28], 2.0, A.min, None, None, k, k)
+    ts(kf[:, 36:40], kf[:, 24:28], -20.0, A.mult, None, None, k, ["l1"])
+    tt(kf[:, 36:40], kf[:, 36:40], kf[:, 8:12], A.add, k + ["l1"], ["l1"])
+    ts(kf[:, 34:35], kf[:, 6:7], -256.0, A.add, kf[:, 4:5], A.subtract, k, ["l2"])
+    ts(kf[:, 44:48], kf[:, 24:28], 2.0, A.is_equal, kf[:, 34:35], A.mult, k + ["l2"], ["l3"])
+    ts(kf[:, 40:44], kf[:, 24:28], 128.0, A.mult, kf[:, 4:5], A.add, k, ["l4"])
+    tt(kf[:, 40:44], kf[:, 40:44], kf[:, 44:48], A.add, ["l3", "l4"], k)
+    floor20(kf[:, 48:52], kf[:, 40:44], 4)
+    ts(kf[:, 52:56], kf[:, 48:52], 1.0, A.add, 15.0, A.min, k, ["l5"])
+    for o, key in ((48, "kf"), (52, "l5")):
+        ts(kf[:, o:o + 4], kf[:, o:o + 4], 20.0, A.mult, None, None, [key], [key])
+    for o, key in ((48, "kf"), (52, "l5")):
+        tt(kf[:, o:o + 4], kf[:, o:o + 4], kf[:, 36:40], A.add, [key, "l1"], [key])
+    ts(T.sl[:, 0:8], kf[:, 48:56], 319.0, A.min, None, None, ["kf", "l5"], ["sl"])
+    cp(T.sl[:, 8:11], kf[:, 0:3], k, ["sl2"])
+    fill(T.mg[:, :], 0.0, ["mg"])
+    for t in range(3):
+        ts(T.mg[:, 20 * t:20 + 20 * t], T.ones[:, 0:20], kf[:, 28 + t:29 + t], A.mult, None, None, ["ones", "ma"], ["mg"], t == 0)
+        ts(T.mg[:, 64 + 20 * t:84 + 20 * t], T.ones[:, 0:20], kf[:, 31 + t:32 + t], A.mult, None, None, ["ones", "mb"], ["mg"], False)
     quant(T.uq[:, :], T.uqs[:, :], T.ut[:, :], ["ut"], ["uq"])
     quant(T.qx[:, :], T.qxs[:, :], T.x0[:, :], ["x"], ["qx"])
 
-    kf, k = T.kf, ["kf"]
-    for c, (m, sh) in enumerate(((15, 0), (31, 0), (1, 4), (3, 5))):
-        op("v", vec.tensor_scalar, (T.ki[:, c:c + 1], T.ip[:, 0:1], sh, m, A.logical_shift_right, A.bitwise_and), ["ip"], ["ki"])
-    cp(kf[:, 3:4], T.ki[:, 0:1], ["ki"], k)
-    ts(kf[:, 4:5], T.ki[:, 3:4], 3.0, A.is_equal, -64.0, A.mult, ["ki"], k)
-    cp(kf[:, 13:14], T.ki[:, 1:2], ["ki"], k)
-    ts(kf[:, 14:15], T.ki[:, 2:3], 16.0, A.mult, None, None, ["ki"], k)
-    ts(kf[:, 0:1], T.ki[:, 3:4], 96.0, A.mult, kf[:, 13:14], A.add, ["ki", "kf"], k)
-    ts(kf[:, 5:6], T.ki[:, 3:4], 96.0, A.mult, kf[:, 14:15], A.add, ["ki", "kf"], k)
-    for t in (1, 2):
-        ts(kf[:, t:t + 1], kf[:, 0:1], 32.0 * t, A.add, kf[:, 4:5], A.add, k, k)
-
-    def floor20(o, i, n):
-        ts(kf[:, 80:80 + n], i, 0.05, A.mult, -0.475, A.add, k, ["fl"])
-        cp(T.ki[:, 16:16 + n], kf[:, 80:80 + n], ["fl"], ["fli"])
-        cp(o, T.ki[:, 16:16 + n], ["fli"], k)
-    ts(kf[:, 16:19], kf[:, 0:3], kf[:, 3:4], A.subtract, None, None, k, k)
-    floor20(kf[:, 20:23], kf[:, 16:19], 3)
-    floor20(kf[:, 24:27], kf[:, 0:3], 3)
-    tt(kf[:, 6:9], kf[:, 20:23], kf[:, 24:27], A.is_equal, k, k)
-    ts(kf[:, 9:12], kf[:, 6:9], -1.0, A.mult, 1.0, A.add, k, k)
-    ts(kf[:, 28:32], T.i4[:, :], kf[:, 3:4], A.add, None, None, ["i4", "kf"], k)
-    floor20(kf[:, 32:36], kf[:, 28:32], 4)
-    ts(kf[:, 32:36], kf[:, 32:36], 2.0, A.min, None, None, k, k)
-    ts(kf[:, 36:40], kf[:, 32:36], -20.0, A.mult, None, None, k, k)
-    tt(kf[:, 36:40], kf[:, 36:40], kf[:, 28:32], A.add, k, k)
-    ts(kf[:, 40:44], kf[:, 32:36], 32.0, A.mult, kf[:, 5:6], A.add, k, k)
-    ts(kf[:, 44:48], kf[:, 32:36], 1.0, A.is_ge, kf[:, 4:5], A.mult, k, k)
-    tt(kf[:, 40:44], kf[:, 40:44], kf[:, 44:48], A.add, k, k)
-    floor20(kf[:, 48:52], kf[:, 40:44], 4)
-    ts(kf[:, 52:56], kf[:, 48:52], 1.0, A.add, 15.0, A.min, k, k)
-    for o in (48, 52):
-        ts(kf[:, o:o + 4], kf[:, o:o + 4], 20.0, A.mult, None, None, k, k)
-        tt(kf[:, o:o + 4], kf[:, o:o + 4], kf[:, 36:40], A.add, k, k)
-        ts(kf[:, o:o + 4], kf[:, o:o + 4], 319.0, A.min, None, None, k, k)
-    cp(T.sl[:, 0:3], kf[:, 0:3], k, ["sl"])
-    cp(T.sl[:, 3:11], kf[:, 48:56], k, ["sl"])
-    op("v", vec.tensor_scalar, (T.iw[:, :], T.iw[:, :], 15, None, A.bitwise_and), ["iw"], ["iw"])
-    ts(T.wmask[:, :], T.iw[:, :], 0.0, A.is_equal, None, None, ["iw"], ["wmask"])
-    fill(T.mg[:, :], 0.0, ["mg"])
-    cp(T.mg[:, 0:48], T.wmask[:, 0:48], ["wmask"], ["mg"])
-    for t in range(3):
-        ts(T.mg[:, 48 + 20 * t:68 + 20 * t], T.ones[:, 0:20], kf[:, 6 + t:7 + t], A.mult, None, None, ["ones", "kf"], ["mg"])
-        ts(T.mg[:, 112 + 20 * t:132 + 20 * t], T.ones[:, 0:20], kf[:, 9 + t:10 + t], A.mult, None, None, ["ones", "kf"], ["mg"])
+    def mask_constants():
+        op("v", vec.tensor_scalar, (T.iw[:, :], T.iw[:, :], 15, None, A.bitwise_and), ["iw"], ["iw"])
+        ts(T.wmask[:, :], T.iw[:, :], 0.0, A.is_equal, None, None, ["iw"], ["wmask"])
+        cp(T.mg[:, 128:176], T.wmask[:, 0:48], ["wmask"], ["mg2"])
 
     def more_constants():
-        cp(T.jrow[:, :], T.ir[:, :], ["ir"], ["jrow"])
+        p = ["phi0"]
+        ts(T.phit[0:32, 0:32], T.phi0[0:32, 0:32], 0.0, A.is_lt, 320.0, A.mult, p, ["phit"])
+        tt(T.phi0[0:32, 0:32], T.phi0[0:32, 0:32], T.phit[0:32, 0:32], A.add, p + ["phit"], p)
+        ts(T.phit[0:32, :], T.phi0[0:32, :], 2.0, A.mult, -256.0, A.add, p, ["phit"])
+        tt(T.phi0[0:32, :], T.phi0[0:32, :], T.phit[0:32, :], A.max, p + ["phit"], p)
+        items = []
+        for t in range(3):
+            for a in range(4):
+                off = 128 * t + 32 * (a if t < 2 else a % 2)
+                items.append(("y", T.phi[32 * a:32 * a + 32, 320 * t + off:320 * t + 320], T.phi0[0:32, 0:320 - off]))
+                if off:
+                    items.append(("y", T.phi[32 * a:32 * a + 32, 320 * t:320 * t + off], T.phi0[0:32, 320 - off:320]))
+        dmas("dp", items, p, ["phi"])
+        for b in range(4):
+            quant(T.eh[:, 128 * b:128 * b + 128], T.ehs[:, 128 * b:128 * b + 128], T.dh[:, 3 - b:515 - b], ["dh"], ["eh%d" % b])
+        for i in range(8):
+            op("v", vec.memset, (T.codv[:, 3 * i:3 * i + 3], 1024.0 * (i + 1)), [], ["codv"], None, False)
+        for t in range(3):
+            fill(T.ct[:, 256 * t:256 * t + 1], 16384.0, ["ct%d" % t])
+
+    def more_constants2():
         op("v", vec.tensor_scalar, (T.iw[:, :], T.ir[:, :], 15, None, A.bitwise_and), ["ir"], ["iw"])
         ts(T.seg[:, :], T.iw[:, :], 0.0, A.not_equal, None, None, ["iw"], ["seg"])
-        for i in range(8):
-            fill(codv[:, 3 * i:3 * i + 3], 1024.0 * (i + 1), ["code"])
         fill(T.res[:, :], 0.0, ["res"])
         for t in range(3):
             fill(T.res[:, 20 * t:20 * t + 1], 2.0, ["res"])
-            fill(T.ct[:, 256 * t:256 * t + 1], 0.0, ["ct%d" % t])
             fill(T.pt[:, 256 * t:256 * t + 1], 0.0, ["pt%d" % t])
-            s = slice(320 * t, 320 * t + 320)
-            ts(T.phi[:, s], T.jrow[:, :], kf[:, t:t + 1], A.subtract, None, None, ["jrow", "kf"], ["phi"])
-        ts(T.phit[:, :], T.phi[:, :], 0.0, A.is_lt, 320.0, A.mult, ["phi"], ["phit"])
-        tt(T.phi[:, :], T.phi[:, :], T.phit[:, :], A.add, ["phi", "phit"], ["phi"])
-        ts(T.phit[:, :], T.phi[:, :], 2.0, A.mult, -256.0, A.add, ["phi"], ["phit"])
-        tt(T.phi[:, :], T.phi[:, :], T.phit[:, :], A.max, ["phi", "phit"], ["phi"])
-        for b in range(4):
-            quant(T.eh[:, 128 * b:128 * b + 128], T.ehs[:, 128 * b:128 * b + 128], T.dh[:, 3 - b:515 - b], ["dh"], ["eh"])
-
-    def later_constants():
-        for i in range(8):
-            cp(T.j24[:, 3 * i:3 * i + 3], kf[:, 0:3], k, ["j24"])
-        ts(T.j16[:, :], T.ir[:, 0:20], 16.0, A.mult, kf[:, 3:4], A.add, ["ir", "kf"], ["j16"])
         for n in ("kg", "ag", "uk", "ua"):
             fill(T[n][:, :], 0.0, [n])
+        for i in range(8):
+            op("v", vec.tensor_copy, (T.j24[:, 3 * i:3 * i + 3], kf[:, 0:3]), k, ["j24"], None, False)
+        ts(T.j16[:, :], T.ir[:, 0:20], 16.0, A.mult, kf[:, 13:14], A.add, ["ir", "p16"], ["j16"])
+
+    def later_constants():
         ts(T.dk[:, :], T.dh[:, :], 64.0, A.mult, None, None, ["dh"], ["dk"])
         for b in range(4):
-            quant(T.ek[:, 128 * b:128 * b + 128], T.eks[:, 128 * b:128 * b + 128], T.dk[:, 3 - b:515 - b], ["dk"], ["ek"])
-        quant(T.vq[:, :], T.vqs[:, :], T.vt[:, :], ["vt"], ["vq"])
+            quant(T.ek[:, 128 * b:128 * b + 128], T.eks[:, 128 * b:128 * b + 128], T.dk[:, 3 - b:515 - b], ["dk"], ["ek%d" % b])
         weights(1)
         weights(2)
+        quant(T.vq[:, :], T.vqs[:, :], T.vt[:, :], ["vt"], ["vq"])
 
     def to_wrapped(src, dst, sem, queues, key_in, key_out):
         items = []
-        for a in range(4):
-            n = 3 if a < 3 else 1
+        for t in range(3):
+            n = 4 if t < 2 else 2
             for gr in range(8):
                 G, h = divmod(gr, 2)
                 items.append((queues[len(items) % len(queues)],
-                              dst[32 * G + 6 * a:32 * G + 6 * a + 2 * n, 16 * h:16 * h + 16],
-                              src[32 * a + 3 * gr:32 * a + 3 * gr + n, 0:32]))
+                              dst[32 * G + 8 * t:32 * G + 8 * t + 2 * n, 16 * h:16 * h + 16],
+                              src[3 * gr + t:32 * n:32, 0:32]))
         dmas(sem, items, [key_in], [key_out])
 
     for t in range(R):
@@ -268,59 +278,82 @@ def rank_program(g, core, T, topo):
             o = 128 * (2 * t + h)
             mm(1 + h, C, T.cw[:, o:o + 128], T.cws[:, o:o + 128], T.bq[:, :], T.bqs[:, :], ["cw%d" % (2 * t + h), "bq"])
         act(T.w4[:, :], T.ps[:, 512:512 + C], AF.Copy, ["ps1"], ["w4"])
-        cp(T.gw[:, :], T.w4[:, 0:C].indirect(T.sl[:, 0:11]), ["w4", "sl"], ["gw"])
-        tt(T.gm[:, :], T.gw[:, :], T.mg[:, :], A.mult, ["gw", "mg"], ["gm"])
-        tt(T.ms[:, :], T.gm[:, 48:108], T.gm[:, 112:172], A.add, ["gm"], ["ms"])
+        if t == 0:
+            mask_constants()
+        cp(T.gw[:, 0:128], T.w4[:, 0:C].indirect(T.sl[:, 0:8]), ["w4", "sl"], ["gw"])
+        tt(T.gm[:, 0:128], T.gw[:, 0:128], T.mg[:, 0:128], A.mult, ["gw", "mg"], ["gm"])
+        tt(T.ms[:, :], T.gm[:, 0:60], T.gm[:, 64:124], A.add, ["gm"], ["ms"])
         cp(T.msg[:, :], T.ms[:, :], ["ms"], ["msg"])
         waits("g", ["msg"], [])
         g.remote_dma(T.pw[:, 0:60], T.msg[:, 0:60], T.sem["rw"], T.sem["rl"], pid, rid, mask)
         cnt["rl"] += neng
         cnt["rw"] += neng
         note(("dma", "rl", None), ["msg"], [])
+        cp(T.gw[:, 128:176], T.w4[:, 0:C].indirect(T.sl[:, 8:11]), ["w4", "sl2"], ["gw2"])
+        tt(T.gm[:, 128:176], T.gw[:, 128:176], T.mg[:, 128:176], A.mult, ["gw2", "mg2"], ["gm2"])
+        for c in range(3):
+            op("v", vec.tensor_reduce, (T.wj[:, c:c + 1], T.gm[:, 128 + 16 * c:144 + 16 * c], X, A.add), ["gm2"], ["wj"], waw=False)
+        cp(T.wji[:, :], T.wj[:, :], ["wj"], ["wji"])
         if t == 0:
             more_constants()
-        for b in range(4):
-            mm(4 + b, C, T.eh[:, 128 * b:128 * b + 128], T.ehs[:, 128 * b:128 * b + 128], T.qx[:, :], T.qxs[:, :], ["eh", "qx"])
-            act(T.fb[:, 320 * b:320 * b + 320], T.ps[:, 512 * (4 + b):512 * (4 + b) + C], AF.Copy, ["ps%d" % (4 + b)], ["fb%d" % b])
-            act(T.fc[:, 320 * b:320 * b + 320], T.ps[:, 512 * (4 + b):512 * (4 + b) + C], AF.Copy, ["ps%d" % (4 + b)], ["fc%d" % b])
-        for c in range(3):
-            op("v", vec.tensor_reduce, (T.wj[:, c:c + 1], T.gm[:, 16 * c:16 * c + 16], X, A.add), ["gm"], ["wj"], waw=False)
-        cp(T.wji[:, :], T.wj[:, :], ["wj"], ["wji"])
         for i in range(8):
             op("v", vec.tensor_scalar, (T.ob[:, 3 * i:3 * i + 3], T.wji[:, :], 2 * i, 1, A.logical_shift_right, A.bitwise_and), ["wji"], ["ob"], waw=False)
-        tt(T.u0[:, :], T.ob[:, :], codv[:, :], A.mult, ["ob", "code"], ["u0"])
-        tt(T.u1[:, :], codv[:, :], T.u0[:, :], A.subtract, ["u0", "code"], ["u1"])
+        tt(T.u0[:, :], T.ob[:, :], T.codv[:, :], A.mult, ["ob", "codv"], ["u0"])
+        cp(T.obf[:, :], T.ob[:, :], ["ob"], ["obf"])
+        ts(T.nb[:, :], T.ob[:, :], -1.0, A.mult, 1.0, A.add, ["ob"], ["nb"])
+        tt(T.u1[:, :], T.codv[:, :], T.u0[:, :], A.subtract, ["u0", "codv"], ["u1"])
+        cols = ["u0", "u1", "nb", "obf"]
+
+        def table(i, c):
+            n = 1 << i
+            lo, hi = slice(256 * c, 256 * c + n), slice(256 * c + n, 256 * c + 2 * n)
+            q = slice(3 * i + c, 3 * i + c + 1)
+            a, b = "ct%d" % c, "ct%dh" % c
+            if c == 0:
+                ts(T.ct[:, hi], T.ct[:, lo], T.obf[:, q], A.mult, T.u1[:, q], A.add, [a, b] + cols, [b])
+                ts(T.ct[:, lo], T.ct[:, lo], T.nb[:, q], A.mult, T.u0[:, q], A.add, [a, b] + cols, [a])
+            else:
+                act(T.ct[:, hi], T.ct[:, lo], AF.Identity, [a, b] + cols, [b], scale=T.obf[:, q], bias=T.u1[:, q])
+                act(T.ct[:, lo], T.ct[:, lo], AF.Identity, [a, b] + cols, [a], scale=T.nb[:, q], bias=T.u0[:, q])
+        for i in range(8):
+            for c in (1, 2):
+                table(i, c)
+        for b in range(4):
+            p = ["ps%d" % (4 + b)]
+            mm(4 + b, C, T.eh[:, 128 * b:128 * b + 128], T.ehs[:, 128 * b:128 * b + 128], T.qx[:, :], T.qxs[:, :], ["eh%d" % b, "qx"])
+            act(T.fb[:, 320 * b:320 * b + 320], T.ps[:, 512 * (4 + b):512 * (4 + b) + C], AF.Copy, p, ["fb%d" % b])
+            if b < 2:
+                act(T.fc[:, 320 * b:320 * b + 320], T.ps[:, 512 * (4 + b):512 * (4 + b) + C], AF.Copy, p, ["fc%d" % b])
+        if t == 0:
+            more_constants2()
         ts(T.sg[:, :], T.ob[:, :], -32768.0, A.mult, 16384.0, A.add, ["ob"], ["sg"])
         ts(T.obb[:, :], T.ob[:, :], 16384.0, A.mult, None, None, ["ob"], ["obb"])
         tt(T.wm[:, :], T.ps[:, 1024:1024 + C], T.wmask[:, :], A.mult, ["ps2", "wmask"], ["wm"])
+        table(0, 0)
         scan(T.wsc[:, :], T.seg[:, :], T.wm[:, :], 0.0, A.mult, A.add, ["seg", "wm"], ["wsc"])
+        table(1, 0)
         cp(T.wl[:, :], T.wsc[:, 15:C:16], ["wsc"], ["wl"])
-        for i in range(8):
-            n = 1 << i
-            for c in range(3):
-                lo, hi = slice(256 * c, 256 * c + n), slice(256 * c + n, 256 * c + 2 * n)
-                col = slice(3 * i + c, 3 * i + c + 1)
-                ts(T.ct[:, hi], T.ct[:, lo], T.u1[:, col], A.max, None, None, ["ct%d" % c, "ct%dh" % c, "u1"], ["ct%dh" % c])
-            for c in range(3):
-                lo = slice(256 * c, 256 * c + n)
-                col = slice(3 * i + c, 3 * i + c + 1)
-                ts(T.ct[:, lo], T.ct[:, lo], T.u0[:, col], A.max, None, None, ["ct%d" % c, "ct%dh" % c, "u0"], ["ct%d" % c])
-        for c in range(3):
+        for i in range(2, 8):
+            table(i, 0)
+
+        def pairs(c):
             s = slice(320 * c, 320 * c + 320)
             tt(T.n0[:, s], T.ct[:, 256 * c:256 * c + 256].indirect(T.wl[:, 0:20]), T.phi[:, s], A.add,
                ["ct%d" % c, "ct%dh" % c, "wl", "phi"], ["n0%d" % c])
             if t < R - 1:
-                fill(T.ct[:, 256 * c:256 * c + 1], 0.0, ["ct%d" % c])
-        if t == 0:
-            later_constants()
+                fill(T.ct[:, 256 * c:256 * c + 1], 16384.0, ["ct%d" % c])
+        pairs(0)
+        pairs(1)
         note(("dma", "rw", cnt["rw"]), [], ["pw"])
         for c in range(3):
             ts(T.sm[:, 20 * c:20 * c + 20], T.pw[:, 20 * c:20 * c + 20], T.wj[:, c:c + 1], A.add, None, None, ["pw", "wj"], ["sm%d" % c])
         op("v", vec.tensor_scalar, (T.vi[:, :], T.sm[:, :], 0x5555, None, A.bitwise_and), ["sm0", "sm1", "sm2"], ["vi"])
         ts(T.vz[:, :], T.vi[:, :], 0.0, A.is_equal, None, None, ["vi"], ["vz"])
         ts(T.vv[:, :], T.vi[:, :], 2.0 ** -15, A.mult, None, None, ["vi"], ["vv"])
-        for i in range(8):
+
+        def digit(i):
             op("v", vec.tensor_scalar, (T.dd[:, 60 * i:60 * i + 60], T.vi[:, :], 4 ** i, None, A.bitwise_and), ["vi"], ["dd%d" % i])
+        digit(0)
         tt(T.vv[:, :], T.vv[:, :], T.vz[:, :], A.max, ["vv", "vz"], ["vv"])
         for i in range(8):
             scan(T.sc[:, :], T.res[:, :], T.vv[:, :], 2.0, A.max, A.min, ["res", "vv"], ["sc"])
@@ -332,6 +365,8 @@ def rank_program(g, core, T, topo):
             c3 = slice(3 * i, 3 * i + 3)
             ts(T.keep[:, c3], T.sc[:, 19:60:20], 2.0 ** -14 * 4 ** i, A.is_lt, None, None, ["sc"], ["keep%d" % i])
             if i < 7:
+                if i < 6:
+                    digit(i + 1)
                 tt(T.vv[:, :], T.vv[:, :], T.kl[:, :], A.max, ["vv", "kl0", "kl1", "kl2"], ["vv"])
             tt(T.pks[:, c3], T.keep[:, c3], T.sg[:, c3], A.mult, ["keep%d" % i, "sg"], ["pks%d" % i])
             n = 1 << i
@@ -341,44 +376,57 @@ def rank_program(g, core, T, topo):
                         bias=T.pks[:, 3 * i + c:3 * i + c + 1])
         keeps = ["keep%d" % i for i in range(8)]
         tt(T.pb[:, :], T.keep[:, :], T.obb[:, :], A.mult, keeps + ["obb"], ["pb"])
+        by_group(lambda o, i: cp(T.kg[:, o], T.keep[:, i], keeps, ["kg"]))
         for c in range(3):
             op("v", vec.tensor_reduce, (T.base[:, c:c + 1], T.pb[:, c:24:3], X, A.add), ["pb"], ["base"], waw=False)
+        op("v", vec.transpose, (T.kt[:, :], T.kg[:, :]), ["kg"], ["kt"])
         tt(T.base[:, 3:6], T.base[:, 0:3], T.pks[:, 21:24], A.add, ["base", "pks7"], ["base2"])
         for c in range(3):
             lo, hi = slice(256 * c, 256 * c + 128), slice(256 * c + 128, 256 * c + 256)
             act(T.pt[:, hi], T.pt[:, lo], AF.Identity, ["pt%d" % c, "base2"], ["pt%dh" % c], bias=T.base[:, 3 + c:4 + c])
             act(T.pt[:, lo], T.pt[:, lo], AF.Identity, ["pt%d" % c, "base"], ["pt%d" % c], bias=T.base[:, c:c + 1])
-        by_group(lambda o, i: cp(T.kg[:, o], T.keep[:, i], keeps, ["kg"]))
-        op("v", vec.transpose, (T.kt[:, :], T.kg[:, :]), ["kg"], ["kt"])
         to_wrapped(T.kt, T.uk, "dk", ["y"], "kt", "uk")
+        pairs(2)
         for c in range(3):
             s = slice(320 * c, 320 * c + 320)
             tt(T.nn[:, s], T.pt[:, 256 * c:256 * c + 256].indirect(T.wl[:, 0:20]), T.n0[:, s], A.add,
                ["pt%d" % c, "pt%dh" % c, "wl", "n0%d" % c], ["nn%d" % c])
         nns = ["nn0", "nn1", "nn2"]
+        for i in range(2, 8):
+            act(T.zz[:, 960 * (i - 2):960 * (i - 1)], T.nn[:, :], AF.Abs, nns, ["zz%d" % i], bias=-1024.0 * (i + 1))
+        for c in range(3):
+            o = 320 * c
+            scan(T.s0[:, 160 * c:160 * c + 160], T.nn[:, o:o + 160], T.nn[:, o + 160:o + 320], 65536.0, A.min, A.min, ["nn%d" % c], ["s0%d" % c])
+        ts(T.zv[:, :], T.nn[:, :], -2048.0, A.add, None, None, nns, ["zv"])
+        ts(T.mn[:, 0:3], T.s0[:, 159:480:160], -1024.0, A.add, None, None, ["s00", "s01", "s02"], ["mn"])
+        for c in range(3):
+            op("v", vec.tensor_reduce, (T.mn[:, 3 + c:4 + c], T.zv[:, 320 * c:320 * c + 320], X, A.min), ["zv"], ["mn"],
+               {"apply_absolute_value": True}, waw=False)
         if t < R - 1:
             for c in range(3):
                 fill(T.pt[:, 256 * c:256 * c + 1], 0.0, ["pt%d" % c])
-        for i in range(7):
-            act(T.zz[:, 960 * i:960 * i + 960], T.nn[:, :], AF.Abs, nns, ["zz%d" % i], bias=-1024.0 * (i + 1))
-        ts(T.zv[:, :], T.nn[:, :], -8192.0, A.add, None, None, nns, ["zv"])
-        for c in range(3):
-            op("v", vec.tensor_reduce, (T.mn[:, 21 + c:22 + c], T.zv[:, 320 * c:320 * c + 320], X, A.min), ["zv"], ["mn"],
-               {"apply_absolute_value": True}, waw=False)
-
-        def firsts(i):
+        for i in range(2, 8):
             for c in range(3):
-                o = 960 * i + 320 * c
+                o = 960 * (i - 2) + 320 * c
                 scan(T.so[:, 160 * c:160 * c + 160], T.zz[:, o:o + 160], T.zz[:, o + 160:o + 320], 65536.0, A.min, A.min, ["zz%d" % i], ["so%d" % c])
-            cp(T.mn[:, 3 * i:3 * i + 3], T.so[:, 159:480:160], ["so0", "so1", "so2"], ["mn"])
-        for i in range(5):
-            firsts(i)
+            op("v", vec.tensor_copy, (T.mn[:, 3 * i:3 * i + 3], T.so[:, 159:480:160]), ["so0", "so1", "so2"], ["mn"], None, False)
+        ac = T.ac
+        ts(ac[:, 0:24], T.mn[:, :], 0.5, A.mult, 128.0, A.add, ["mn"], ["ac0"])
+        ts(ac[:, 24:48], T.mn[:, :], 500.0, A.is_lt, None, None, ["mn"], ["ac1"])
+        tt(ac[:, 0:24], ac[:, 0:24], T.mn[:, :], A.min, ["ac0", "mn"], ["ac0"])
+        tt(ac[:, 24:48], ac[:, 24:48], T.keep[:, :], A.is_gt, ["ac1"] + keeps, ["ac1"])
+        tt(ac[:, 0:24], ac[:, 0:24], ac[:, 24:48], A.mult, ["ac0", "ac1"], ["ac0"])
+        tt(ac[:, 0:24], ac[:, 0:24], T.j24[:, :], A.add, ["ac0", "j24"], ["ac0"])
+        ts(ac[:, 24:48], ac[:, 0:24], 320.0, A.is_ge, -320.0, A.mult, ["ac0"], ["ac1"])
+        by_group(lambda o, i: tt(T.ag[:, o], ac[:, i], ac[:, 24 + i.start:24 + i.stop], A.add, ["ac0", "ac1"], ["ag"]))
+        op("v", vec.transpose, (T.at[:, :], T.ag[:, :]), ["ag"], ["at"])
+        to_wrapped(T.at, T.ua, "da", ["y", "s"], "at", "ua")
         scan(T.us[:, :], T.seg[:, 0:32], T.uk[:, :], 0.0, A.mult, A.add, ["seg", "uk"], ["us"])
+        op("v", vec.transpose, (T.kw[:, :], T.uk[:, :]), ["uk"], ["kw"])
         for h in range(2):
             ts(T.uto[:, 16 * h:16 * h + 16], T.ones[:, 0:16], T.us[:, 16 * h + 15:16 * h + 16], A.mult, None, None, ["ones", "us"], ["uto%d" % h])
         op("v", vec.transpose, (T.ust[:, :], T.us[:, :]), ["us"], ["ust"])
         op("v", vec.transpose, (T.utt[:, :], T.uto[:, :]), ["uto0", "uto1"], ["utt"])
-        op("v", vec.transpose, (T.kw[:, :], T.uk[:, :]), ["uk"], ["kw"])
         pq, q = T.pq, ["pq"]
         scan(pq[:, 0:20], T.ones[:, 0:20], T.utt[:, 0:20], 0.0, A.mult, A.add, ["ones", "utt"], q)
         tt(pq[:, 20:40], T.ust[:, 0:20], T.utt[:, 0:20], A.subtract, ["ust", "utt"], ["pq1"])
@@ -391,37 +439,27 @@ def rank_program(g, core, T, topo):
         tt(pq[:, 60:80], pq[:, 60:80], pq[:, 80:100], A.add, ["pq3", "pq4"], ["pq3"])
         cp(T.poff[:, :], pq[:, 60:80], ["pq3"], ["poff"])
         op("v", vec.tensor_copy, (T.lw[:, 0:C].indirect(T.poff[:, 0:20]), T.jrow[:, :]), ["poff", "jrow"], ["lw"])
-        ts(pq[:, 100:120], pq[:, 60:80], 128.0, A.is_lt, None, None, ["pq3"], ["pq5"])
-        ts(pq[:, 60:80], pq[:, 60:80], 320.0, A.add, None, None, ["pq3"], ["pq3"])
-        tt(pq[:, 60:80], pq[:, 60:80], T.j16[:, :], A.subtract, ["pq3", "j16"], ["pq3"])
-        tt(pq[:, 60:80], pq[:, 60:80], pq[:, 100:120], A.mult, ["pq3", "pq5"], ["pq3"])
-        tt(pq[:, 60:80], pq[:, 60:80], T.j16[:, :], A.add, ["pq3", "j16"], ["pq3"])
-        cp(T.selo[:, :], pq[:, 60:80], ["pq3"], ["selo"])
         tt(T.lm[:, :], T.lw[:, 0:128], T.wmask[:, 0:128], A.mult, ["lw", "wmask"], ["lm"])
         scan(T.ls[:, :], T.seg[:, 0:128], T.lm[:, :], 0.0, A.mult, A.add, ["seg", "lm"], ["ls"])
         cp(T.loff[:, :], T.ls[:, 15:128:16], ["ls"], ["loff"])
-        for i in range(5, 7):
-            firsts(i)
-        ac = T.ac
-        ts(ac[:, 0:24], T.mn[:, :], 0.5, A.mult, 128.0, A.add, ["mn"], ["ac0"])
-        ts(ac[:, 24:48], T.mn[:, :], 500.0, A.is_lt, None, None, ["mn"], ["ac1"])
-        tt(ac[:, 0:24], ac[:, 0:24], T.mn[:, :], A.min, ["ac0", "mn"], ["ac0"])
-        tt(ac[:, 24:48], ac[:, 24:48], T.keep[:, :], A.is_gt, ["ac1"] + keeps, ["ac1"])
-        tt(ac[:, 0:24], ac[:, 0:24], ac[:, 24:48], A.mult, ["ac0", "ac1"], ["ac0"])
-        tt(ac[:, 0:24], ac[:, 0:24], T.j24[:, :], A.add, ["ac0", "j24"], ["ac0"])
-        ts(ac[:, 24:48], ac[:, 0:24], 320.0, A.is_ge, -320.0, A.mult, ["ac0"], ["ac1"])
-        by_group(lambda o, i: tt(T.ag[:, o], ac[:, i], ac[:, 24 + i.start:24 + i.stop], A.add, ["ac0", "ac1"], ["ag"]))
-        op("v", vec.transpose, (T.at[:, :], T.ag[:, :]), ["ag"], ["at"])
-        to_wrapped(T.at, T.ua, "da", ["y", "s"], "at", "ua")
         if t == R - 1:
-            dmas("do", [("y", T.al[:, 96 * a:96 * a + 96], T.at[32 * a:32 * a + 24, 0:32]) for a in range(3)]
-                 + [("y", T.al[:, 288:320], T.at[96:120:3, 0:32]), ("y", T.al[:, 320:448], T.lw[0:128:16, 0:128])], ["at", "lw"], ["al"])
+            dmas("do", [("y", T.al[:, 128 * c + 32 * a:128 * c + 32 * a + 32], T.at[32 * a + c:32 * a + 24:3, 0:32])
+                        for c in range(3) for a in range(4 if c < 2 else 2)] + [("y", T.al[:, 320:448], T.lw[0:128:16, 0:128])], ["at", "lw"], ["al"])
         op("v", vec.transpose, (T.aw[:, :], T.ua[:, :]), ["ua"], ["aw"])
         cp(T.aoff[:, :], T.aw[:, 0:20], ["aw"], ["aoff"])
+        for b in (2, 3):
+            act(T.zg[:, 320 * b - 640:320 * b - 320], T.fb[:, 320 * b:320 * b + 320].indirect(T.aoff[:, 0:20]), AF.Copy, ["fb%d" % b, "aoff"], ["zg%d" % b])
         for b in range(4):
-            f = slice(320 * b, 320 * b + 320)
-            tt(T.zt[:, 448 * b:448 * b + 320], T.fb[:, f].indirect(T.aoff[:, 0:20]), T.fc[:, f], A.add, ["fb%d" % b, "fc%d" % b, "aoff"], ["zt%d" % b])
-            act(T.et[:, b:512:4], T.zt[:, 448 * b:448 * b + 320].indirect(T.loff[:, 0:8]), AF.Copy, ["zt%d" % b, "loff"], ["et%d" % b])
+            f, z = slice(320 * b, 320 * b + 320), T.zt[:, 448 * b:448 * b + 320]
+            if b < 2:
+                tt(z, T.fb[:, f].indirect(T.aoff[:, 0:20]), T.fc[:, f], A.add, ["fb%d" % b, "fc%d" % b, "aoff"], ["zt%d" % b])
+            else:
+                tt(z, T.zg[:, 320 * b - 640:320 * b - 320], T.ps[:, 512 * (4 + b):512 * (4 + b) + C], A.add, ["zg%d" % b, "ps%d" % (4 + b)], ["zt%d" % b])
+            e = (T.et[:, b:512:4], z.indirect(T.loff[:, 0:8]))
+            if b < 3:
+                act(e[0], e[1], AF.Copy, ["zt%d" % b, "loff"], ["et%d" % b])
+            else:
+                cp(e[0], e[1], ["zt%d" % b, "loff"], ["et%d" % b])
         quant(T.qe[:, :], T.qes[:, :], T.et[:, :], ["et%d" % b for b in range(4)], ["qe"])
         waits("g", ["qe"], [])
         g.remote_dma(T.qa[:, 0:128].bitcast(dt.uint8), T.qe[:, 0:128].bitcast(dt.uint8), T.sem["re"], T.sem["rl"], pid, rid, mask)
@@ -430,10 +468,18 @@ def rank_program(g, core, T, topo):
         cnt["re"] += 2 * neng
         note(("dma", "rl", None), ["qe"], [])
         note(("dma", "re", cnt["re"]), [], ["qa"])
+        ts(pq[:, 100:120], pq[:, 60:80], 128.0, A.is_lt, None, None, ["pq3"], ["pq5"])
+        ts(pq[:, 60:80], pq[:, 60:80], 320.0, A.add, None, None, ["pq3"], ["pq3"])
+        tt(pq[:, 60:80], pq[:, 60:80], T.j16[:, :], A.subtract, ["pq3", "j16"], ["pq3"])
+        tt(pq[:, 60:80], pq[:, 60:80], pq[:, 100:120], A.mult, ["pq3", "pq5"], ["pq3"])
+        tt(pq[:, 60:80], pq[:, 60:80], T.j16[:, :], A.add, ["pq3", "j16"], ["pq3"])
+        cp(T.selo[:, :], pq[:, 60:80], ["pq3"], ["selo"])
+        if t == 0:
+            later_constants()
         for b in range(4):
             w = slice(128 * b, 128 * b + 128)
             mm(4 + b, 128, T.wq[:, w], T.wqs[:, w], T.qa[:, :], T.qas[:, :], ["w", "qa"], True, False)
-            mm(4 + b, 128, T.ek[:, w], T.eks[:, w], T.qa[:, :], T.qas[:, :], ["ek", "qa"], False, True)
+            mm(4 + b, 128, T.ek[:, w], T.eks[:, w], T.qa[:, :], T.qas[:, :], ["ek%d" % b, "qa"], False, True)
             o, i = T.zt[:, 448 * b + 320:448 * b + 448], T.ps[:, 512 * (4 + b):512 * (4 + b) + 128]
             n, win = T.xs[:, b:1280:4], T.zt[:, 448 * b:448 * b + 448].indirect(T.selo[:, 0:20])
             if b % 2 == 0:
@@ -447,6 +493,6 @@ def rank_program(g, core, T, topo):
     mm(0, C, T.vq[:, :], T.vqs[:, :], T.qx[:, :], T.qxs[:, :], ["vq", "qx"])
     act(T.yo[:, :], T.ps[:, 0:C], AF.Copy, ["ps0"], ["yo"])
     dmas("do", [("y", T.y[:, :], T.yo[:, :])], ["yo"], ["y"])
-    for s in ("do", "cv", "cs", "ct", "cg", "dx", "du", "dv", "dw", "dk", "da", "rw", "re", "rl"):
+    for s in SEMAPHORES:
         if seen["y"].get(s, 0) < cnt[s]:
             need("y", ("end", s, cnt[s]))

@@ -2,6 +2,8 @@ from concourse.bass import DstId, RemoteDMATransfer
 from concourse.mybir import dt, AluOpType, AxisListType, ActivationFunctionType
 
 C, K, R = 320, 128, 3
+EARLY = 4
+SOME5, SOME6 = 0, 4
 F8, F32, BF, I32, U16, U8 = "float8_e4m3fn_x4", "float32", "bfloat16", "int32", "uint16", "uint8"
 
 
@@ -31,12 +33,14 @@ SCRATCH = {
     "obb": _sb(24, F32), "ct": _sb(768, BF), "pt": _sb(768, BF), "n0": _sb(960, F32), "nn": _sb(960, F32),
     "sm": _sb(60, I32), "vi": _sb(60, I32), "dd": _sb(480, I32), "vv": _sb(60, F32), "vz": _sb(60, F32), "sc": _sb(60, F32),
     "kl": _sb(60, F32), "keep": _sb(24, F32), "pks": _sb(24, F32), "pb": _sb(24, F32), "base": _sb(8, F32),
-    "zz": _sb(6 * 960, BF), "zv": _sb(960, F32), "so": _sb(480, BF), "s0": _sb(480, F32), "mn": _sb(24, F32), "ac": _sb(48, F32),
+    "zz": _sb(6 * 960, F32), "zv": _sb(960, F32), "so": _sb(24 * 160, F32), "s0": _sb(480, F32), "jk": _sb(24, F32), "ac": _sb(48, F32),
+    "cu": _sb(768, BF), "pv": _sb(768, BF), "nbb": _sb(24, F32), "pka": _sb(24, F32), "pkb": _sb(24, F32), "j24b": _sb(24, F32), "s20": _sb(60, F32),
+    "am": _sb(64, F32), "ve": _sb(60, F32),
     "kg": _sb(32, F32), "kt": _sb(32, F32), "ag": _sb(32, F32), "at": _sb(32, F32), "uk": _sb(32, F32), "ua": _sb(32, F32),
     "us": _sb(32, F32), "uto": _sb(32, F32), "ust": _sb(32, F32), "utt": _sb(32, F32), "kw": _sb(32, F32), "pq": _sb(160, F32),
     "poff": _sb(20, U16), "selo": _sb(20, U16), "lw": _sb(C, F32), "lm": _sb(128, F32), "ls": _sb(128, F32), "loff": _sb(8, U16),
     "aw": _sb(32, F32), "aoff": _sb(20, U16),
-    "fb": _sb(1280, BF), "fc": _sb(640, BF), "zg": _sb(640, F32), "zt": _sb(4 * 448, BF), "et": _sb(512, BF),
+    "fb": _sb(2560, BF), "fc": _sb(640, BF), "zg": _sb(640, F32), "zt": _sb(4 * 448, BF), "et": _sb(512, BF),
     "qe": _sb(128, F8), "qes": _sb(128, U8), "qa": _sb(128, F8), "qas": _sb(128, U8), "yo": _sb(C, F32),
 }
 SEMAPHORES = ["cv", "cs", "ct", "cg", "dx", "du", "dv", "dw", "dk", "da", "do", "dp", "rw", "re", "rl"]
@@ -84,7 +88,23 @@ def rank_program(g, core, T, topo):
             wr[k] = [tok]
             rd[k] = []
 
+    rec = [None]
+
+    def record(*fns):
+        rec[0] = []
+        for fn in fns:
+            fn()
+        r, rec[0] = rec[0], None
+        return r
+
+    def merge(*lists):
+        for _, _, c in sorted(((i + 0.5) / len(l), n, c) for n, l in enumerate(lists) for i, c in enumerate([(n, i) for i in range(len(l))])):
+            op(*lists[c[0]][c[1]])
+
     def op(q, call, args, reads, writes, kw=None, waw=True):
+        if rec[0] is not None:
+            rec[0].append((q, call, args, reads, writes, kw, waw))
+            return
         waits(q, reads, writes, waw)
         s = own[q]
         call(*args, **(kw or {})).then_inc(T.sem[s], 1)
@@ -141,19 +161,21 @@ def rank_program(g, core, T, topo):
     iota(T.i4[:, :], [[16, 4]], 0, 0, ["i4"])
     iota(T.iw[:, :], [[1, C]], 128, -1, ["iw"])
     fill(T.ones[:, :], 1.0, ["ones"])
-    fill(T.tmp8[:, 8:16], 0.0, ["t8b"])
-    for base, buf in ((4.0, T.pw4), (2.0, T.pw2)):
-        fill(T.tmp8[:, 0:8], base, ["t8"])
-        scan(buf[:, 0:8], T.tmp8[:, 0:8], T.tmp8[:, 8:16], 1.0 / base, A.mult, A.add, ["t8", "t8b"], ["pw"])
-        cp(buf[:, 8:16], buf[:, 0:8], ["pw"], ["pw"])
-    fill(T.cwt[:, :], 0.0, ["cwt"])
-    fill(T.bt[:, :], 0.0, ["bt"])
     fill(T.dg[:, :], 0.5, ["dg"])
+
+    def powers():
+        fill(T.tmp8[:, 8:16], 0.0, ["t8b"])
+        for base, buf in ((4.0, T.pw4), (2.0, T.pw2)):
+            fill(T.tmp8[:, 0:8], base, ["t8"])
+            scan(buf[:, 0:8], T.tmp8[:, 0:8], T.tmp8[:, 8:16], 1.0 / base, A.mult, A.add, ["t8", "t8b"], ["pw"])
+            cp(buf[:, 8:16], buf[:, 0:8], ["pw"], ["pw"])
+        fill(T.cwt[:, :], 0.0, ["cwt"])
+        fill(T.bt[:, :], 0.0, ["bt"])
+        ts(T.oneh[:, :], T.io8[:, :], 0.0, A.is_equal, None, None, ["io8"], ["oneh"])
     op("g", g.affine_select, (T.dh[:, :], T.dg[:, :], [[-1, 516]], A.is_equal, 0.0, 3, 4), ["dg"], ["dh"])
     iota(T.phi0[0:32, :], [[1, C]], 0, -1, ["phi0"], allow_small_or_imprecise_dtypes=True)
     iota(T.ir[:, :], [[1, C]], 0, 0, ["ir"])
     iota(T.jrow[:, :], [[1, C]], 0, 0, ["jrow"], allow_small_or_imprecise_dtypes=True)
-    ts(T.oneh[:, :], T.io8[:, :], 0.0, A.is_equal, None, None, ["io8"], ["oneh"])
 
     def weights(t):
         s = (-3 * t) % 8
@@ -163,9 +185,9 @@ def rank_program(g, core, T, topo):
             ts(T.cwt[:, 0:512:4], T.ones[:, 0:128], T.kf[:, 90:91], A.mult, None, None, ["ones", "wcol"], ["cwt"])
             o = 128 * (2 * t + h)
             quant(T.cw[:, o:o + 128], T.cws[:, o:o + 128], T.cwt[:, :], ["cwt"], ["cw%d" % (2 * t + h)])
-    weights(0)
 
     kf, k, ki = T.kf, ["kf"], ["ki"]
+    rec[0] = []
     fill(kf[:, 0:12], 0.0, k)
     op("v", vec.tensor_scalar, (T.ki[:, 0:1], T.ip[:, 0:1], 15, None, A.bitwise_and), ["ip"], ki)
     op("v", vec.tensor_scalar, (T.ki[:, 1:2], T.ip[:, 0:1], 63, None, A.bitwise_and), ["ip"], ki, waw=False)
@@ -202,20 +224,19 @@ def rank_program(g, core, T, topo):
     for t in range(3):
         ts(T.mg[:, 20 * t:20 + 20 * t], T.ones[:, 0:20], kf[:, 28 + t:29 + t], A.mult, None, None, ["ones", "ma"], ["mg"], t == 0)
         ts(T.mg[:, 64 + 20 * t:84 + 20 * t], T.ones[:, 0:20], kf[:, 31 + t:32 + t], A.mult, None, None, ["ones", "mb"], ["mg"], False)
-    quant(T.uq[:, :], T.uqs[:, :], T.ut[:, :], ["ut"], ["uq"])
-    quant(T.qx[:, :], T.qxs[:, :], T.x0[:, :], ["x"], ["qx"])
+    op("v", vec.tensor_scalar, (T.iw[:, :], T.iw[:, :], 15, None, A.bitwise_and), ["iw"], ["iw"])
+    ts(T.wmask[:, :], T.iw[:, :], 0.0, A.is_equal, None, None, ["iw"], ["wmask"])
+    cp(T.mg[:, 128:176], T.wmask[:, 0:48], ["wmask"], ["mg2"])
+    places, rec[0] = rec[0], None
 
-    def mask_constants():
-        op("v", vec.tensor_scalar, (T.iw[:, :], T.iw[:, :], 15, None, A.bitwise_and), ["iw"], ["iw"])
-        ts(T.wmask[:, :], T.iw[:, :], 0.0, A.is_equal, None, None, ["iw"], ["wmask"])
-        cp(T.mg[:, 128:176], T.wmask[:, 0:48], ["wmask"], ["mg2"])
+    def first_codes():
+        quant(T.uq[:, :], T.uqs[:, :], T.ut[:, :], ["ut"], ["uq"])
+        quant(T.qx[:, :], T.qxs[:, :], T.x0[:, :], ["x"], ["qx"])
 
     def more_constants():
         p = ["phi0"]
         ts(T.phit[0:32, 0:32], T.phi0[0:32, 0:32], 0.0, A.is_lt, 320.0, A.mult, p, ["phit"])
         tt(T.phi0[0:32, 0:32], T.phi0[0:32, 0:32], T.phit[0:32, 0:32], A.add, p + ["phit"], p)
-        ts(T.phit[0:32, :], T.phi0[0:32, :], 2.0, A.mult, -256.0, A.add, p, ["phit"])
-        tt(T.phi0[0:32, :], T.phi0[0:32, :], T.phit[0:32, :], A.max, p + ["phit"], p)
         items = []
         for t in range(3):
             for a in range(4):
@@ -242,6 +263,10 @@ def rank_program(g, core, T, topo):
             fill(T[n][:, :], 0.0, [n])
         for i in range(8):
             op("v", vec.tensor_copy, (T.j24[:, 3 * i:3 * i + 3], kf[:, 0:3]), k, ["j24"], None, False)
+        ts(T.j24b[:, :], T.j24[:, :], 320.0, A.add, None, None, ["j24"], ["j24b"])
+        fill(T.s20[:, :], 1.0, ["s20"])
+        for t in range(3):
+            fill(T.s20[:, 20 * t:20 * t + 1], 0.0, ["s20"])
         ts(T.j16[:, :], T.ir[:, 0:20], 16.0, A.mult, kf[:, 13:14], A.add, ["ir", "p16"], ["j16"])
 
     def later_constants():
@@ -271,17 +296,20 @@ def rank_program(g, core, T, topo):
             fn(slice(3 * rot, 24), slice(0, 3 * n))
             if rot:
                 fn(slice(0, 3 * rot), slice(3 * n, 24))
-        mm(0, C, T.uq[:, :], T.uqs[:, :], T.qx[:, :], T.qxs[:, :], ["uq", "qx"])
-        ts(T.bt[:, 0:1280:4], T.ps[:, 0:C], 0.0, A.is_gt, None, None, ["ps0"], ["bt"])
-        quant(T.bq[:, :], T.bqs[:, :], T.bt[:, :], ["bt"], ["bq"])
-        for h in range(2):
-            o = 128 * (2 * t + h)
-            mm(1 + h, C, T.cw[:, o:o + 128], T.cws[:, o:o + 128], T.bq[:, :], T.bqs[:, :], ["cw%d" % (2 * t + h), "bq"])
-        act(T.w4[:, :], T.ps[:, 512:512 + C], AF.Copy, ["ps1"], ["w4"])
+        def words():
+            mm(0, C, T.uq[:, :], T.uqs[:, :], T.qx[:, :], T.qxs[:, :], ["uq", "qx"])
+            ts(T.bt[:, 0:1280:4], T.ps[:, 0:C], 0.0, A.is_gt, None, None, ["ps0"], ["bt"])
+            quant(T.bq[:, :], T.bqs[:, :], T.bt[:, :], ["bt"], ["bq"])
+            for h in range(2):
+                o = 128 * (2 * t + h)
+                mm(1 + h, C, T.cw[:, o:o + 128], T.cws[:, o:o + 128], T.bq[:, :], T.bqs[:, :], ["cw%d" % (2 * t + h), "bq"])
+            act(T.w4[:, :], T.ps[:, 512:512 + C], AF.Copy, ["ps1"], ["w4"])
         if t == 0:
-            mask_constants()
-        cp(T.gw[:, 0:128], T.w4[:, 0:C].indirect(T.sl[:, 0:8]), ["w4", "sl"], ["gw"])
-        tt(T.gm[:, 0:128], T.gw[:, 0:128], T.mg[:, 0:128], A.mult, ["gw", "mg"], ["gm"])
+            merge(record(powers, lambda: weights(0), first_codes, words), places)
+        else:
+            words()
+        tt(T.gm[:, 0:128], T.w4[:, 0:C].indirect(T.sl[:, 0:8]), T.mg[:, 0:128], A.mult, ["w4", "sl", "mg"], ["gm"])
+        tt(T.gm[:, 128:176], T.w4[:, 0:C].indirect(T.sl[:, 8:11]), T.mg[:, 128:176], A.mult, ["w4", "sl2", "mg2"], ["gm2"])
         tt(T.ms[:, :], T.gm[:, 0:60], T.gm[:, 64:124], A.add, ["gm"], ["ms"])
         cp(T.msg[:, :], T.ms[:, :], ["ms"], ["msg"])
         waits("g", ["msg"], [])
@@ -289,8 +317,6 @@ def rank_program(g, core, T, topo):
         cnt["rl"] += neng
         cnt["rw"] += neng
         note(("dma", "rl", None), ["msg"], [])
-        cp(T.gw[:, 128:176], T.w4[:, 0:C].indirect(T.sl[:, 8:11]), ["w4", "sl2"], ["gw2"])
-        tt(T.gm[:, 128:176], T.gw[:, 128:176], T.mg[:, 128:176], A.mult, ["gw2", "mg2"], ["gm2"])
         for c in range(3):
             op("v", vec.tensor_reduce, (T.wj[:, c:c + 1], T.gm[:, 128 + 16 * c:144 + 16 * c], X, A.add), ["gm2"], ["wj"], waw=False)
         cp(T.wji[:, :], T.wj[:, :], ["wj"], ["wji"])
@@ -298,52 +324,54 @@ def rank_program(g, core, T, topo):
             more_constants()
         for i in range(8):
             op("v", vec.tensor_scalar, (T.ob[:, 3 * i:3 * i + 3], T.wji[:, :], 2 * i, 1, A.logical_shift_right, A.bitwise_and), ["wji"], ["ob"], waw=False)
+        ts(T.nb[:, :], T.ob[:, :], -1.0, A.mult, 1.0, A.add, ["ob"], ["nb"])
         tt(T.u0[:, :], T.ob[:, :], T.codv[:, :], A.mult, ["ob", "codv"], ["u0"])
         cp(T.obf[:, :], T.ob[:, :], ["ob"], ["obf"])
-        ts(T.nb[:, :], T.ob[:, :], -1.0, A.mult, 1.0, A.add, ["ob"], ["nb"])
-        tt(T.u1[:, :], T.codv[:, :], T.u0[:, :], A.subtract, ["u0", "codv"], ["u1"])
+        tt(T.u1[:, :], T.nb[:, :], T.codv[:, :], A.mult, ["nb", "codv"], ["u1"])
         cols = ["u0", "u1", "nb", "obf"]
 
         def table(i, c):
             n = 1 << i
             lo, hi = slice(256 * c, 256 * c + n), slice(256 * c + n, 256 * c + 2 * n)
             q = slice(3 * i + c, 3 * i + c + 1)
-            a, b = "ct%d" % c, "ct%dh" % c
+            a, b = ("ct", "cu")[i % 2], ("cu", "ct")[i % 2]
+            o, r, w = T[b], [a + str(c)] + cols, [b + str(c)]
             if c == 0:
-                ts(T.ct[:, hi], T.ct[:, lo], T.obf[:, q], A.mult, T.u1[:, q], A.add, [a, b] + cols, [b])
-                ts(T.ct[:, lo], T.ct[:, lo], T.nb[:, q], A.mult, T.u0[:, q], A.add, [a, b] + cols, [a])
+                ts(o[:, hi], T[a][:, lo], T.obf[:, q], A.mult, T.u1[:, q], A.add, r, w)
+                ts(o[:, lo], T[a][:, lo], T.nb[:, q], A.mult, T.u0[:, q], A.add, r, w, False)
             else:
-                act(T.ct[:, hi], T.ct[:, lo], AF.Identity, [a, b] + cols, [b], scale=T.obf[:, q], bias=T.u1[:, q])
-                act(T.ct[:, lo], T.ct[:, lo], AF.Identity, [a, b] + cols, [a], scale=T.nb[:, q], bias=T.u0[:, q])
+                op("s", sca.activation, (o[:, hi], T[a][:, lo], AF.Identity), r, w, {"scale": T.obf[:, q], "bias": T.u1[:, q]})
+                op("s", sca.activation, (o[:, lo], T[a][:, lo], AF.Identity), r, w, {"scale": T.nb[:, q], "bias": T.u0[:, q]}, False)
         for i in range(8):
             for c in (1, 2):
                 table(i, c)
         for b in range(4):
             p = ["ps%d" % (4 + b)]
             mm(4 + b, C, T.eh[:, 128 * b:128 * b + 128], T.ehs[:, 128 * b:128 * b + 128], T.qx[:, :], T.qxs[:, :], ["eh%d" % b, "qx"])
-            act(T.fb[:, 320 * b:320 * b + 320], T.ps[:, 512 * (4 + b):512 * (4 + b) + C], AF.Copy, p, ["fb%d" % b])
+            for h in range(2):
+                act(T.fb[:, 640 * b + 320 * h:640 * b + 320 * h + 320], T.ps[:, 512 * (4 + b):512 * (4 + b) + C], AF.Copy, p, ["fb%d%d" % (b, h)])
             if b < 2:
                 act(T.fc[:, 320 * b:320 * b + 320], T.ps[:, 512 * (4 + b):512 * (4 + b) + C], AF.Copy, p, ["fc%d" % b])
         if t == 0:
             more_constants2()
-        ts(T.sg[:, :], T.ob[:, :], -32768.0, A.mult, 16384.0, A.add, ["ob"], ["sg"])
+        ts(T.nbb[:, :], T.ob[:, :], -16384.0, A.mult, 16384.0, A.add, ["ob"], ["nbb"])
         ts(T.obb[:, :], T.ob[:, :], 16384.0, A.mult, None, None, ["ob"], ["obb"])
         tt(T.wm[:, :], T.ps[:, 1024:1024 + C], T.wmask[:, :], A.mult, ["ps2", "wmask"], ["wm"])
         table(0, 0)
         scan(T.wsc[:, :], T.seg[:, :], T.wm[:, :], 0.0, A.mult, A.add, ["seg", "wm"], ["wsc"])
         table(1, 0)
         cp(T.wl[:, :], T.wsc[:, 15:C:16], ["wsc"], ["wl"])
-        for i in range(2, 8):
+        for i in range(2, EARLY):
             table(i, 0)
 
         def pairs(c):
             s = slice(320 * c, 320 * c + 320)
             tt(T.n0[:, s], T.ct[:, 256 * c:256 * c + 256].indirect(T.wl[:, 0:20]), T.phi[:, s], A.add,
-               ["ct%d" % c, "ct%dh" % c, "wl", "phi"], ["n0%d" % c])
+               ["ct%d" % c, "wl", "phi"], ["n0%d" % c])
             if t < R - 1:
                 fill(T.ct[:, 256 * c:256 * c + 1], 16384.0, ["ct%d" % c])
-        pairs(0)
-        pairs(1)
+        fillers = record(*[lambda i=i: table(i, 0) for i in range(EARLY, 8)], lambda: pairs(1), lambda: pairs(2), lambda: pairs(0))
+        rec[0] = []
         note(("dma", "rw", cnt["rw"]), [], ["pw"])
         for c in range(3):
             ts(T.sm[:, 20 * c:20 * c + 20], T.pw[:, 20 * c:20 * c + 20], T.wj[:, c:c + 1], A.add, None, None, ["pw", "wj"], ["sm%d" % c])
@@ -354,105 +382,116 @@ def rank_program(g, core, T, topo):
         def digit(i):
             op("v", vec.tensor_scalar, (T.dd[:, 60 * i:60 * i + 60], T.vi[:, :], 4 ** i, None, A.bitwise_and), ["vi"], ["dd%d" % i])
         digit(0)
+        ts(T.ve[:, :], T.vi[:, :], 1.0, A.is_equal, None, None, ["vi"], ["ve"])
         tt(T.vv[:, :], T.vv[:, :], T.vz[:, :], A.max, ["vv", "vz"], ["vv"])
+        scan(T.sc[:, :], T.s20[:, :], T.ve[:, :], 0.0, A.mult, A.max, ["s20", "ve"], ["sc"])
         for i in range(8):
-            scan(T.sc[:, :], T.res[:, :], T.vv[:, :], 2.0, A.max, A.min, ["res", "vv"], ["sc"])
+            if i:
+                scan(T.sc[:, :], T.res[:, :], T.vv[:, :], 2.0, A.max, A.min, ["res", "vv"], ["sc"])
             if i < 7:
                 for c in range(3):
                     m = T.sc[:, 20 * c + 19:20 * c + 20]
-                    ts(T.kl[:, 20 * c:20 * c + 20], T.dd[:, 60 * i + 20 * c:60 * i + 20 * c + 20], 2.0 ** -14, A.mult, m, A.is_gt,
-                       ["dd%d" % i, "sc"], ["kl%d" % c])
+                    d = T.dd[:, 60 * i + 20 * c:60 * i + 20 * c + 20]
+                    if i:
+                        ts(T.kl[:, 20 * c:20 * c + 20], d, 2.0 ** -14, A.mult, m, A.is_gt, ["dd%d" % i, "sc"], ["kl%d" % c])
+                    else:
+                        ts(T.kl[:, 20 * c:20 * c + 20], d, m, A.mult, None, None, ["dd%d" % i, "sc"], ["kl%d" % c])
             c3 = slice(3 * i, 3 * i + 3)
-            ts(T.keep[:, c3], T.sc[:, 19:60:20], 2.0 ** -14 * 4 ** i, A.is_lt, None, None, ["sc"], ["keep%d" % i])
+            if i:
+                ts(T.keep[:, c3], T.sc[:, 19:60:20], 2.0 ** -14 * 4 ** i, A.is_lt, None, None, ["sc"], ["keep%d" % i])
+            else:
+                cp(T.keep[:, c3], T.sc[:, 19:60:20], ["sc"], ["keep%d" % i])
             if i < 7:
                 if i < 6:
                     digit(i + 1)
                 tt(T.vv[:, :], T.vv[:, :], T.kl[:, :], A.max, ["vv", "kl0", "kl1", "kl2"], ["vv"])
-            tt(T.pks[:, c3], T.keep[:, c3], T.sg[:, c3], A.mult, ["keep%d" % i, "sg"], ["pks%d" % i])
+            tt(T.pka[:, c3], T.keep[:, c3], T.obb[:, c3], A.mult, ["keep%d" % i, "obb"], ["pka%d" % i])
+            tt(T.pkb[:, c3], T.keep[:, c3], T.nbb[:, c3], A.mult, ["keep%d" % i, "nbb"], ["pkb%d" % i])
             n = 1 << i
-            if i < 7:
-                for c in range(3):
-                    act(T.pt[:, 256 * c + n:256 * c + 2 * n], T.pt[:, 256 * c:256 * c + n], AF.Identity, ["pt%d" % c, "pks%d" % i], ["pt%d" % c],
-                        bias=T.pks[:, 3 * i + c:3 * i + c + 1])
+            a, b = ("pt", "pv")[i % 2], ("pv", "pt")[i % 2]
+            for c in range(3):
+                o = 256 * c
+                col = slice(3 * i + c, 3 * i + c + 1)
+                op("s", sca.activation, (T[b][:, o:o + n], T[a][:, o:o + n], AF.Identity), [a + str(c), "pka%d" % i], [b + str(c)], {"bias": T.pka[:, col]})
+                op("s", sca.activation, (T[b][:, o + n:o + 2 * n], T[a][:, o:o + n], AF.Identity), [a + str(c), "pkb%d" % i], [b + str(c)], {"bias": T.pkb[:, col]}, False)
+        drops, rec[0] = rec[0], None
+        merge(drops, fillers)
         keeps = ["keep%d" % i for i in range(8)]
-        tt(T.pb[:, :], T.keep[:, :], T.obb[:, :], A.mult, keeps + ["obb"], ["pb"])
-        by_group(lambda o, i: cp(T.kg[:, o], T.keep[:, i], keeps, ["kg"]))
-        for c in range(3):
-            op("v", vec.tensor_reduce, (T.base[:, c:c + 1], T.pb[:, c:24:3], X, A.add), ["pb"], ["base"], waw=False)
+        by_group(lambda o, i: op("v", vec.tensor_copy, (T.kg[:, o], T.keep[:, i]), keeps, ["kg"], None, False))
         op("v", vec.transpose, (T.kt[:, :], T.kg[:, :]), ["kg"], ["kt"])
-        tt(T.base[:, 3:6], T.base[:, 0:3], T.pks[:, 21:24], A.add, ["base", "pks7"], ["base2"])
-        for c in range(3):
-            lo, hi = slice(256 * c, 256 * c + 128), slice(256 * c + 128, 256 * c + 256)
-            act(T.pt[:, hi], T.pt[:, lo], AF.Identity, ["pt%d" % c, "base2"], ["pt%dh" % c], bias=T.base[:, 3 + c:4 + c])
-            act(T.pt[:, lo], T.pt[:, lo], AF.Identity, ["pt%d" % c, "base"], ["pt%d" % c], bias=T.base[:, c:c + 1])
         to_wrapped(T.kt, T.uk, "dk", ["y"], "kt", "uk")
-        pairs(2)
         for c in range(3):
             s = slice(320 * c, 320 * c + 320)
             tt(T.nn[:, s], T.pt[:, 256 * c:256 * c + 256].indirect(T.wl[:, 0:20]), T.n0[:, s], A.add,
-               ["pt%d" % c, "pt%dh" % c, "wl", "n0%d" % c], ["nn%d" % c])
+               ["pt%d" % c, "wl", "n0%d" % c], ["nn%d" % c])
+            for i in (2, 3):
+                z = slice(960 * (i - 2) + 320 * c, 960 * (i - 2) + 320 * c + 320)
+                act(T.zz[:, z], T.nn[:, s], AF.Abs, ["nn%d" % c], ["zz%d%d" % (i, c)], bias=-1024.0 * (i + 1))
         nns = ["nn0", "nn1", "nn2"]
-        for i in range(2, 8):
-            act(T.zz[:, 960 * (i - 2):960 * (i - 1)], T.nn[:, :], AF.Abs, nns, ["zz%d" % i], bias=-1024.0 * (i + 1))
+        ts(T.ac[:, 0:24], T.keep[:, :], 1000.0, A.mult, None, None, keeps, ["ac0"])
+        for i in range(4, 8):
+            op("s", sca.activation, (T.zz[:, 960 * (i - 2):960 * (i - 1)], T.nn[:, :], AF.Abs), nns, ["zz%d%d" % (i, c) for c in range(3)], {"bias": -1024.0 * (i + 1)})
         for c in range(3):
             o = 320 * c
             scan(T.s0[:, 160 * c:160 * c + 160], T.nn[:, o:o + 160], T.nn[:, o + 160:o + 320], 65536.0, A.min, A.min, ["nn%d" % c], ["s0%d" % c])
         ts(T.zv[:, :], T.nn[:, :], -2048.0, A.add, None, None, nns, ["zv"])
-        ts(T.mn[:, 0:3], T.s0[:, 159:480:160], -1024.0, A.add, None, None, ["s00", "s01", "s02"], ["mn"])
+        tt(T.jk[:, :], T.ac[:, 0:24], T.j24[:, :], A.add, ["ac0", "j24"], ["jk"])
+        so = T.so
+        ts(so[:, 159:480:160], T.s0[:, 159:480:160], -1024.0, A.add, None, None, ["s00", "s01", "s02"], ["so"])
         for c in range(3):
-            op("v", vec.tensor_reduce, (T.mn[:, 3 + c:4 + c], T.zv[:, 320 * c:320 * c + 320], X, A.min), ["zv"], ["mn"],
+            op("v", vec.tensor_reduce, (so[:, 639 + 160 * c:640 + 160 * c], T.zv[:, 320 * c:320 * c + 320], X, A.min), ["zv"], ["so"],
                {"apply_absolute_value": True}, waw=False)
         if t < R - 1:
             for c in range(3):
                 fill(T.pt[:, 256 * c:256 * c + 1], 0.0, ["pt%d" % c])
+
+        pq = T.pq
+        order = [
+            lambda: scan(T.us[:, :], T.seg[:, 0:32], T.uk[:, :], 0.0, A.mult, A.add, ["seg", "uk"], ["us"]),
+            lambda: op("v", vec.transpose, (T.kw[:, :], T.uk[:, :]), ["uk"], ["kw"]),
+            lambda: ts(T.uto[:, 0:16], T.ones[:, 0:16], T.us[:, 15:16], A.mult, None, None, ["ones", "us"], ["uto0"]),
+            lambda: ts(T.uto[:, 16:32], T.ones[:, 0:16], T.us[:, 31:32], A.mult, None, None, ["ones", "us"], ["uto1"]),
+            lambda: op("v", vec.transpose, (T.ust[:, :], T.us[:, :]), ["us"], ["ust"]),
+            lambda: op("v", vec.transpose, (T.utt[:, :], T.uto[:, :]), ["uto0", "uto1"], ["utt"]),
+            lambda: ts(pq[:, 80:100], T.kw[:, 0:20], 1000.0, A.mult, -1000.0, A.add, ["kw"], ["pq4"]),
+            lambda: scan(pq[:, 0:20], T.ones[:, 0:20], T.utt[:, 0:20], 0.0, A.mult, A.add, ["ones", "utt"], ["pq"]),
+            lambda: tt(pq[:, 20:40], T.ust[:, 0:20], T.utt[:, 0:20], A.subtract, ["ust", "utt"], ["pq1"]),
+            lambda: ts(pq[:, 40:41], pq[:, 19:20], -1.0, A.mult, 319.0, A.add, ["pq"], ["pq2"]),
+            lambda: tt(pq[:, 20:40], pq[:, 20:40], pq[:, 0:20], A.add, ["pq", "pq1"], ["pq1"]),
+            lambda: ts(pq[:, 80:100], pq[:, 80:100], pq[:, 40:41], A.add, None, None, ["pq4", "pq2"], ["pq4"]),
+            lambda: tt(pq[:, 60:80], T.j16[:, :], pq[:, 20:40], A.subtract, ["j16", "pq1"], ["pq3"]),
+            lambda: tt(pq[:, 80:100], pq[:, 80:100], pq[:, 20:40], A.add, ["pq1", "pq4"], ["pq4"]),
+            lambda: tt(pq[:, 60:80], pq[:, 60:80], pq[:, 80:100], A.max, ["pq3", "pq4"], ["pq3"]),
+            lambda: cp(T.poff[:, :], pq[:, 60:80], ["pq3"], ["poff"]),
+            lambda: op("v", vec.tensor_copy, (T.lw[:, 0:C].indirect(T.poff[:, 0:20]), T.jrow[:, :]), ["poff", "jrow"], ["lw"]),
+            lambda: tt(T.lm[:, :], T.lw[:, 0:128], T.wmask[:, 0:128], A.mult, ["lw", "wmask"], ["lm"]),
+            lambda: scan(T.ls[:, :], T.seg[:, 0:128], T.lm[:, :], 0.0, A.mult, A.add, ["seg", "lm"], ["ls"]),
+            lambda: cp(T.loff[:, :], T.ls[:, 15:128:16], ["ls"], ["loff"]),
+        ]
+
+        def some(n):
+            for _ in range(n):
+                if order:
+                    order.pop(0)()
         for i in range(2, 8):
             for c in range(3):
                 o = 960 * (i - 2) + 320 * c
-                scan(T.so[:, 160 * c:160 * c + 160], T.zz[:, o:o + 160], T.zz[:, o + 160:o + 320], 65536.0, A.min, A.min, ["zz%d" % i], ["so%d" % c])
-            op("v", vec.tensor_copy, (T.mn[:, 3 * i:3 * i + 3], T.so[:, 159:480:160]), ["so0", "so1", "so2"], ["mn"], None, False)
-        ac = T.ac
-        ts(ac[:, 0:24], T.mn[:, :], 0.5, A.mult, 128.0, A.add, ["mn"], ["ac0"])
-        ts(ac[:, 24:48], T.mn[:, :], 500.0, A.is_lt, None, None, ["mn"], ["ac1"])
-        tt(ac[:, 0:24], ac[:, 0:24], T.mn[:, :], A.min, ["ac0", "mn"], ["ac0"])
-        tt(ac[:, 24:48], ac[:, 24:48], T.keep[:, :], A.is_gt, ["ac1"] + keeps, ["ac1"])
-        tt(ac[:, 0:24], ac[:, 0:24], ac[:, 24:48], A.mult, ["ac0", "ac1"], ["ac0"])
-        tt(ac[:, 0:24], ac[:, 0:24], T.j24[:, :], A.add, ["ac0", "j24"], ["ac0"])
-        ts(ac[:, 24:48], ac[:, 0:24], 320.0, A.is_ge, -320.0, A.mult, ["ac0"], ["ac1"])
-        by_group(lambda o, i: tt(T.ag[:, o], ac[:, i], ac[:, 24 + i.start:24 + i.stop], A.add, ["ac0", "ac1"], ["ag"]))
+                op("v", vec.tensor_tensor_scan, (so[:, 480 * i + 160 * c:480 * i + 160 * c + 160], T.zz[:, o:o + 160], T.zz[:, o + 160:o + 320], 65536.0, A.min, A.min),
+                   ["zz%d%d" % (i, c)], ["so"], None, False)
+            some((0, 0, 0, 0, 0, SOME5, SOME6, 0)[i])
+        tt(T.ac[:, 24:48], so[:, 159:3840:160], T.jk[:, :], A.add, ["so", "jk"], ["ac1"])
+        by_group(lambda o, i: op("v", vec.tensor_tensor, (T.ag[:, o], T.ac[:, 24 + i.start:24 + i.stop], T.j24b[:, i], A.min), ["ac1", "j24b"], ["ag"], None, False))
         op("v", vec.transpose, (T.at[:, :], T.ag[:, :]), ["ag"], ["at"])
         to_wrapped(T.at, T.ua, "da", ["y", "s"], "at", "ua")
-        scan(T.us[:, :], T.seg[:, 0:32], T.uk[:, :], 0.0, A.mult, A.add, ["seg", "uk"], ["us"])
-        op("v", vec.transpose, (T.kw[:, :], T.uk[:, :]), ["uk"], ["kw"])
-        for h in range(2):
-            ts(T.uto[:, 16 * h:16 * h + 16], T.ones[:, 0:16], T.us[:, 16 * h + 15:16 * h + 16], A.mult, None, None, ["ones", "us"], ["uto%d" % h])
-        op("v", vec.transpose, (T.ust[:, :], T.us[:, :]), ["us"], ["ust"])
-        op("v", vec.transpose, (T.utt[:, :], T.uto[:, :]), ["uto0", "uto1"], ["utt"])
-        pq, q = T.pq, ["pq"]
-        scan(pq[:, 0:20], T.ones[:, 0:20], T.utt[:, 0:20], 0.0, A.mult, A.add, ["ones", "utt"], q)
-        tt(pq[:, 20:40], T.ust[:, 0:20], T.utt[:, 0:20], A.subtract, ["ust", "utt"], ["pq1"])
-        tt(pq[:, 20:40], pq[:, 20:40], pq[:, 0:20], A.add, q + ["pq1"], ["pq1"])
-        ts(pq[:, 40:41], pq[:, 19:20], -1.0, A.mult, 319.0, A.add, q, ["pq2"])
-        tt(pq[:, 60:80], T.j16[:, :], pq[:, 20:40], A.subtract, ["j16", "pq1"], ["pq3"])
-        ts(pq[:, 80:100], pq[:, 20:40], pq[:, 40:41], A.add, None, None, ["pq1", "pq2"], ["pq4"])
-        tt(pq[:, 80:100], pq[:, 80:100], pq[:, 60:80], A.subtract, ["pq3", "pq4"], ["pq4"])
-        tt(pq[:, 80:100], pq[:, 80:100], T.kw[:, 0:20], A.mult, ["pq4", "kw"], ["pq4"])
-        tt(pq[:, 60:80], pq[:, 60:80], pq[:, 80:100], A.add, ["pq3", "pq4"], ["pq3"])
-        cp(T.poff[:, :], pq[:, 60:80], ["pq3"], ["poff"])
-        op("v", vec.tensor_copy, (T.lw[:, 0:C].indirect(T.poff[:, 0:20]), T.jrow[:, :]), ["poff", "jrow"], ["lw"])
-        tt(T.lm[:, :], T.lw[:, 0:128], T.wmask[:, 0:128], A.mult, ["lw", "wmask"], ["lm"])
-        scan(T.ls[:, :], T.seg[:, 0:128], T.lm[:, :], 0.0, A.mult, A.add, ["seg", "lm"], ["ls"])
-        cp(T.loff[:, :], T.ls[:, 15:128:16], ["ls"], ["loff"])
-        if t == R - 1:
-            dmas("do", [("y", T.al[:, 128 * c + 32 * a:128 * c + 32 * a + 32], T.at[32 * a + c:32 * a + 24:3, 0:32])
-                        for c in range(3) for a in range(4 if c < 2 else 2)] + [("y", T.al[:, 320:448], T.lw[0:128:16, 0:128])], ["at", "lw"], ["al"])
+        some(20)
         op("v", vec.transpose, (T.aw[:, :], T.ua[:, :]), ["ua"], ["aw"])
         cp(T.aoff[:, :], T.aw[:, 0:20], ["aw"], ["aoff"])
         for b in (2, 3):
-            act(T.zg[:, 320 * b - 640:320 * b - 320], T.fb[:, 320 * b:320 * b + 320].indirect(T.aoff[:, 0:20]), AF.Copy, ["fb%d" % b, "aoff"], ["zg%d" % b])
+            act(T.zg[:, 320 * b - 640:320 * b - 320], T.fb[:, 640 * b:640 * b + 640].indirect(T.aoff[:, 0:20]), AF.Copy, ["fb%d0" % b, "fb%d1" % b, "aoff"], ["zg%d" % b])
         for b in range(4):
             f, z = slice(320 * b, 320 * b + 320), T.zt[:, 448 * b:448 * b + 320]
             if b < 2:
-                tt(z, T.fb[:, f].indirect(T.aoff[:, 0:20]), T.fc[:, f], A.add, ["fb%d" % b, "fc%d" % b, "aoff"], ["zt%d" % b])
+                tt(z, T.fb[:, 640 * b:640 * b + 640].indirect(T.aoff[:, 0:20]), T.fc[:, f], A.add, ["fb%d0" % b, "fb%d1" % b, "fc%d" % b, "aoff"], ["zt%d" % b])
             else:
                 tt(z, T.zg[:, 320 * b - 640:320 * b - 320], T.ps[:, 512 * (4 + b):512 * (4 + b) + C], A.add, ["zg%d" % b, "ps%d" % (4 + b)], ["zt%d" % b])
             e = (T.et[:, b:512:4], z.indirect(T.loff[:, 0:8]))
@@ -476,6 +515,11 @@ def rank_program(g, core, T, topo):
         cp(T.selo[:, :], pq[:, 60:80], ["pq3"], ["selo"])
         if t == 0:
             later_constants()
+        if t == R - 1:
+            ts(T.am[:, 0:32], T.at[:, :], 320.0, A.is_ge, -320.0, A.mult, ["at"], ["am"])
+            tt(T.am[:, 32:64], T.at[:, :], T.am[:, 0:32], A.add, ["at", "am"], ["am2"])
+            dmas("do", [("y", T.al[:, 128 * c + 32 * a:128 * c + 32 * a + 32], T.am[32 * a + c:32 * a + 24:3, 32:64])
+                        for c in range(3) for a in range(4 if c < 2 else 2)] + [("y", T.al[:, 320:448], T.lw[0:128:16, 0:128])], ["am2", "lw"], ["al"])
         for b in range(4):
             w = slice(128 * b, 128 * b + 128)
             mm(4 + b, 128, T.wq[:, w], T.wqs[:, w], T.qa[:, :], T.qas[:, :], ["w", "qa"], True, False)

@@ -2,8 +2,8 @@ from concourse.bass import DstId, RemoteDMATransfer
 from concourse.mybir import dt, AluOpType, AxisListType, ActivationFunctionType
 
 C, K, R = 320, 128, 3
-EARLY = 4
-SOME5, SOME6 = 0, 4
+SOME = (0, 0, 0, 2, 2, 2, 3, 2, 2, 2)
+EPS, KEPT, SAME = 2.0 ** -12, 2.0 ** 99, 12288.0
 F8, F32, BF, I32, U16, U8 = "float8_e4m3fn_x4", "float32", "bfloat16", "int32", "uint16", "uint8"
 
 
@@ -24,20 +24,17 @@ SCRATCH = {
     "kf": _sb(96, F32), "ki": _sb(32, I32), "jrow": _sb(C, F32), "wmask": _sb(C, F32), "seg": _sb(C, F32),
     "ones": _sb(128, F32), "pw4": _sb(16, F32), "pw2": _sb(16, F32), "tmp8": _sb(16, F32), "oneh": _sb(8, F32),
     "sl": _sb(12, U16), "mg": _sb(176, F32), "phi0": _sb(C, F32), "phit": _sb(C, F32), "phi": _sb(960, F32), "j24": _sb(24, F32),
-    "j16": _sb(20, F32), "codv": _sb(24, F32), "res": _sb(60, F32),
+    "j24b": _sb(24, F32), "j16": _sb(32, F32), "codv": _sb(24, F32), "res": _sb(60, F32), "s20": _sb(60, F32),
     "bt": _sb(1280, BF), "bq": _sb(C, F8), "bqs": _sb(C, U8),
-    "w4": _sb(C, F32), "gw": _sb(176, F32), "gm": _sb(176, F32), "ms": _sb(60, F32), "msg": _sb(60, U16), "pw": _sb(60, U16),
+    "w4": _sb(C, F32), "gm": _sb(176, F32), "ms": _sb(60, F32), "msg": _sb(60, U16), "pw": _sb(60, U16),
     "wm": _sb(C, F32), "wsc": _sb(C, F32), "wl": _sb(20, U16),
-    "wj": _sb(3, F32), "wji": _sb(3, I32), "ob": _sb(24, I32), "obf": _sb(24, F32), "nb": _sb(24, F32),
-    "u0": _sb(24, F32), "u1": _sb(24, F32), "sg": _sb(24, F32),
-    "obb": _sb(24, F32), "ct": _sb(768, BF), "pt": _sb(768, BF), "n0": _sb(960, F32), "nn": _sb(960, F32),
-    "sm": _sb(60, I32), "vi": _sb(60, I32), "dd": _sb(480, I32), "vv": _sb(60, F32), "vz": _sb(60, F32), "sc": _sb(60, F32),
-    "kl": _sb(60, F32), "keep": _sb(24, F32), "pks": _sb(24, F32), "pb": _sb(24, F32), "base": _sb(8, F32),
-    "zz": _sb(6 * 960, F32), "zv": _sb(960, F32), "so": _sb(24 * 160, F32), "s0": _sb(480, F32), "jk": _sb(24, F32), "ac": _sb(48, F32),
-    "cu": _sb(768, BF), "pv": _sb(768, BF), "nbb": _sb(24, F32), "pka": _sb(24, F32), "pkb": _sb(24, F32), "j24b": _sb(24, F32), "s20": _sb(60, F32),
-    "am": _sb(64, F32), "ve": _sb(60, F32),
-    "kg": _sb(32, F32), "kt": _sb(32, F32), "ag": _sb(32, F32), "at": _sb(32, F32), "uk": _sb(32, F32), "ua": _sb(32, F32),
-    "us": _sb(32, F32), "uto": _sb(32, F32), "ust": _sb(32, F32), "utt": _sb(32, F32), "kw": _sb(32, F32), "pq": _sb(160, F32),
+    "wj": _sb(3, F32), "wji": _sb(3, I32), "ob": _sb(24, I32), "nb": _sb(24, F32),
+    "tp": _sb(96, F32), "tq": _sb(96, F32), "sb": _sb(96, F32), "pt": _sb(768, BF), "pv": _sb(768, BF), "nn": _sb(960, F32),
+    "sm": _sb(60, I32), "vi": _sb(60, I32), "dd": _sb(480, I32), "vv": _sb(60, F32), "vz": _sb(60, F32), "ve": _sb(60, F32),
+    "sc": _sb(60, F32), "kl": _sb(60, F32), "keep": _sb(32, F32),
+    "zz": _sb(6 * 960 + 320, F32), "zv": _sb(640, F32), "so": _sb(24 * 160, F32), "s0": _sb(480, F32), "jk": _sb(24, F32), "ac": _sb(48, F32),
+    "kt": _sb(32, F32), "ag": _sb(32, F32), "at": _sb(32, F32), "am": _sb(64, F32), "uk": _sb(32, F32), "ua": _sb(32, F32),
+    "us": _sb(32, F32), "uto": _sb(32, F32), "ust": _sb(32, F32), "utt": _sb(32, F32), "kw": _sb(32, F32), "pq": _sb(176, F32),
     "poff": _sb(20, U16), "selo": _sb(20, U16), "lw": _sb(C, F32), "lm": _sb(128, F32), "ls": _sb(128, F32), "loff": _sb(8, U16),
     "aw": _sb(32, F32), "aoff": _sb(20, U16),
     "fb": _sb(2560, BF), "fc": _sb(640, BF), "zg": _sb(640, F32), "zt": _sb(4 * 448, BF), "et": _sb(512, BF),
@@ -98,8 +95,8 @@ def rank_program(g, core, T, topo):
         return r
 
     def merge(*lists):
-        for _, _, c in sorted(((i + 0.5) / len(l), n, c) for n, l in enumerate(lists) for i, c in enumerate([(n, i) for i in range(len(l))])):
-            op(*lists[c[0]][c[1]])
+        for _, n, i in sorted(((i + 0.5) / len(l), n, i) for n, l in enumerate(lists) for i in range(len(l))):
+            op(*lists[n][i])
 
     def op(q, call, args, reads, writes, kw=None, waw=True):
         if rec[0] is not None:
@@ -127,26 +124,29 @@ def rank_program(g, core, T, topo):
         else:
             op("v", vec.tensor_scalar, (o, i, s1, s2, o1, o2), reads, writes, None, waw)
 
-    def tt(o, a, b, f, reads, writes):
-        op("v", vec.tensor_tensor, (o, a, b, f), reads, writes)
+    def tt(o, a, b, f, reads, writes, waw=True):
+        op("v", vec.tensor_tensor, (o, a, b, f), reads, writes, None, waw)
 
-    def cp(o, i, reads, writes):
-        op("v", vec.tensor_copy, (o, i), reads, writes)
+    def cp(o, i, reads, writes, waw=True):
+        op("v", vec.tensor_copy, (o, i), reads, writes, None, waw)
 
-    def act(o, i, f, reads, writes, **kw):
-        op("s", sca.activation, (o, i, f), reads, writes, kw)
+    def act(o, i, f, reads, writes, waw=True, **kw):
+        op("s", sca.activation, (o, i, f), reads, writes, kw, waw)
 
-    def fill(o, c, w):
-        op("v", vec.memset, (o, c), [], w)
+    def fill(o, c, w, waw=True):
+        op("v", vec.memset, (o, c), [], w, None, waw)
 
-    def scan(o, a, b, init, f, h, reads, writes):
-        op("v", vec.tensor_tensor_scan, (o, a, b, init, f, h), reads, writes)
+    def scan(o, a, b, init, f, h, reads, writes, waw=True):
+        op("v", vec.tensor_tensor_scan, (o, a, b, init, f, h), reads, writes, None, waw)
+
+    def turn(o, i, reads, writes):
+        op("v", vec.transpose, (o, i), reads, writes)
 
     def quant(q, s, t, reads, writes):
         op("v", vec.quantize_mx, (q, s, t), reads, writes)
 
     def mm(bank, n, l, ls, r, rs, reads, start=True, stop=True):
-        op("t", g.tensor.matmul_mx, (T.ps[:, 512 * bank:512 * bank + n], l, ls, r, rs, start, stop), reads, ["ps%d" % bank], waw=start)
+        op("t", g.tensor.matmul_mx, (T.ps[:, 512 * bank:512 * bank + n], l, ls, r, rs, start, stop), reads, ["ps%d" % bank], None, start)
 
     def iota(o, pat, base, cm, w, **kw):
         op("g", g.iota, (o, pat, base, cm), [], w, kw)
@@ -187,87 +187,89 @@ def rank_program(g, core, T, topo):
             quant(T.cw[:, o:o + 128], T.cws[:, o:o + 128], T.cwt[:, :], ["cwt"], ["cw%d" % (2 * t + h)])
 
     kf, k, ki = T.kf, ["kf"], ["ki"]
-    rec[0] = []
-    fill(kf[:, 0:12], 0.0, k)
-    op("v", vec.tensor_scalar, (T.ki[:, 0:1], T.ip[:, 0:1], 15, None, A.bitwise_and), ["ip"], ki)
-    op("v", vec.tensor_scalar, (T.ki[:, 1:2], T.ip[:, 0:1], 63, None, A.bitwise_and), ["ip"], ki, waw=False)
-    cp(kf[:, 13:14], T.ki[:, 0:1], ki, ["p16"])
-    cp(kf[:, 0:1], T.ip[:, 0:1], ["ip"], k)
-    ts(kf[:, 1:2], T.ip[:, 0:1], 128.0, A.add, None, None, ["ip"], k, False)
-    ts(kf[:, 2:3], T.ki[:, 1:2], 256.0, A.add, None, None, ki, k, False)
-    ts(kf[:, 8:12], T.i4[:, :], kf[:, 13:14], A.add, None, None, ["i4", "p16"], k, False)
-    ts(kf[:, 4:7], kf[:, 0:3], kf[:, 13:14], A.subtract, None, None, k + ["p16"], k)
 
     def floor20(o, i, n):
         ts(kf[:, 72:72 + n], i, 0.05, A.mult, -0.475, A.add, k, ["fl"])
         cp(T.ki[:, 16:16 + n], kf[:, 72:72 + n], ["fl"], ["fli"])
         cp(o, T.ki[:, 16:16 + n], ["fli"], k)
-    floor20(kf[:, 16:28], kf[:, 0:12], 12)
-    tt(kf[:, 28:31], kf[:, 16:19], kf[:, 20:23], A.is_equal, k, ["ma"])
-    ts(kf[:, 31:34], kf[:, 28:31], -1.0, A.mult, 1.0, A.add, ["ma"], ["mb"])
-    ts(kf[:, 24:28], kf[:, 24:28], 2.0, A.min, None, None, k, k)
-    ts(kf[:, 36:40], kf[:, 24:28], -20.0, A.mult, None, None, k, ["l1"])
-    tt(kf[:, 36:40], kf[:, 36:40], kf[:, 8:12], A.add, k + ["l1"], ["l1"])
-    ts(kf[:, 34:35], kf[:, 6:7], -256.0, A.add, kf[:, 4:5], A.subtract, k, ["l2"])
-    ts(kf[:, 44:48], kf[:, 24:28], 2.0, A.is_equal, kf[:, 34:35], A.mult, k + ["l2"], ["l3"])
-    ts(kf[:, 40:44], kf[:, 24:28], 128.0, A.mult, kf[:, 4:5], A.add, k, ["l4"])
-    tt(kf[:, 40:44], kf[:, 40:44], kf[:, 44:48], A.add, ["l3", "l4"], k)
-    floor20(kf[:, 48:52], kf[:, 40:44], 4)
-    ts(kf[:, 52:56], kf[:, 48:52], 1.0, A.add, 15.0, A.min, k, ["l5"])
-    for o, key in ((48, "kf"), (52, "l5")):
-        ts(kf[:, o:o + 4], kf[:, o:o + 4], 20.0, A.mult, None, None, [key], [key])
-    for o, key in ((48, "kf"), (52, "l5")):
-        tt(kf[:, o:o + 4], kf[:, o:o + 4], kf[:, 36:40], A.add, [key, "l1"], [key])
-    ts(T.sl[:, 0:8], kf[:, 48:56], 319.0, A.min, None, None, ["kf", "l5"], ["sl"])
-    cp(T.sl[:, 8:11], kf[:, 0:3], k, ["sl2"])
-    fill(T.mg[:, :], 0.0, ["mg"])
-    for t in range(3):
-        ts(T.mg[:, 20 * t:20 + 20 * t], T.ones[:, 0:20], kf[:, 28 + t:29 + t], A.mult, None, None, ["ones", "ma"], ["mg"], t == 0)
-        ts(T.mg[:, 64 + 20 * t:84 + 20 * t], T.ones[:, 0:20], kf[:, 31 + t:32 + t], A.mult, None, None, ["ones", "mb"], ["mg"], False)
-    op("v", vec.tensor_scalar, (T.iw[:, :], T.iw[:, :], 15, None, A.bitwise_and), ["iw"], ["iw"])
-    ts(T.wmask[:, :], T.iw[:, :], 0.0, A.is_equal, None, None, ["iw"], ["wmask"])
-    cp(T.mg[:, 128:176], T.wmask[:, 0:48], ["wmask"], ["mg2"])
-    places, rec[0] = rec[0], None
+
+    def make_places():
+        fill(kf[:, 0:12], 0.0, k)
+        op("v", vec.tensor_scalar, (T.ki[:, 0:1], T.ip[:, 0:1], 15, None, A.bitwise_and), ["ip"], ki)
+        op("v", vec.tensor_scalar, (T.ki[:, 1:2], T.ip[:, 0:1], 5, None, A.logical_shift_right), ["ip"], ["ki1"])
+        cp(kf[:, 12:13], T.ip[:, 0:1], ["ip"], ["ipf"])
+        cp(kf[:, 13:14], T.ki[:, 0:1], ki, ["p16"])
+        ts(kf[:, 0:1], T.ki[:, 1:2], 64.0, A.mult, kf[:, 12:13], A.add, ["ki1", "ipf"], k)
+        ts(kf[:, 34:35], T.ki[:, 1:2], 3.0, A.is_equal, -64.0, A.mult, ["ki1"], ["l2"])
+        ts(kf[:, 1:2], kf[:, 0:1], 32.0, A.add, kf[:, 34:35], A.add, k + ["l2"], k)
+        ts(kf[:, 2:3], kf[:, 0:1], 64.0, A.add, kf[:, 34:35], A.add, k + ["l2"], k, False)
+        ts(kf[:, 8:12], T.i4[:, :], kf[:, 13:14], A.add, None, None, ["i4", "p16"], k, False)
+        ts(kf[:, 4:7], kf[:, 0:3], kf[:, 13:14], A.subtract, None, None, k + ["p16"], k)
+        floor20(kf[:, 16:28], kf[:, 0:12], 12)
+        tt(kf[:, 28:31], kf[:, 16:19], kf[:, 20:23], A.is_equal, k, ["ma"])
+        ts(kf[:, 31:34], kf[:, 28:31], -1.0, A.mult, 1.0, A.add, ["ma"], ["mb"])
+        ts(kf[:, 24:28], kf[:, 24:28], 2.0, A.min, None, None, k, k)
+        ts(kf[:, 36:40], kf[:, 24:28], -20.0, A.mult, None, None, k, ["l1"])
+        tt(kf[:, 36:40], kf[:, 36:40], kf[:, 8:12], A.add, k + ["l1"], ["l1"])
+        ts(kf[:, 44:48], kf[:, 24:28], 1.0, A.is_ge, kf[:, 34:35], A.mult, k + ["l2"], ["l3"])
+        ts(kf[:, 40:44], kf[:, 24:28], 32.0, A.mult, kf[:, 4:5], A.add, k, ["l4"])
+        tt(kf[:, 40:44], kf[:, 40:44], kf[:, 44:48], A.add, ["l3", "l4"], k)
+        floor20(kf[:, 48:52], kf[:, 40:44], 4)
+        ts(kf[:, 52:56], kf[:, 48:52], 1.0, A.add, 15.0, A.min, k, ["l5"])
+        for o, key in ((48, "kf"), (52, "l5")):
+            ts(kf[:, o:o + 4], kf[:, o:o + 4], 20.0, A.mult, None, None, [key], [key])
+        for o, key in ((48, "kf"), (52, "l5")):
+            tt(kf[:, o:o + 4], kf[:, o:o + 4], kf[:, 36:40], A.add, [key, "l1"], [key])
+        ts(T.sl[:, 0:8], kf[:, 48:56], 319.0, A.min, None, None, ["kf", "l5"], ["sl"])
+        cp(T.sl[:, 8:11], kf[:, 0:3], k, ["sl2"])
+        fill(T.mg[:, :], 0.0, ["mg"])
+        for t in range(3):
+            ts(T.mg[:, 20 * t:20 + 20 * t], T.ones[:, 0:20], kf[:, 28 + t:29 + t], A.mult, None, None, ["ones", "ma"], ["mg"], t == 0)
+            ts(T.mg[:, 64 + 20 * t:84 + 20 * t], T.ones[:, 0:20], kf[:, 31 + t:32 + t], A.mult, None, None, ["ones", "mb"], ["mg"], False)
+        op("v", vec.tensor_scalar, (T.iw[:, :], T.iw[:, :], 15, None, A.bitwise_and), ["iw"], ["iw"])
+        ts(T.wmask[:, :], T.iw[:, :], 0.0, A.is_equal, None, None, ["iw"], ["wmask"])
+        cp(T.mg[:, 128:176], T.wmask[:, 0:48], ["wmask"], ["mg2"])
+        ts(T.phit[0:32, 0:32], T.phi0[0:32, 0:32], 0.0, A.is_lt, 320.0, A.mult, ["phi0"], ["phit"])
+        tt(T.phi0[0:32, 0:32], T.phi0[0:32, 0:32], T.phit[0:32, 0:32], A.add, ["phi0", "phit"], ["phi0"])
+
+    def spread_distances():
+        items = []
+        for t in range(3):
+            for a in range(4):
+                off = 96 * a + 32 * t - (64 if a == 3 and t else 0)
+                items.append(("y", T.phi[32 * a:32 * a + 32, 320 * t + off:320 * t + 320], T.phi0[0:32, 0:320 - off]))
+                if off:
+                    items.append(("y", T.phi[32 * a:32 * a + 32, 320 * t:320 * t + off], T.phi0[0:32, 320 - off:320]))
+        dmas("dp", items, ["phi0"], ["phi"])
 
     def first_codes():
         quant(T.uq[:, :], T.uqs[:, :], T.ut[:, :], ["ut"], ["uq"])
         quant(T.qx[:, :], T.qxs[:, :], T.x0[:, :], ["x"], ["qx"])
 
     def more_constants():
-        p = ["phi0"]
-        ts(T.phit[0:32, 0:32], T.phi0[0:32, 0:32], 0.0, A.is_lt, 320.0, A.mult, p, ["phit"])
-        tt(T.phi0[0:32, 0:32], T.phi0[0:32, 0:32], T.phit[0:32, 0:32], A.add, p + ["phit"], p)
-        items = []
-        for t in range(3):
-            for a in range(4):
-                off = 128 * t + 32 * (a if t < 2 else a % 2)
-                items.append(("y", T.phi[32 * a:32 * a + 32, 320 * t + off:320 * t + 320], T.phi0[0:32, 0:320 - off]))
-                if off:
-                    items.append(("y", T.phi[32 * a:32 * a + 32, 320 * t:320 * t + off], T.phi0[0:32, 320 - off:320]))
-        dmas("dp", items, p, ["phi"])
+        for i in range(8):
+            fill(T.codv[:, 3 * i:3 * i + 3], 1024.0 * (i + 1), ["codv"], False)
         for b in range(4):
             quant(T.eh[:, 128 * b:128 * b + 128], T.ehs[:, 128 * b:128 * b + 128], T.dh[:, 3 - b:515 - b], ["dh"], ["eh%d" % b])
-        for i in range(8):
-            op("v", vec.memset, (T.codv[:, 3 * i:3 * i + 3], 1024.0 * (i + 1)), [], ["codv"], None, False)
-        for t in range(3):
-            fill(T.ct[:, 256 * t:256 * t + 1], 16384.0, ["ct%d" % t])
-
-    def more_constants2():
         op("v", vec.tensor_scalar, (T.iw[:, :], T.ir[:, :], 15, None, A.bitwise_and), ["ir"], ["iw"])
         ts(T.seg[:, :], T.iw[:, :], 0.0, A.not_equal, None, None, ["iw"], ["seg"])
         fill(T.res[:, :], 0.0, ["res"])
-        for t in range(3):
-            fill(T.res[:, 20 * t:20 * t + 1], 2.0, ["res"])
-            fill(T.pt[:, 256 * t:256 * t + 1], 0.0, ["pt%d" % t])
-        for n in ("kg", "ag", "uk", "ua"):
-            fill(T[n][:, :], 0.0, [n])
-        for i in range(8):
-            op("v", vec.tensor_copy, (T.j24[:, 3 * i:3 * i + 3], kf[:, 0:3]), k, ["j24"], None, False)
-        ts(T.j24b[:, :], T.j24[:, :], 320.0, A.add, None, None, ["j24"], ["j24b"])
         fill(T.s20[:, :], 1.0, ["s20"])
         for t in range(3):
+            fill(T.res[:, 20 * t:20 * t + 1], 2.0, ["res"])
             fill(T.s20[:, 20 * t:20 * t + 1], 0.0, ["s20"])
-        ts(T.j16[:, :], T.ir[:, 0:20], 16.0, A.mult, kf[:, 13:14], A.add, ["ir", "p16"], ["j16"])
+            fill(T.pt[:, 256 * t:256 * t + 1], SAME, ["pt%d" % t])
+
+    def more_constants2():
+        for n in ("ag", "uk", "ua"):
+            fill(T[n][:, :], 0.0, [n])
+        fill(T.keep[:, 24:32], 0.0, ["keepz"])
+        for i in range(3):
+            ts(T.j24[:, 8 * i:8 * i + 8], T.ones[:, 0:8], kf[:, i:i + 1], A.mult, None, None, k + ["ones"], ["j24"], False)
+        ts(T.j24b[:, :], T.j24[:, :], 320.0, A.add, None, None, ["j24"], ["j24b"])
+        ts(T.j16[:, 0:8], T.ir[:, 0:8], 16.0, A.mult, kf[:, 13:14], A.add, ["ir", "p16"], ["j16"])
+        for a in range(1, 4):
+            ts(T.j16[:, 8 * a:8 * a + 8], T.j16[:, 0:8], 96.0 * a, A.add, None, None, ["j16"], ["j16b"], False)
 
     def later_constants():
         ts(T.dk[:, :], T.dh[:, :], 64.0, A.mult, None, None, ["dh"], ["dk"])
@@ -279,23 +281,19 @@ def rank_program(g, core, T, topo):
 
     def to_wrapped(src, dst, sem, queues, key_in, key_out):
         items = []
-        for t in range(3):
-            n = 4 if t < 2 else 2
-            for gr in range(8):
-                G, h = divmod(gr, 2)
-                items.append((queues[len(items) % len(queues)],
-                              dst[32 * G + 8 * t:32 * G + 8 * t + 2 * n, 16 * h:16 * h + 16],
-                              src[3 * gr + t:32 * n:32, 0:32]))
+        for gr in range(8):
+            G, h = divmod(gr, 2)
+            items.append((queues[gr % len(queues)], dst[32 * G:32 * G + 32, 16 * h:16 * h + 16], src[gr:128:8, 0:32]))
         dmas(sem, items, [key_in], [key_out])
 
-    for t in range(R):
-        rot = (3 * t) % 8
+    def to_list(dst, src, o, reads, writes):
+        for a in range(4):
+            n = 6 if a < 3 else 2
+            cp(dst[:, 6 * a:6 * a + n], src[:, o + 8 * a:o + 8 * a + n], reads, writes, False)
 
-        def by_group(fn):
-            n = 8 - rot
-            fn(slice(3 * rot, 24), slice(0, 3 * n))
-            if rot:
-                fn(slice(0, 3 * rot), slice(3 * n, 24))
+    for t in range(R):
+        grp = [(3 * t + i) % 8 for i in range(8)]
+
         def words():
             mm(0, C, T.uq[:, :], T.uqs[:, :], T.qx[:, :], T.qxs[:, :], ["uq", "qx"])
             ts(T.bt[:, 0:1280:4], T.ps[:, 0:C], 0.0, A.is_gt, None, None, ["ps0"], ["bt"])
@@ -305,7 +303,8 @@ def rank_program(g, core, T, topo):
                 mm(1 + h, C, T.cw[:, o:o + 128], T.cws[:, o:o + 128], T.bq[:, :], T.bqs[:, :], ["cw%d" % (2 * t + h), "bq"])
             act(T.w4[:, :], T.ps[:, 512:512 + C], AF.Copy, ["ps1"], ["w4"])
         if t == 0:
-            merge(record(powers, lambda: weights(0), first_codes, words), places)
+            merge(record(powers, lambda: weights(0), first_codes, words), record(make_places))
+            spread_distances()
         else:
             words()
         tt(T.gm[:, 0:128], T.w4[:, 0:C].indirect(T.sl[:, 0:8]), T.mg[:, 0:128], A.mult, ["w4", "sl", "mg"], ["gm"])
@@ -318,33 +317,26 @@ def rank_program(g, core, T, topo):
         cnt["rw"] += neng
         note(("dma", "rl", None), ["msg"], [])
         for c in range(3):
-            op("v", vec.tensor_reduce, (T.wj[:, c:c + 1], T.gm[:, 128 + 16 * c:144 + 16 * c], X, A.add), ["gm2"], ["wj"], waw=False)
-        cp(T.wji[:, :], T.wj[:, :], ["wj"], ["wji"])
-        if t == 0:
-            more_constants()
-        for i in range(8):
-            op("v", vec.tensor_scalar, (T.ob[:, 3 * i:3 * i + 3], T.wji[:, :], 2 * i, 1, A.logical_shift_right, A.bitwise_and), ["wji"], ["ob"], waw=False)
-        ts(T.nb[:, :], T.ob[:, :], -1.0, A.mult, 1.0, A.add, ["ob"], ["nb"])
-        tt(T.u0[:, :], T.ob[:, :], T.codv[:, :], A.mult, ["ob", "codv"], ["u0"])
-        cp(T.obf[:, :], T.ob[:, :], ["ob"], ["obf"])
-        tt(T.u1[:, :], T.nb[:, :], T.codv[:, :], A.mult, ["nb", "codv"], ["u1"])
-        cols = ["u0", "u1", "nb", "obf"]
+            op("v", vec.tensor_reduce, (T.wj[:, c:c + 1], T.gm[:, 128 + 16 * c:144 + 16 * c], X, A.add), ["gm2"], ["wj"], None, False)
 
-        def table(i, c):
-            n = 1 << i
-            lo, hi = slice(256 * c, 256 * c + n), slice(256 * c + n, 256 * c + 2 * n)
-            q = slice(3 * i + c, 3 * i + c + 1)
-            a, b = ("ct", "cu")[i % 2], ("cu", "ct")[i % 2]
-            o, r, w = T[b], [a + str(c)] + cols, [b + str(c)]
-            if c == 0:
-                ts(o[:, hi], T[a][:, lo], T.obf[:, q], A.mult, T.u1[:, q], A.add, r, w)
-                ts(o[:, lo], T[a][:, lo], T.nb[:, q], A.mult, T.u0[:, q], A.add, r, w, False)
-            else:
-                op("s", sca.activation, (o[:, hi], T[a][:, lo], AF.Identity), r, w, {"scale": T.obf[:, q], "bias": T.u1[:, q]})
-                op("s", sca.activation, (o[:, lo], T[a][:, lo], AF.Identity), r, w, {"scale": T.nb[:, q], "bias": T.u0[:, q]}, False)
-        for i in range(8):
-            for c in (1, 2):
-                table(i, c)
+        def bits():
+            cp(T.wji[:, :], T.wj[:, :], ["wj"], ["wji"])
+            for i in range(8):
+                op("v", vec.tensor_scalar, (T.ob[:, 3 * i:3 * i + 3], T.wji[:, :], 2 * i, 1, A.logical_shift_right, A.bitwise_and), ["wji"], ["ob"], None, False)
+            ob, nb = T.ob[:, :], T.nb[:, :]
+            ts(nb, ob, -1.0, A.mult, 1.0, A.add, ["ob"], ["nb"])
+            ts(T.tp[:, 0:96:4], ob, EPS - 1.0, A.mult, 1.0, A.add, ["ob"], ["tp"])
+            ts(T.tq[:, 0:96:4], ob, 1.0 - EPS, A.mult, None, None, ["ob"], ["tq"])
+            ts(T.tp[:, 2:96:4], ob, 1.0 - EPS, A.mult, EPS, A.add, ["ob"], ["tp"], False)
+            ts(T.tq[:, 2:96:4], nb, 1.0 - EPS, A.mult, None, None, ["nb"], ["tq"], False)
+            tt(T.tp[:, 1:96:4], ob, T.codv[:, :], A.mult, ["ob", "codv"], ["tp"], False)
+            tt(T.tp[:, 3:96:4], nb, T.codv[:, :], A.mult, ["nb", "codv"], ["tp"], False)
+            ts(T.tq[:, 1:96:4], ob, KEPT, A.mult, None, None, ["ob"], ["tq"], False)
+            ts(T.tq[:, 3:96:4], nb, KEPT, A.mult, None, None, ["nb"], ["tq"], False)
+        if t == 0:
+            merge(record(bits), record(more_constants))
+        else:
+            bits()
         for b in range(4):
             p = ["ps%d" % (4 + b)]
             mm(4 + b, C, T.eh[:, 128 * b:128 * b + 128], T.ehs[:, 128 * b:128 * b + 128], T.qx[:, :], T.qxs[:, :], ["eh%d" % b, "qx"])
@@ -352,118 +344,114 @@ def rank_program(g, core, T, topo):
                 act(T.fb[:, 640 * b + 320 * h:640 * b + 320 * h + 320], T.ps[:, 512 * (4 + b):512 * (4 + b) + C], AF.Copy, p, ["fb%d%d" % (b, h)])
             if b < 2:
                 act(T.fc[:, 320 * b:320 * b + 320], T.ps[:, 512 * (4 + b):512 * (4 + b) + C], AF.Copy, p, ["fc%d" % b])
-        if t == 0:
-            more_constants2()
-        ts(T.nbb[:, :], T.ob[:, :], -16384.0, A.mult, 16384.0, A.add, ["ob"], ["nbb"])
-        ts(T.obb[:, :], T.ob[:, :], 16384.0, A.mult, None, None, ["ob"], ["obb"])
         tt(T.wm[:, :], T.ps[:, 1024:1024 + C], T.wmask[:, :], A.mult, ["ps2", "wmask"], ["wm"])
-        table(0, 0)
         scan(T.wsc[:, :], T.seg[:, :], T.wm[:, :], 0.0, A.mult, A.add, ["seg", "wm"], ["wsc"])
-        table(1, 0)
         cp(T.wl[:, :], T.wsc[:, 15:C:16], ["wsc"], ["wl"])
-        for i in range(2, EARLY):
-            table(i, 0)
-
-        def pairs(c):
-            s = slice(320 * c, 320 * c + 320)
-            tt(T.n0[:, s], T.ct[:, 256 * c:256 * c + 256].indirect(T.wl[:, 0:20]), T.phi[:, s], A.add,
-               ["ct%d" % c, "wl", "phi"], ["n0%d" % c])
-            if t < R - 1:
-                fill(T.ct[:, 256 * c:256 * c + 1], 16384.0, ["ct%d" % c])
-        fillers = record(*[lambda i=i: table(i, 0) for i in range(EARLY, 8)], lambda: pairs(1), lambda: pairs(2), lambda: pairs(0))
-        rec[0] = []
         note(("dma", "rw", cnt["rw"]), [], ["pw"])
-        for c in range(3):
-            ts(T.sm[:, 20 * c:20 * c + 20], T.pw[:, 20 * c:20 * c + 20], T.wj[:, c:c + 1], A.add, None, None, ["pw", "wj"], ["sm%d" % c])
-        op("v", vec.tensor_scalar, (T.vi[:, :], T.sm[:, :], 0x5555, None, A.bitwise_and), ["sm0", "sm1", "sm2"], ["vi"])
-        ts(T.vz[:, :], T.vi[:, :], 0.0, A.is_equal, None, None, ["vi"], ["vz"])
-        ts(T.vv[:, :], T.vi[:, :], 2.0 ** -15, A.mult, None, None, ["vi"], ["vv"])
 
         def digit(i):
             op("v", vec.tensor_scalar, (T.dd[:, 60 * i:60 * i + 60], T.vi[:, :], 4 ** i, None, A.bitwise_and), ["vi"], ["dd%d" % i])
-        digit(0)
-        ts(T.ve[:, :], T.vi[:, :], 1.0, A.is_equal, None, None, ["vi"], ["ve"])
-        tt(T.vv[:, :], T.vv[:, :], T.vz[:, :], A.max, ["vv", "vz"], ["vv"])
-        scan(T.sc[:, :], T.s20[:, :], T.ve[:, :], 0.0, A.mult, A.max, ["s20", "ve"], ["sc"])
-        for i in range(8):
-            if i:
-                scan(T.sc[:, :], T.res[:, :], T.vv[:, :], 2.0, A.max, A.min, ["res", "vv"], ["sc"])
-            if i < 7:
-                for c in range(3):
-                    m = T.sc[:, 20 * c + 19:20 * c + 20]
-                    d = T.dd[:, 60 * i + 20 * c:60 * i + 20 * c + 20]
-                    if i:
-                        ts(T.kl[:, 20 * c:20 * c + 20], d, 2.0 ** -14, A.mult, m, A.is_gt, ["dd%d" % i, "sc"], ["kl%d" % c])
-                    else:
-                        ts(T.kl[:, 20 * c:20 * c + 20], d, m, A.mult, None, None, ["dd%d" % i, "sc"], ["kl%d" % c])
-            c3 = slice(3 * i, 3 * i + 3)
-            if i:
-                ts(T.keep[:, c3], T.sc[:, 19:60:20], 2.0 ** -14 * 4 ** i, A.is_lt, None, None, ["sc"], ["keep%d" % i])
-            else:
-                cp(T.keep[:, c3], T.sc[:, 19:60:20], ["sc"], ["keep%d" % i])
-            if i < 7:
-                if i < 6:
-                    digit(i + 1)
-                tt(T.vv[:, :], T.vv[:, :], T.kl[:, :], A.max, ["vv", "kl0", "kl1", "kl2"], ["vv"])
-            tt(T.pka[:, c3], T.keep[:, c3], T.obb[:, c3], A.mult, ["keep%d" % i, "obb"], ["pka%d" % i])
-            tt(T.pkb[:, c3], T.keep[:, c3], T.nbb[:, c3], A.mult, ["keep%d" % i, "nbb"], ["pkb%d" % i])
+
+        def double(i):
+            q = slice(12 * i, 12 * i + 12)
+            tt(T.sb[:, q], T.sb[:, q], T.tp[:, q], A.add, ["sb%d" % i, "tp"], ["sb%d" % i])
             n = 1 << i
             a, b = ("pt", "pv")[i % 2], ("pv", "pt")[i % 2]
             for c in range(3):
-                o = 256 * c
-                col = slice(3 * i + c, 3 * i + c + 1)
-                op("s", sca.activation, (T[b][:, o:o + n], T[a][:, o:o + n], AF.Identity), [a + str(c), "pka%d" % i], [b + str(c)], {"bias": T.pka[:, col]})
-                op("s", sca.activation, (T[b][:, o + n:o + 2 * n], T[a][:, o:o + n], AF.Identity), [a + str(c), "pkb%d" % i], [b + str(c)], {"bias": T.pkb[:, col]}, False)
-        drops, rec[0] = rec[0], None
-        merge(drops, fillers)
+                o, x = 256 * c, 12 * i + 4 * c
+                for h in range(2):
+                    act(T[b][:, o + h * n:o + h * n + n], T[a][:, o:o + n], AF.Identity, [a + str(c), "sb%d" % i], [b + str(c)], h == 0,
+                        scale=T.sb[:, x + 2 * h:x + 2 * h + 1], bias=T.sb[:, x + 2 * h + 1:x + 2 * h + 2])
+
+        def drops():
+            for c in range(3):
+                ts(T.sm[:, 20 * c:20 * c + 20], T.pw[:, 20 * c:20 * c + 20], T.wj[:, c:c + 1], A.add, None, None, ["pw", "wj"], ["sm%d" % c])
+            op("v", vec.tensor_scalar, (T.vi[:, :], T.sm[:, :], 0x5555, None, A.bitwise_and), ["sm0", "sm1", "sm2"], ["vi"])
+            ts(T.ve[:, :], T.vi[:, :], 1.0, A.is_equal, None, None, ["vi"], ["ve"])
+            ts(T.vz[:, :], T.vi[:, :], 0.0, A.is_equal, None, None, ["vi"], ["vz"])
+            ts(T.vv[:, :], T.vi[:, :], 2.0 ** -15, A.mult, None, None, ["vi"], ["vv"])
+            digit(0)
+            scan(T.sc[:, :], T.s20[:, :], T.ve[:, :], 0.0, A.mult, A.max, ["s20", "ve"], ["sc"])
+            tt(T.vv[:, :], T.vv[:, :], T.vz[:, :], A.max, ["vv", "vz"], ["vv"])
+            for i in range(8):
+                if i:
+                    scan(T.sc[:, :], T.res[:, :], T.vv[:, :], 2.0, A.max, A.min, ["res", "vv"], ["sc"])
+                if i < 7:
+                    for c in range(3):
+                        m = T.sc[:, 20 * c + 19:20 * c + 20]
+                        d = T.dd[:, 60 * i + 20 * c:60 * i + 20 * c + 20]
+                        o = T.kl[:, 20 * c:20 * c + 20]
+                        if i:
+                            ts(o, d, 2.0 ** -14, A.mult, m, A.is_gt, ["dd%d" % i, "sc"], ["kl%d" % c])
+                        else:
+                            ts(o, d, m, A.mult, None, None, ["dd%d" % i, "sc"], ["kl%d" % c])
+                c3 = slice(grp[i], 24, 8)
+                if i:
+                    ts(T.keep[:, c3], T.sc[:, 19:60:20], 2.0 ** -14 * 4 ** i, A.is_lt, None, None, ["sc"], ["keep%d" % i])
+                else:
+                    cp(T.keep[:, c3], T.sc[:, 19:60:20], ["sc"], ["keep%d" % i])
+                if i < 6:
+                    digit(i + 1)
+                if i:
+                    double(i - 1)
+                if i < 7:
+                    tt(T.vv[:, :], T.vv[:, :], T.kl[:, :], A.max, ["vv", "kl0", "kl1", "kl2"], ["vv"])
+                for c in range(3):
+                    r = slice(12 * i + 4 * c, 12 * i + 4 * c + 4)
+                    ts(T.sb[:, r], T.tq[:, r], T.keep[:, 8 * c + grp[i]:8 * c + grp[i] + 1], A.mult, None, None, ["keep%d" % i, "tq"], ["sb%d" % i], False)
+            double(7)
+        if t == 0:
+            merge(record(drops), record(more_constants2))
+        else:
+            drops()
         keeps = ["keep%d" % i for i in range(8)]
-        by_group(lambda o, i: op("v", vec.tensor_copy, (T.kg[:, o], T.keep[:, i]), keeps, ["kg"], None, False))
-        op("v", vec.transpose, (T.kt[:, :], T.kg[:, :]), ["kg"], ["kt"])
+        turn(T.kt[:, :], T.keep[:, :], keeps + ["keepz"], ["kt"])
         to_wrapped(T.kt, T.uk, "dk", ["y"], "kt", "uk")
         for c in range(3):
             s = slice(320 * c, 320 * c + 320)
-            tt(T.nn[:, s], T.pt[:, 256 * c:256 * c + 256].indirect(T.wl[:, 0:20]), T.n0[:, s], A.add,
-               ["pt%d" % c, "wl", "n0%d" % c], ["nn%d" % c])
+            tt(T.nn[:, s], T.pt[:, 256 * c:256 * c + 256].indirect(T.wl[:, 0:20]), T.phi[:, s], A.add, ["pt%d" % c, "wl", "phi"], ["nn%d" % c])
             for i in (2, 3):
                 z = slice(960 * (i - 2) + 320 * c, 960 * (i - 2) + 320 * c + 320)
                 act(T.zz[:, z], T.nn[:, s], AF.Abs, ["nn%d" % c], ["zz%d%d" % (i, c)], bias=-1024.0 * (i + 1))
         nns = ["nn0", "nn1", "nn2"]
-        ts(T.ac[:, 0:24], T.keep[:, :], 1000.0, A.mult, None, None, keeps, ["ac0"])
+        act(T.zz[:, 5760:6080], T.nn[:, 640:960], AF.Abs, ["nn2"], ["zz12"], bias=-2048.0)
         for i in range(4, 8):
-            op("s", sca.activation, (T.zz[:, 960 * (i - 2):960 * (i - 1)], T.nn[:, :], AF.Abs), nns, ["zz%d%d" % (i, c) for c in range(3)], {"bias": -1024.0 * (i + 1)})
-        for c in range(3):
-            o = 320 * c
-            scan(T.s0[:, 160 * c:160 * c + 160], T.nn[:, o:o + 160], T.nn[:, o + 160:o + 320], 65536.0, A.min, A.min, ["nn%d" % c], ["s0%d" % c])
-        ts(T.zv[:, :], T.nn[:, :], -2048.0, A.add, None, None, nns, ["zv"])
-        tt(T.jk[:, :], T.ac[:, 0:24], T.j24[:, :], A.add, ["ac0", "j24"], ["jk"])
+            act(T.zz[:, 960 * (i - 2):960 * (i - 1)], T.nn[:, :], AF.Abs, nns, ["zz%d%d" % (i, c) for c in range(3)], bias=-1024.0 * (i + 1))
         so = T.so
-        ts(so[:, 159:480:160], T.s0[:, 159:480:160], -1024.0, A.add, None, None, ["s00", "s01", "s02"], ["so"])
+
+        def least(o, src, x, reads, w, buf=None):
+            scan((so if buf is None else buf)[:, o:o + 160], src[:, x:x + 160], src[:, x + 160:x + 320], 65536.0, A.min, A.min, reads, w, False)
         for c in range(3):
-            op("v", vec.tensor_reduce, (so[:, 639 + 160 * c:640 + 160 * c], T.zv[:, 320 * c:320 * c + 320], X, A.min), ["zv"], ["so"],
-               {"apply_absolute_value": True}, waw=False)
-        if t < R - 1:
-            for c in range(3):
-                fill(T.pt[:, 256 * c:256 * c + 1], 0.0, ["pt%d" % c])
+            least(160 * c, T.nn, 320 * c, ["nn%d" % c], ["s0"], T.s0)
+        ts(T.zv[:, 0:640], T.nn[:, 0:640], -2048.0, A.add, None, None, nns, ["zv"])
+        ts(so[:, 160 * grp[0] + 159:3840:1280], T.s0[:, 159:480:160], -1024.0, A.add, None, None, ["s0"], ["so"])
+        for c in range(2):
+            o = 160 * (8 * c + grp[1]) + 159
+            op("v", vec.tensor_reduce, (so[:, o:o + 1], T.zv[:, 320 * c:320 * c + 320], X, A.min), ["zv"], ["so"],
+               {"apply_absolute_value": True}, False)
 
         pq = T.pq
+        n32 = slice(0, 32)
         order = [
-            lambda: scan(T.us[:, :], T.seg[:, 0:32], T.uk[:, :], 0.0, A.mult, A.add, ["seg", "uk"], ["us"]),
-            lambda: op("v", vec.transpose, (T.kw[:, :], T.uk[:, :]), ["uk"], ["kw"]),
+            lambda: ts(T.ac[:, 0:24], T.keep[:, 0:24], 1000.0, A.mult, None, None, keeps, ["ac0"]),
+            lambda: tt(T.jk[:, :], T.ac[:, 0:24], T.j24[:, :], A.add, ["ac0", "j24"], ["jk"]),
+            lambda: scan(T.us[:, :], T.seg[:, n32], T.uk[:, :], 0.0, A.mult, A.add, ["seg", "uk"], ["us"]),
+            lambda: turn(T.kw[:, :], T.uk[:, :], ["uk"], ["kw"]),
             lambda: ts(T.uto[:, 0:16], T.ones[:, 0:16], T.us[:, 15:16], A.mult, None, None, ["ones", "us"], ["uto0"]),
             lambda: ts(T.uto[:, 16:32], T.ones[:, 0:16], T.us[:, 31:32], A.mult, None, None, ["ones", "us"], ["uto1"]),
-            lambda: op("v", vec.transpose, (T.ust[:, :], T.us[:, :]), ["us"], ["ust"]),
-            lambda: op("v", vec.transpose, (T.utt[:, :], T.uto[:, :]), ["uto0", "uto1"], ["utt"]),
-            lambda: ts(pq[:, 80:100], T.kw[:, 0:20], 1000.0, A.mult, -1000.0, A.add, ["kw"], ["pq4"]),
-            lambda: scan(pq[:, 0:20], T.ones[:, 0:20], T.utt[:, 0:20], 0.0, A.mult, A.add, ["ones", "utt"], ["pq"]),
-            lambda: tt(pq[:, 20:40], T.ust[:, 0:20], T.utt[:, 0:20], A.subtract, ["ust", "utt"], ["pq1"]),
-            lambda: ts(pq[:, 40:41], pq[:, 19:20], -1.0, A.mult, 319.0, A.add, ["pq"], ["pq2"]),
-            lambda: tt(pq[:, 20:40], pq[:, 20:40], pq[:, 0:20], A.add, ["pq", "pq1"], ["pq1"]),
-            lambda: ts(pq[:, 80:100], pq[:, 80:100], pq[:, 40:41], A.add, None, None, ["pq4", "pq2"], ["pq4"]),
-            lambda: tt(pq[:, 60:80], T.j16[:, :], pq[:, 20:40], A.subtract, ["j16", "pq1"], ["pq3"]),
-            lambda: tt(pq[:, 80:100], pq[:, 80:100], pq[:, 20:40], A.add, ["pq1", "pq4"], ["pq4"]),
-            lambda: tt(pq[:, 60:80], pq[:, 60:80], pq[:, 80:100], A.max, ["pq3", "pq4"], ["pq3"]),
-            lambda: cp(T.poff[:, :], pq[:, 60:80], ["pq3"], ["poff"]),
-            lambda: op("v", vec.tensor_copy, (T.lw[:, 0:C].indirect(T.poff[:, 0:20]), T.jrow[:, :]), ["poff", "jrow"], ["lw"]),
+            lambda: turn(T.ust[:, :], T.us[:, :], ["us"], ["ust"]),
+            lambda: ts(pq[:, 96:128], T.kw[:, :], 1000.0, A.mult, -1000.0, A.add, ["kw"], ["pq4"]),
+            lambda: turn(T.utt[:, :], T.uto[:, :], ["uto0", "uto1"], ["utt"]),
+            lambda: scan(pq[:, n32], T.ones[:, n32], T.utt[:, :], 0.0, A.mult, A.add, ["ones", "utt"], ["pq"]),
+            lambda: tt(pq[:, 32:64], T.ust[:, :], T.utt[:, :], A.subtract, ["ust", "utt"], ["pq1"]),
+            lambda: ts(pq[:, 128:129], pq[:, 25:26], -1.0, A.mult, 319.0, A.add, ["pq"], ["pq2"]),
+            lambda: tt(pq[:, 32:64], pq[:, 32:64], pq[:, n32], A.add, ["pq", "pq1"], ["pq1"]),
+            lambda: ts(pq[:, 96:128], pq[:, 96:128], pq[:, 128:129], A.add, None, None, ["pq4", "pq2"], ["pq4"]),
+            lambda: tt(pq[:, 64:96], T.j16[:, :], pq[:, 32:64], A.subtract, ["j16", "j16b", "pq1"], ["pq3"]),
+            lambda: tt(pq[:, 96:128], pq[:, 96:128], pq[:, 32:64], A.add, ["pq1", "pq4"], ["pq4"]),
+            lambda: tt(pq[:, 64:96], pq[:, 64:96], pq[:, 96:128], A.max, ["pq3", "pq4"], ["pq3"]),
+            lambda: to_list(T.poff, pq, 64, ["pq3"], ["poff"]),
+            lambda: cp(T.lw[:, 0:C].indirect(T.poff[:, 0:20]), T.jrow[:, :], ["poff", "jrow"], ["lw"]),
             lambda: tt(T.lm[:, :], T.lw[:, 0:128], T.wmask[:, 0:128], A.mult, ["lw", "wmask"], ["lm"]),
             lambda: scan(T.ls[:, :], T.seg[:, 0:128], T.lm[:, :], 0.0, A.mult, A.add, ["seg", "lm"], ["ls"]),
             lambda: cp(T.loff[:, :], T.ls[:, 15:128:16], ["ls"], ["loff"]),
@@ -473,19 +461,25 @@ def rank_program(g, core, T, topo):
             for _ in range(n):
                 if order:
                     order.pop(0)()
-        for i in range(2, 8):
+        for i in range(1, 8):
             for c in range(3):
-                o = 960 * (i - 2) + 320 * c
-                op("v", vec.tensor_tensor_scan, (so[:, 480 * i + 160 * c:480 * i + 160 * c + 160], T.zz[:, o:o + 160], T.zz[:, o + 160:o + 320], 65536.0, A.min, A.min),
-                   ["zz%d%d" % (i, c)], ["so"], None, False)
-            some((0, 0, 0, 0, 0, SOME5, SOME6, 0)[i])
+                if i > 1:
+                    least(160 * (8 * c + grp[i]), T.zz, 960 * (i - 2) + 320 * c, ["zz%d%d" % (i, c)], ["so"])
+                elif c == 2:
+                    least(160 * (8 * c + grp[i]), T.zz, 5760, ["zz12"], ["so"])
+            some(SOME[i])
         tt(T.ac[:, 24:48], so[:, 159:3840:160], T.jk[:, :], A.add, ["so", "jk"], ["ac1"])
-        by_group(lambda o, i: op("v", vec.tensor_tensor, (T.ag[:, o], T.ac[:, 24 + i.start:24 + i.stop], T.j24b[:, i], A.min), ["ac1", "j24b"], ["ag"], None, False))
-        op("v", vec.transpose, (T.at[:, :], T.ag[:, :]), ["ag"], ["at"])
+        some(SOME[8])
+        tt(T.ag[:, 0:24], T.ac[:, 24:48], T.j24b[:, :], A.min, ["ac1", "j24b"], ["ag"])
+        some(SOME[9])
+        turn(T.at[:, :], T.ag[:, :], ["ag"], ["at"])
         to_wrapped(T.at, T.ua, "da", ["y", "s"], "at", "ua")
-        some(20)
-        op("v", vec.transpose, (T.aw[:, :], T.ua[:, :]), ["ua"], ["aw"])
-        cp(T.aoff[:, :], T.aw[:, 0:20], ["aw"], ["aoff"])
+        if t < R - 1:
+            for c in range(3):
+                fill(T.pt[:, 256 * c:256 * c + 1], SAME, ["pt%d" % c])
+        some(40)
+        turn(T.aw[:, :], T.ua[:, :], ["ua"], ["aw"])
+        to_list(T.aoff, T.aw, 0, ["aw"], ["aoff"])
         for b in (2, 3):
             act(T.zg[:, 320 * b - 640:320 * b - 320], T.fb[:, 640 * b:640 * b + 640].indirect(T.aoff[:, 0:20]), AF.Copy, ["fb%d0" % b, "fb%d1" % b, "aoff"], ["zg%d" % b])
         for b in range(4):
@@ -507,30 +501,33 @@ def rank_program(g, core, T, topo):
         cnt["re"] += 2 * neng
         note(("dma", "rl", None), ["qe"], [])
         note(("dma", "re", cnt["re"]), [], ["qa"])
-        ts(pq[:, 100:120], pq[:, 60:80], 128.0, A.is_lt, None, None, ["pq3"], ["pq5"])
-        ts(pq[:, 60:80], pq[:, 60:80], 320.0, A.add, None, None, ["pq3"], ["pq3"])
-        tt(pq[:, 60:80], pq[:, 60:80], T.j16[:, :], A.subtract, ["pq3", "j16"], ["pq3"])
-        tt(pq[:, 60:80], pq[:, 60:80], pq[:, 100:120], A.mult, ["pq3", "pq5"], ["pq3"])
-        tt(pq[:, 60:80], pq[:, 60:80], T.j16[:, :], A.add, ["pq3", "j16"], ["pq3"])
-        cp(T.selo[:, :], pq[:, 60:80], ["pq3"], ["selo"])
+        ts(pq[:, 132:164], pq[:, 64:96], 128.0, A.is_lt, None, None, ["pq3"], ["pq5"])
+        ts(pq[:, 64:96], pq[:, 64:96], 320.0, A.add, None, None, ["pq3"], ["pq3"])
+        tt(pq[:, 64:96], pq[:, 64:96], T.j16[:, :], A.subtract, ["pq3", "j16", "j16b"], ["pq3"])
+        tt(pq[:, 64:96], pq[:, 64:96], pq[:, 132:164], A.mult, ["pq3", "pq5"], ["pq3"])
+        tt(pq[:, 64:96], pq[:, 64:96], T.j16[:, :], A.add, ["pq3", "j16"], ["pq3"])
+        to_list(T.selo, pq, 64, ["pq3"], ["selo"])
         if t == 0:
             later_constants()
         if t == R - 1:
             ts(T.am[:, 0:32], T.at[:, :], 320.0, A.is_ge, -320.0, A.mult, ["at"], ["am"])
             tt(T.am[:, 32:64], T.at[:, :], T.am[:, 0:32], A.add, ["at", "am"], ["am2"])
-            dmas("do", [("y", T.al[:, 128 * c + 32 * a:128 * c + 32 * a + 32], T.am[32 * a + c:32 * a + 24:3, 32:64])
-                        for c in range(3) for a in range(4 if c < 2 else 2)] + [("y", T.al[:, 320:448], T.lw[0:128:16, 0:128])], ["am2", "lw"], ["al"])
+            dmas("do", [("y", T.al[:, 96 * a + 32 * c:96 * a + 32 * c + 32], T.am[32 * a + 8 * c:32 * a + 8 * c + 8, 32:64])
+                        for a in range(4) for c in range(3 if a < 3 else 1)] + [("y", T.al[:, 320:448], T.lw[0:128:16, 0:128])], ["am2", "lw"], ["al"])
         for b in range(4):
             w = slice(128 * b, 128 * b + 128)
             mm(4 + b, 128, T.wq[:, w], T.wqs[:, w], T.qa[:, :], T.qas[:, :], ["w", "qa"], True, False)
             mm(4 + b, 128, T.ek[:, w], T.eks[:, w], T.qa[:, :], T.qas[:, :], ["ek%d" % b, "qa"], False, True)
             o, i = T.zt[:, 448 * b + 320:448 * b + 448], T.ps[:, 512 * (4 + b):512 * (4 + b) + 128]
-            n, win = T.xs[:, b:1280:4], T.zt[:, 448 * b:448 * b + 448].indirect(T.selo[:, 0:20])
             if b % 2 == 0:
                 act(o, i, AF.Copy, ["ps%d" % (4 + b)], ["tm%d" % b], scale=0.03125)
-                act(n, win, AF.Copy, ["zt%d" % b, "tm%d" % b, "selo"], ["xs%d" % b])
             else:
                 ts(o, i, 0.03125, A.mult, None, None, ["ps%d" % (4 + b)], ["tm%d" % b])
+        for b in range(4):
+            n, win = T.xs[:, b:1280:4], T.zt[:, 448 * b:448 * b + 448].indirect(T.selo[:, 0:20])
+            if b % 2 == 0:
+                act(n, win, AF.Copy, ["zt%d" % b, "tm%d" % b, "selo"], ["xs%d" % b])
+            else:
                 cp(n, win, ["zt%d" % b, "tm%d" % b, "selo"], ["xs%d" % b])
         quant(T.qx[:, :], T.qxs[:, :], T.xs[:, :], ["xs%d" % b for b in range(4)], ["qx"])
     dmas("do", [("y", T.oc[:, :], T.qx[:, 0:C].bitcast(dt.uint8))] + [("s", T.osc[4 * i:4 * i + 4, :], T.qxs[32 * i:32 * i + 4, 0:C]) for i in range(4)], ["qx"], ["oc"])

from concourse.bass import DstId, RemoteDMATransfer
from concourse.mybir import dt, AluOpType, AxisListType, ActivationFunctionType

C, K, R = 320, 128, 3
SOME = (0, 0, 0, 2, 2, 2, 3, 2, 2, 2)
EPS, KEPT, SAME = 2.0 ** -12, 2.0 ** 99, 12288.0
F8, F32, BF, I32, U16, U8 = "float8_e4m3fn_x4", "float32", "bfloat16", "int32", "uint16", "uint8"


def _sb(n, d):
    return ("sbuf", [128, n], d)


SCRATCH = {
    "ps": ("psum", [128, 4096], F32),
    "x0": _sb(1280, BF), "xs": _sb(1280, BF), "qx": _sb(C, F8), "qxs": _sb(C, U8),
    "ut": _sb(512, BF), "uq": _sb(128, F8), "uqs": _sb(128, U8),
    "vt": _sb(512, BF), "vq": _sb(128, F8), "vqs": _sb(128, U8),
    "wq": _sb(512, F8), "wqs": _sb(512, U8),
    "dg": _sb(516, BF), "dh": _sb(516, BF), "dk": _sb(516, BF),
    "eh": _sb(512, F8), "ehs": _sb(512, U8), "ek": _sb(512, F8), "eks": _sb(512, U8),
    "cwt": _sb(512, BF), "cw": _sb(768, F8), "cws": _sb(768, U8),
    "ip": _sb(4, I32), "ir": _sb(C, I32), "iw": _sb(C, I32), "io8": _sb(8, I32), "i4": _sb(4, I32),
    "kf": _sb(96, F32), "ki": _sb(32, I32), "jrow": _sb(C, F32), "wmask": _sb(C, F32), "seg": _sb(C, F32),
    "ones": _sb(128, F32), "pw4": _sb(16, F32), "pw2": _sb(16, F32), "tmp8": _sb(16, F32), "oneh": _sb(8, F32),
    "sl": _sb(12, U16), "mg": _sb(176, F32), "phi0": _sb(C, F32), "phit": _sb(C, F32), "phi": _sb(960, F32), "j24": _sb(24, F32),
    "j24b": _sb(24, F32), "j16": _sb(32, F32), "codv": _sb(24, F32), "res": _sb(60, F32), "s20": _sb(60, F32),
    "bt": _sb(1280, BF), "bq": _sb(C, F8), "bqs": _sb(C, U8),
    "w4": _sb(C, F32), "gm": _sb(176, F32), "ms": _sb(60, F32), "msg": _sb(60, U16), "pw": _sb(60, U16),
    "wm": _sb(C, F32), "wsc": _sb(C, F32), "wl": _sb(20, U16),
    "wj": _sb(3, F32), "wji": _sb(3, I32), "ob": _sb(24, I32), "nb": _sb(24, F32),
    "tp": _sb(96, F32), "tq": _sb(96, F32), "sb": _sb(96, F32), "pt": _sb(768, BF), "pv": _sb(768, BF), "nn": _sb(960, F32),
    "sm": _sb(60, I32), "vi": _sb(60, I32), "dd": _sb(480, I32), "vv": _sb(60, F32), "vz": _sb(60, F32), "ve": _sb(60, F32),
    "sc": _sb(60, F32), "kl": _sb(60, F32), "keep": _sb(32, F32),
    "zz": _sb(6 * 960 + 320, F32), "zv": _sb(640, F32), "so": _sb(24 * 160, F32), "s0": _sb(480, F32), "jk": _sb(24, F32), "ac": _sb(48, F32),
    "kt": _sb(32, F32), "ag": _sb(32, F32), "at": _sb(32, F32), "am": _sb(64, F32), "uk": _sb(32, F32), "ua": _sb(32, F32),
    "us": _sb(32, F32), "uto": _sb(32, F32), "ust": _sb(32, F32), "utt": _sb(32, F32), "kw": _sb(32, F32), "pq": _sb(176, F32),
    "poff": _sb(20, U16), "selo": _sb(20, U16), "lw": _sb(C, F32), "lm": _sb(128, F32), "ls": _sb(128, F32), "loff": _sb(8, U16),
    "aw": _sb(32, F32), "aoff": _sb(20, U16),
    "fb": _sb(2560, BF), "fc": _sb(640, BF), "zg": _sb(640, F32), "zt": _sb(4 * 448, BF), "et": _sb(512, BF),
    "qe": _sb(128, F8), "qes": _sb(128, U8), "qa": _sb(128, F8), "qas": _sb(128, U8), "yo": _sb(C, F32),
}
SEMAPHORES = ["cv", "cs", "ct", "cg", "dx", "du", "dv", "dw", "dk", "da", "do", "dp", "rw", "re", "rl"]


def rank_program(g, core, T, topo):
    rank = T.rank_of(core)
    if rank is None:
        return
    A, AF, X = AluOpType, ActivationFunctionType, AxisListType.X
    partner = T.cores[rank ^ 1]
    rid, pid = topo.addr(partner)[:2]
    mask, neng = topo.mask(core, partner), len(topo.engines(core, partner))
    eng = {"v": g.vector, "s": g.scalar, "t": g.tensor, "g": g, "y": g.sync}
    own = {"v": "cv", "s": "cs", "t": "ct", "g": "cg"}
    cnt = {s: 0 for s in SEMAPHORES}
    seen = {q: {} for q in eng}
    wr, rd = {}, {}

    def need(q, tok):
        v = cnt[tok[1]] if tok[2] is None else tok[2]
        if seen[q].get(tok[1], 0) < v:
            eng[q].wait_ge(T.sem[tok[1]], v)
            seen[q][tok[1]] = v

    def waits(q, reads, writes, waw=True):
        for k in reads:
            for tok in wr.get(k, []):
                need(q, tok)
            if k[:2] == "ps":
                for tok in rd.get(k, []):
                    if tok[0] != q:
                        need(q, tok)
        for k in writes:
            for tok in wr.get(k, []):
                if waw or tok[0] != q:
                    need(q, tok)
            for tok in rd.get(k, []):
                need(q, tok)

    def note(tok, reads, writes):
        for k in reads:
            rd.setdefault(k, []).append(tok)
        for k in writes:
            wr[k] = [tok]
            rd[k] = []

    rec = [None]

    def record(*fns):
        rec[0] = []
        for fn in fns:
            fn()
        r, rec[0] = rec[0], None
        return r

    def merge(*lists):
        for _, n, i in sorted(((i + 0.5) / len(l), n, i) for n, l in enumerate(lists) for i in range(len(l))):
            op(*lists[n][i])

    def op(q, call, args, reads, writes, kw=None, waw=True):
        if rec[0] is not None:
            rec[0].append((q, call, args, reads, writes, kw, waw))
            return
        waits(q, reads, writes, waw)
        s = own[q]
        call(*args, **(kw or {})).then_inc(T.sem[s], 1)
        cnt[s] += 1
        note((q, s, cnt[s]), reads, writes)

    def dmas(sem, items, reads, writes):
        for q in sorted(set(i[0] for i in items)):
            waits(q, reads, writes)
        for q, o, i in items:
            eng[q].dma_start(o, i).then_inc(T.sem[sem], 16)
            cnt[sem] += 16
        note(("dma", sem, None), reads, writes)

    vec, sca = g.vector, g.scalar

    def ts(o, i, s1, o1, s2, o2, reads, writes, waw=True):
        if o2 is None:
            op("v", vec.tensor_scalar, (o, i, s1, None, o1), reads, writes, None, waw)
        else:
            op("v", vec.tensor_scalar, (o, i, s1, s2, o1, o2), reads, writes, None, waw)

    def tt(o, a, b, f, reads, writes, waw=True):
        op("v", vec.tensor_tensor, (o, a, b, f), reads, writes, None, waw)

    def cp(o, i, reads, writes, waw=True):
        op("v", vec.tensor_copy, (o, i), reads, writes, None, waw)

    def act(o, i, f, reads, writes, waw=True, **kw):
        op("s", sca.activation, (o, i, f), reads, writes, kw, waw)

    def fill(o, c, w, waw=True):
        op("v", vec.memset, (o, c), [], w, None, waw)

    def scan(o, a, b, init, f, h, reads, writes, waw=True):
        op("v", vec.tensor_tensor_scan, (o, a, b, init, f, h), reads, writes, None, waw)

    def turn(o, i, reads, writes):
        op("v", vec.transpose, (o, i), reads, writes)

    def quant(q, s, t, reads, writes):
        op("v", vec.quantize_mx, (q, s, t), reads, writes)

    def mm(bank, n, l, ls, r, rs, reads, start=True, stop=True):
        op("t", g.tensor.matmul_mx, (T.ps[:, 512 * bank:512 * bank + n], l, ls, r, rs, start, stop), reads, ["ps%d" % bank], None, start)

    def iota(o, pat, base, cm, w, **kw):
        op("g", g.iota, (o, pat, base, cm), [], w, kw)

    dmas("dx", [("y", T.x0[:, 0:640], T.x[:, 0:640]), ("s", T.x0[:, 640:1280], T.x[:, 640:1280])], [], ["x"])
    dmas("du", [("s", T.ut[:], T.u[:, :])], [], ["ut"])
    dmas("dw", [("y", T.wq[:, 0:512].bitcast(dt.uint8), T.wc[:, 0:2048]), ("y", T.wqs[:, 0:512], T.ws[:, 0:512])], [], ["w"])
    dmas("dv", [("y", T.vt[:], T.v[:, :])], [], ["vt"])

    iota(T.ip[:, 0:1], [[1, 1]], 0, 1, ["ip"])
    iota(T.io8[:, :], [[-16, 8]], 0, 1, ["io8"])
    iota(T.i4[:, :], [[16, 4]], 0, 0, ["i4"])
    iota(T.iw[:, :], [[1, C]], 128, -1, ["iw"])
    fill(T.ones[:, :], 1.0, ["ones"])
    fill(T.dg[:, :], 0.5, ["dg"])

    def powers():
        fill(T.tmp8[:, 8:16], 0.0, ["t8b"])
        for base, buf in ((4.0, T.pw4), (2.0, T.pw2)):
            fill(T.tmp8[:, 0:8], base, ["t8"])
            scan(buf[:, 0:8], T.tmp8[:, 0:8], T.tmp8[:, 8:16], 1.0 / base, A.mult, A.add, ["t8", "t8b"], ["pw"])
            cp(buf[:, 8:16], buf[:, 0:8], ["pw"], ["pw"])
        fill(T.cwt[:, :], 0.0, ["cwt"])
        fill(T.bt[:, :], 0.0, ["bt"])
        ts(T.oneh[:, :], T.io8[:, :], 0.0, A.is_equal, None, None, ["io8"], ["oneh"])
    op("g", g.affine_select, (T.dh[:, :], T.dg[:, :], [[-1, 516]], A.is_equal, 0.0, 3, 4), ["dg"], ["dh"])
    iota(T.phi0[0:32, :], [[1, C]], 0, -1, ["phi0"], allow_small_or_imprecise_dtypes=True)
    iota(T.ir[:, :], [[1, C]], 0, 0, ["ir"])
    iota(T.jrow[:, :], [[1, C]], 0, 0, ["jrow"], allow_small_or_imprecise_dtypes=True)

    def weights(t):
        s = (-3 * t) % 8
        for h, buf in enumerate((T.pw4, T.pw2)):
            tt(T.tmp8[:, 0:8], T.oneh[:, :], buf[:, s:s + 8], A.mult, ["oneh", "pw"], ["t8"])
            op("v", vec.tensor_reduce, (T.kf[:, 90:91], T.tmp8[:, 0:8], X, A.add), ["t8"], ["wcol"])
            ts(T.cwt[:, 0:512:4], T.ones[:, 0:128], T.kf[:, 90:91], A.mult, None, None, ["ones", "wcol"], ["cwt"])
            o = 128 * (2 * t + h)
            quant(T.cw[:, o:o + 128], T.cws[:, o:o + 128], T.cwt[:, :], ["cwt"], ["cw%d" % (2 * t + h)])

    kf, k, ki = T.kf, ["kf"], ["ki"]

    def floor20(o, i, n):
        ts(kf[:, 72:72 + n], i, 0.05, A.mult, -0.475, A.add, k, ["fl"])
        cp(T.ki[:, 16:16 + n], kf[:, 72:72 + n], ["fl"], ["fli"])
        cp(o, T.ki[:, 16:16 + n], ["fli"], k)

    def make_places():
        fill(kf[:, 0:12], 0.0, k)
        op("v", vec.tensor_scalar, (T.ki[:, 0:1], T.ip[:, 0:1], 15, None, A.bitwise_and), ["ip"], ki)
        op("v", vec.tensor_scalar, (T.ki[:, 1:2], T.ip[:, 0:1], 5, None, A.logical_shift_right), ["ip"], ["ki1"])
        cp(kf[:, 12:13], T.ip[:, 0:1], ["ip"], ["ipf"])
        cp(kf[:, 13:14], T.ki[:, 0:1], ki, ["p16"])
        ts(kf[:, 0:1], T.ki[:, 1:2], 64.0, A.mult, kf[:, 12:13], A.add, ["ki1", "ipf"], k)
        ts(kf[:, 34:35], T.ki[:, 1:2], 3.0, A.is_equal, -64.0, A.mult, ["ki1"], ["l2"])
        ts(kf[:, 1:2], kf[:, 0:1], 32.0, A.add, kf[:, 34:35], A.add, k + ["l2"], k)
        ts(kf[:, 2:3], kf[:, 0:1], 64.0, A.add, kf[:, 34:35], A.add, k + ["l2"], k, False)
        ts(kf[:, 8:12], T.i4[:, :], kf[:, 13:14], A.add, None, None, ["i4", "p16"], k, False)
        ts(kf[:, 4:7], kf[:, 0:3], kf[:, 13:14], A.subtract, None, None, k + ["p16"], k)
        floor20(kf[:, 16:28], kf[:, 0:12], 12)
        tt(kf[:, 28:31], kf[:, 16:19], kf[:, 20:23], A.is_equal, k, ["ma"])
        ts(kf[:, 31:34], kf[:, 28:31], -1.0, A.mult, 1.0, A.add, ["ma"], ["mb"])
        ts(kf[:, 24:28], kf[:, 24:28], 2.0, A.min, None, None, k, k)
        ts(kf[:, 36:40], kf[:, 24:28], -20.0, A.mult, None, None, k, ["l1"])
        tt(kf[:, 36:40], kf[:, 36:40], kf[:, 8:12], A.add, k + ["l1"], ["l1"])
        ts(kf[:, 44:48], kf[:, 24:28], 1.0, A.is_ge, kf[:, 34:35], A.mult, k + ["l2"], ["l3"])
        ts(kf[:, 40:44], kf[:, 24:28], 32.0, A.mult, kf[:, 4:5], A.add, k, ["l4"])
        tt(kf[:, 40:44], kf[:, 40:44], kf[:, 44:48], A.add, ["l3", "l4"], k)
        floor20(kf[:, 48:52], kf[:, 40:44], 4)
        ts(kf[:, 52:56], kf[:, 48:52], 1.0, A.add, 15.0, A.min, k, ["l5"])
        for o, key in ((48, "kf"), (52, "l5")):
            ts(kf[:, o:o + 4], kf[:, o:o + 4], 20.0, A.mult, None, None, [key], [key])
        for o, key in ((48, "kf"), (52, "l5")):
            tt(kf[:, o:o + 4], kf[:, o:o + 4], kf[:, 36:40], A.add, [key, "l1"], [key])
        ts(T.sl[:, 0:8], kf[:, 48:56], 319.0, A.min, None, None, ["kf", "l5"], ["sl"])
        cp(T.sl[:, 8:11], kf[:, 0:3], k, ["sl2"])
        fill(T.mg[:, :], 0.0, ["mg"])
        for t in range(3):
            ts(T.mg[:, 20 * t:20 + 20 * t], T.ones[:, 0:20], kf[:, 28 + t:29 + t], A.mult, None, None, ["ones", "ma"], ["mg"], t == 0)
            ts(T.mg[:, 64 + 20 * t:84 + 20 * t], T.ones[:, 0:20], kf[:, 31 + t:32 + t], A.mult, None, None, ["ones", "mb"], ["mg"], False)
        op("v", vec.tensor_scalar, (T.iw[:, :], T.iw[:, :], 15, None, A.bitwise_and), ["iw"], ["iw"])
        ts(T.wmask[:, :], T.iw[:, :], 0.0, A.is_equal, None, None, ["iw"], ["wmask"])
        cp(T.mg[:, 128:176], T.wmask[:, 0:48], ["wmask"], ["mg2"])
        ts(T.phit[0:32, 0:32], T.phi0[0:32, 0:32], 0.0, A.is_lt, 320.0, A.mult, ["phi0"], ["phit"])
        tt(T.phi0[0:32, 0:32], T.phi0[0:32, 0:32], T.phit[0:32, 0:32], A.add, ["phi0", "phit"], ["phi0"])

    def spread_distances():
        items = []
        for t in range(3):
            for a in range(4):
                off = 96 * a + 32 * t - (64 if a == 3 and t else 0)
                items.append(("y", T.phi[32 * a:32 * a + 32, 320 * t + off:320 * t + 320], T.phi0[0:32, 0:320 - off]))
                if off:
                    items.append(("y", T.phi[32 * a:32 * a + 32, 320 * t:320 * t + off], T.phi0[0:32, 320 - off:320]))
        dmas("dp", items, ["phi0"], ["phi"])

    def first_codes():
        quant(T.uq[:, :], T.uqs[:, :], T.ut[:, :], ["ut"], ["uq"])
        quant(T.qx[:, :], T.qxs[:, :], T.x0[:, :], ["x"], ["qx"])

    def more_constants():
        for i in range(8):
            fill(T.codv[:, 3 * i:3 * i + 3], 1024.0 * (i + 1), ["codv"], False)
        for b in range(4):
            quant(T.eh[:, 128 * b:128 * b + 128], T.ehs[:, 128 * b:128 * b + 128], T.dh[:, 3 - b:515 - b], ["dh"], ["eh%d" % b])
        op("v", vec.tensor_scalar, (T.iw[:, :], T.ir[:, :], 15, None, A.bitwise_and), ["ir"], ["iw"])
        ts(T.seg[:, :], T.iw[:, :], 0.0, A.not_equal, None, None, ["iw"], ["seg"])
        fill(T.res[:, :], 0.0, ["res"])
        fill(T.s20[:, :], 1.0, ["s20"])
        for t in range(3):
            fill(T.res[:, 20 * t:20 * t + 1], 2.0, ["res"])
            fill(T.s20[:, 20 * t:20 * t + 1], 0.0, ["s20"])
            fill(T.pt[:, 256 * t:256 * t + 1], SAME, ["pt%d" % t])

    def more_constants2():
        for n in ("ag", "uk", "ua"):
            fill(T[n][:, :], 0.0, [n])
        fill(T.keep[:, 24:32], 0.0, ["keepz"])
        for i in range(3):
            ts(T.j24[:, 8 * i:8 * i + 8], T.ones[:, 0:8], kf[:, i:i + 1], A.mult, None, None, k + ["ones"], ["j24"], False)
        ts(T.j24b[:, :], T.j24[:, :], 320.0, A.add, None, None, ["j24"], ["j24b"])
        ts(T.j16[:, 0:8], T.ir[:, 0:8], 16.0, A.mult, kf[:, 13:14], A.add, ["ir", "p16"], ["j16"])
        for a in range(1, 4):
            ts(T.j16[:, 8 * a:8 * a + 8], T.j16[:, 0:8], 96.0 * a, A.add, None, None, ["j16"], ["j16b"], False)

    def later_constants():
        ts(T.dk[:, :], T.dh[:, :], 64.0, A.mult, None, None, ["dh"], ["dk"])
        for b in range(4):
            quant(T.ek[:, 128 * b:128 * b + 128], T.eks[:, 128 * b:128 * b + 128], T.dk[:, 3 - b:515 - b], ["dk"], ["ek%d" % b])
        weights(1)
        weights(2)
        quant(T.vq[:, :], T.vqs[:, :], T.vt[:, :], ["vt"], ["vq"])

    def to_wrapped(src, dst, sem, queues, key_in, key_out):
        items = []
        for gr in range(8):
            G, h = divmod(gr, 2)
            items.append((queues[gr % len(queues)], dst[32 * G:32 * G + 32, 16 * h:16 * h + 16], src[gr:128:8, 0:32]))
        dmas(sem, items, [key_in], [key_out])

    def to_list(dst, src, o, reads, writes):
        for a in range(4):
            n = 6 if a < 3 else 2
            cp(dst[:, 6 * a:6 * a + n], src[:, o + 8 * a:o + 8 * a + n], reads, writes, False)

    for t in range(R):
        grp = [(3 * t + i) % 8 for i in range(8)]

        def words():
            mm(0, C, T.uq[:, :], T.uqs[:, :], T.qx[:, :], T.qxs[:, :], ["uq", "qx"])
            ts(T.bt[:, 0:1280:4], T.ps[:, 0:C], 0.0, A.is_gt, None, None, ["ps0"], ["bt"])
            quant(T.bq[:, :], T.bqs[:, :], T.bt[:, :], ["bt"], ["bq"])
            for h in range(2):
                o = 128 * (2 * t + h)
                mm(1 + h, C, T.cw[:, o:o + 128], T.cws[:, o:o + 128], T.bq[:, :], T.bqs[:, :], ["cw%d" % (2 * t + h), "bq"])
            act(T.w4[:, :], T.ps[:, 512:512 + C], AF.Copy, ["ps1"], ["w4"])
        if t == 0:
            merge(record(powers, lambda: weights(0), first_codes, words), record(make_places))
            spread_distances()
        else:
            words()
        tt(T.gm[:, 0:128], T.w4[:, 0:C].indirect(T.sl[:, 0:8]), T.mg[:, 0:128], A.mult, ["w4", "sl", "mg"], ["gm"])
        tt(T.gm[:, 128:176], T.w4[:, 0:C].indirect(T.sl[:, 8:11]), T.mg[:, 128:176], A.mult, ["w4", "sl2", "mg2"], ["gm2"])
        tt(T.ms[:, :], T.gm[:, 0:60], T.gm[:, 64:124], A.add, ["gm"], ["ms"])
        cp(T.msg[:, :], T.ms[:, :], ["ms"], ["msg"])
        waits("g", ["msg"], [])
        g.remote_dma(T.pw[:, 0:60], T.msg[:, 0:60], T.sem["rw"], T.sem["rl"], pid, rid, mask)
        cnt["rl"] += neng
        cnt["rw"] += neng
        note(("dma", "rl", None), ["msg"], [])
        for c in range(3):
            op("v", vec.tensor_reduce, (T.wj[:, c:c + 1], T.gm[:, 128 + 16 * c:144 + 16 * c], X, A.add), ["gm2"], ["wj"], None, False)

        def bits():
            cp(T.wji[:, :], T.wj[:, :], ["wj"], ["wji"])
            for i in range(8):
                op("v", vec.tensor_scalar, (T.ob[:, 3 * i:3 * i + 3], T.wji[:, :], 2 * i, 1, A.logical_shift_right, A.bitwise_and), ["wji"], ["ob"], None, False)
            ob, nb = T.ob[:, :], T.nb[:, :]
            ts(nb, ob, -1.0, A.mult, 1.0, A.add, ["ob"], ["nb"])
            ts(T.tp[:, 0:96:4], ob, EPS - 1.0, A.mult, 1.0, A.add, ["ob"], ["tp"])
            ts(T.tq[:, 0:96:4], ob, 1.0 - EPS, A.mult, None, None, ["ob"], ["tq"])
            ts(T.tp[:, 2:96:4], ob, 1.0 - EPS, A.mult, EPS, A.add, ["ob"], ["tp"], False)
            ts(T.tq[:, 2:96:4], nb, 1.0 - EPS, A.mult, None, None, ["nb"], ["tq"], False)
            tt(T.tp[:, 1:96:4], ob, T.codv[:, :], A.mult, ["ob", "codv"], ["tp"], False)
            tt(T.tp[:, 3:96:4], nb, T.codv[:, :], A.mult, ["nb", "codv"], ["tp"], False)
            ts(T.tq[:, 1:96:4], ob, KEPT, A.mult, None, None, ["ob"], ["tq"], False)
            ts(T.tq[:, 3:96:4], nb, KEPT, A.mult, None, None, ["nb"], ["tq"], False)
        if t == 0:
            merge(record(bits), record(more_constants))
        else:
            bits()
        for b in range(4):
            p = ["ps%d" % (4 + b)]
            mm(4 + b, C, T.eh[:, 128 * b:128 * b + 128], T.ehs[:, 128 * b:128 * b + 128], T.qx[:, :], T.qxs[:, :], ["eh%d" % b, "qx"])
            for h in range(2):
                act(T.fb[:, 640 * b + 320 * h:640 * b + 320 * h + 320], T.ps[:, 512 * (4 + b):512 * (4 + b) + C], AF.Copy, p, ["fb%d%d" % (b, h)])
            if b < 2:
                act(T.fc[:, 320 * b:320 * b + 320], T.ps[:, 512 * (4 + b):512 * (4 + b) + C], AF.Copy, p, ["fc%d" % b])
        tt(T.wm[:, :], T.ps[:, 1024:1024 + C], T.wmask[:, :], A.mult, ["ps2", "wmask"], ["wm"])
        scan(T.wsc[:, :], T.seg[:, :], T.wm[:, :], 0.0, A.mult, A.add, ["seg", "wm"], ["wsc"])
        cp(T.wl[:, :], T.wsc[:, 15:C:16], ["wsc"], ["wl"])
        note(("dma", "rw", cnt["rw"]), [], ["pw"])

        def digit(i):
            op("v", vec.tensor_scalar, (T.dd[:, 60 * i:60 * i + 60], T.vi[:, :], 4 ** i, None, A.bitwise_and), ["vi"], ["dd%d" % i])

        def double(i):
            q = slice(12 * i, 12 * i + 12)
            tt(T.sb[:, q], T.sb[:, q], T.tp[:, q], A.add, ["sb%d" % i, "tp"], ["sb%d" % i])
            n = 1 << i
            a, b = ("pt", "pv")[i % 2], ("pv", "pt")[i % 2]
            for c in range(3):
                o, x = 256 * c, 12 * i + 4 * c
                for h in range(2):
                    act(T[b][:, o + h * n:o + h * n + n], T[a][:, o:o + n], AF.Identity, [a + str(c), "sb%d" % i], [b + str(c)], h == 0,
                        scale=T.sb[:, x + 2 * h:x + 2 * h + 1], bias=T.sb[:, x + 2 * h + 1:x + 2 * h + 2])

        def drops():
            for c in range(3):
                ts(T.sm[:, 20 * c:20 * c + 20], T.pw[:, 20 * c:20 * c + 20], T.wj[:, c:c + 1], A.add, None, None, ["pw", "wj"], ["sm%d" % c])
            op("v", vec.tensor_scalar, (T.vi[:, :], T.sm[:, :], 0x5555, None, A.bitwise_and), ["sm0", "sm1", "sm2"], ["vi"])
            ts(T.ve[:, :], T.vi[:, :], 1.0, A.is_equal, None, None, ["vi"], ["ve"])
            ts(T.vz[:, :], T.vi[:, :], 0.0, A.is_equal, None, None, ["vi"], ["vz"])
            ts(T.vv[:, :], T.vi[:, :], 2.0 ** -15, A.mult, None, None, ["vi"], ["vv"])
            digit(0)
            scan(T.sc[:, :], T.s20[:, :], T.ve[:, :], 0.0, A.mult, A.max, ["s20", "ve"], ["sc"])
            tt(T.vv[:, :], T.vv[:, :], T.vz[:, :], A.max, ["vv", "vz"], ["vv"])
            for i in range(8):
                if i:
                    scan(T.sc[:, :], T.res[:, :], T.vv[:, :], 2.0, A.max, A.min, ["res", "vv"], ["sc"])
                if i < 7:
                    for c in range(3):
                        m = T.sc[:, 20 * c + 19:20 * c + 20]
                        d = T.dd[:, 60 * i + 20 * c:60 * i + 20 * c + 20]
                        o = T.kl[:, 20 * c:20 * c + 20]
                        if i:
                            ts(o, d, 2.0 ** -14, A.mult, m, A.is_gt, ["dd%d" % i, "sc"], ["kl%d" % c])
                        else:
                            ts(o, d, m, A.mult, None, None, ["dd%d" % i, "sc"], ["kl%d" % c])
                c3 = slice(grp[i], 24, 8)
                if i:
                    ts(T.keep[:, c3], T.sc[:, 19:60:20], 2.0 ** -14 * 4 ** i, A.is_lt, None, None, ["sc"], ["keep%d" % i])
                else:
                    cp(T.keep[:, c3], T.sc[:, 19:60:20], ["sc"], ["keep%d" % i])
                if i < 6:
                    digit(i + 1)
                if i:
                    double(i - 1)
                if i < 7:
                    tt(T.vv[:, :], T.vv[:, :], T.kl[:, :], A.max, ["vv", "kl0", "kl1", "kl2"], ["vv"])
                for c in range(3):
                    r = slice(12 * i + 4 * c, 12 * i + 4 * c + 4)
                    ts(T.sb[:, r], T.tq[:, r], T.keep[:, 8 * c + grp[i]:8 * c + grp[i] + 1], A.mult, None, None, ["keep%d" % i, "tq"], ["sb%d" % i], False)
            double(7)
        if t == 0:
            merge(record(drops), record(more_constants2))
        else:
            drops()
        keeps = ["keep%d" % i for i in range(8)]
        turn(T.kt[:, :], T.keep[:, :], keeps + ["keepz"], ["kt"])
        to_wrapped(T.kt, T.uk, "dk", ["y"], "kt", "uk")
        for c in range(3):
            s = slice(320 * c, 320 * c + 320)
            tt(T.nn[:, s], T.pt[:, 256 * c:256 * c + 256].indirect(T.wl[:, 0:20]), T.phi[:, s], A.add, ["pt%d" % c, "wl", "phi"], ["nn%d" % c])
            for i in (2, 3):
                z = slice(960 * (i - 2) + 320 * c, 960 * (i - 2) + 320 * c + 320)
                act(T.zz[:, z], T.nn[:, s], AF.Abs, ["nn%d" % c], ["zz%d%d" % (i, c)], bias=-1024.0 * (i + 1))
        nns = ["nn0", "nn1", "nn2"]
        act(T.zz[:, 5760:6080], T.nn[:, 640:960], AF.Abs, ["nn2"], ["zz12"], bias=-2048.0)
        for i in range(4, 8):
            act(T.zz[:, 960 * (i - 2):960 * (i - 1)], T.nn[:, :], AF.Abs, nns, ["zz%d%d" % (i, c) for c in range(3)], bias=-1024.0 * (i + 1))
        so = T.so

        def least(o, src, x, reads, w, buf=None):
            scan((so if buf is None else buf)[:, o:o + 160], src[:, x:x + 160], src[:, x + 160:x + 320], 65536.0, A.min, A.min, reads, w, False)
        for c in range(3):
            least(160 * c, T.nn, 320 * c, ["nn%d" % c], ["s0"], T.s0)
        ts(T.zv[:, 0:640], T.nn[:, 0:640], -2048.0, A.add, None, None, nns, ["zv"])
        ts(so[:, 160 * grp[0] + 159:3840:1280], T.s0[:, 159:480:160], -1024.0, A.add, None, None, ["s0"], ["so"])
        for c in range(2):
            o = 160 * (8 * c + grp[1]) + 159
            op("v", vec.tensor_reduce, (so[:, o:o + 1], T.zv[:, 320 * c:320 * c + 320], X, A.min), ["zv"], ["so"],
               {"apply_absolute_value": True}, False)

        pq = T.pq
        n32 = slice(0, 32)
        order = [
            lambda: ts(T.ac[:, 0:24], T.keep[:, 0:24], 1000.0, A.mult, None, None, keeps, ["ac0"]),
            lambda: tt(T.jk[:, :], T.ac[:, 0:24], T.j24[:, :], A.add, ["ac0", "j24"], ["jk"]),
            lambda: scan(T.us[:, :], T.seg[:, n32], T.uk[:, :], 0.0, A.mult, A.add, ["seg", "uk"], ["us"]),
            lambda: turn(T.kw[:, :], T.uk[:, :], ["uk"], ["kw"]),
            lambda: ts(T.uto[:, 0:16], T.ones[:, 0:16], T.us[:, 15:16], A.mult, None, None, ["ones", "us"], ["uto0"]),
            lambda: ts(T.uto[:, 16:32], T.ones[:, 0:16], T.us[:, 31:32], A.mult, None, None, ["ones", "us"], ["uto1"]),
            lambda: turn(T.ust[:, :], T.us[:, :], ["us"], ["ust"]),
            lambda: ts(pq[:, 96:128], T.kw[:, :], 1000.0, A.mult, -1000.0, A.add, ["kw"], ["pq4"]),
            lambda: turn(T.utt[:, :], T.uto[:, :], ["uto0", "uto1"], ["utt"]),
            lambda: scan(pq[:, n32], T.ones[:, n32], T.utt[:, :], 0.0, A.mult, A.add, ["ones", "utt"], ["pq"]),
            lambda: tt(pq[:, 32:64], T.ust[:, :], T.utt[:, :], A.subtract, ["ust", "utt"], ["pq1"]),
            lambda: ts(pq[:, 128:129], pq[:, 25:26], -1.0, A.mult, 319.0, A.add, ["pq"], ["pq2"]),
            lambda: tt(pq[:, 32:64], pq[:, 32:64], pq[:, n32], A.add, ["pq", "pq1"], ["pq1"]),
            lambda: ts(pq[:, 96:128], pq[:, 96:128], pq[:, 128:129], A.add, None, None, ["pq4", "pq2"], ["pq4"]),
            lambda: tt(pq[:, 64:96], T.j16[:, :], pq[:, 32:64], A.subtract, ["j16", "j16b", "pq1"], ["pq3"]),
            lambda: tt(pq[:, 96:128], pq[:, 96:128], pq[:, 32:64], A.add, ["pq1", "pq4"], ["pq4"]),
            lambda: tt(pq[:, 64:96], pq[:, 64:96], pq[:, 96:128], A.max, ["pq3", "pq4"], ["pq3"]),
            lambda: to_list(T.poff, pq, 64, ["pq3"], ["poff"]),
            lambda: cp(T.lw[:, 0:C].indirect(T.poff[:, 0:20]), T.jrow[:, :], ["poff", "jrow"], ["lw"]),
            lambda: tt(T.lm[:, :], T.lw[:, 0:128], T.wmask[:, 0:128], A.mult, ["lw", "wmask"], ["lm"]),
            lambda: scan(T.ls[:, :], T.seg[:, 0:128], T.lm[:, :], 0.0, A.mult, A.add, ["seg", "lm"], ["ls"]),
            lambda: cp(T.loff[:, :], T.ls[:, 15:128:16], ["ls"], ["loff"]),
        ]

        def some(n):
            for _ in range(n):
                if order:
                    order.pop(0)()
        for i in range(1, 8):
            for c in range(3):
                if i > 1:
                    least(160 * (8 * c + grp[i]), T.zz, 960 * (i - 2) + 320 * c, ["zz%d%d" % (i, c)], ["so"])
                elif c == 2:
                    least(160 * (8 * c + grp[i]), T.zz, 5760, ["zz12"], ["so"])
            some(SOME[i])
        tt(T.ac[:, 24:48], so[:, 159:3840:160], T.jk[:, :], A.add, ["so", "jk"], ["ac1"])
        some(SOME[8])
        tt(T.ag[:, 0:24], T.ac[:, 24:48], T.j24b[:, :], A.min, ["ac1", "j24b"], ["ag"])
        some(SOME[9])
        turn(T.at[:, :], T.ag[:, :], ["ag"], ["at"])
        to_wrapped(T.at, T.ua, "da", ["y", "s"], "at", "ua")
        if t < R - 1:
            for c in range(3):
                fill(T.pt[:, 256 * c:256 * c + 1], SAME, ["pt%d" % c])
        some(40)
        turn(T.aw[:, :], T.ua[:, :], ["ua"], ["aw"])
        to_list(T.aoff, T.aw, 0, ["aw"], ["aoff"])
        for b in (2, 3):
            act(T.zg[:, 320 * b - 640:320 * b - 320], T.fb[:, 640 * b:640 * b + 640].indirect(T.aoff[:, 0:20]), AF.Copy, ["fb%d0" % b, "fb%d1" % b, "aoff"], ["zg%d" % b])
        for b in range(4):
            f, z = slice(320 * b, 320 * b + 320), T.zt[:, 448 * b:448 * b + 320]
            if b < 2:
                tt(z, T.fb[:, 640 * b:640 * b + 640].indirect(T.aoff[:, 0:20]), T.fc[:, f], A.add, ["fb%d0" % b, "fb%d1" % b, "fc%d" % b, "aoff"], ["zt%d" % b])
            else:
                tt(z, T.zg[:, 320 * b - 640:320 * b - 320], T.ps[:, 512 * (4 + b):512 * (4 + b) + C], A.add, ["zg%d" % b, "ps%d" % (4 + b)], ["zt%d" % b])
            e = (T.et[:, b:512:4], z.indirect(T.loff[:, 0:8]))
            if b < 3:
                act(e[0], e[1], AF.Copy, ["zt%d" % b, "loff"], ["et%d" % b])
            else:
                cp(e[0], e[1], ["zt%d" % b, "loff"], ["et%d" % b])
        quant(T.qe[:, :], T.qes[:, :], T.et[:, :], ["et%d" % b for b in range(4)], ["qe"])
        waits("g", ["qe"], [])
        g.remote_dma(T.qa[:, 0:128].bitcast(dt.uint8), T.qe[:, 0:128].bitcast(dt.uint8), T.sem["re"], T.sem["rl"], pid, rid, mask)
        g.remote_dma(T.qas[:, 0:128], T.qes[:, 0:128], T.sem["re"], T.sem["rl"], pid, rid, mask)
        cnt["rl"] += 2 * neng
        cnt["re"] += 2 * neng
        note(("dma", "rl", None), ["qe"], [])
        note(("dma", "re", cnt["re"]), [], ["qa"])
        ts(pq[:, 132:164], pq[:, 64:96], 128.0, A.is_lt, None, None, ["pq3"], ["pq5"])
        ts(pq[:, 64:96], pq[:, 64:96], 320.0, A.add, None, None, ["pq3"], ["pq3"])
        tt(pq[:, 64:96], pq[:, 64:96], T.j16[:, :], A.subtract, ["pq3", "j16", "j16b"], ["pq3"])
        tt(pq[:, 64:96], pq[:, 64:96], pq[:, 132:164], A.mult, ["pq3", "pq5"], ["pq3"])
        tt(pq[:, 64:96], pq[:, 64:96], T.j16[:, :], A.add, ["pq3", "j16"], ["pq3"])
        to_list(T.selo, pq, 64, ["pq3"], ["selo"])
        if t == 0:
            later_constants()
        if t == R - 1:
            ts(T.am[:, 0:32], T.at[:, :], 320.0, A.is_ge, -320.0, A.mult, ["at"], ["am"])
            tt(T.am[:, 32:64], T.at[:, :], T.am[:, 0:32], A.add, ["at", "am"], ["am2"])
            dmas("do", [("y", T.al[:, 96 * a + 32 * c:96 * a + 32 * c + 32], T.am[32 * a + 8 * c:32 * a + 8 * c + 8, 32:64])
                        for a in range(4) for c in range(3 if a < 3 else 1)] + [("y", T.al[:, 320:448], T.lw[0:128:16, 0:128])], ["am2", "lw"], ["al"])
        for b in range(4):
            w = slice(128 * b, 128 * b + 128)
            mm(4 + b, 128, T.wq[:, w], T.wqs[:, w], T.qa[:, :], T.qas[:, :], ["w", "qa"], True, False)
            mm(4 + b, 128, T.ek[:, w], T.eks[:, w], T.qa[:, :], T.qas[:, :], ["ek%d" % b, "qa"], False, True)
            o, i = T.zt[:, 448 * b + 320:448 * b + 448], T.ps[:, 512 * (4 + b):512 * (4 + b) + 128]
            if b % 2 == 0:
                act(o, i, AF.Copy, ["ps%d" % (4 + b)], ["tm%d" % b], scale=0.03125)
            else:
                ts(o, i, 0.03125, A.mult, None, None, ["ps%d" % (4 + b)], ["tm%d" % b])
        for b in range(4):
            n, win = T.xs[:, b:1280:4], T.zt[:, 448 * b:448 * b + 448].indirect(T.selo[:, 0:20])
            if b % 2 == 0:
                act(n, win, AF.Copy, ["zt%d" % b, "tm%d" % b, "selo"], ["xs%d" % b])
            else:
                cp(n, win, ["zt%d" % b, "tm%d" % b, "selo"], ["xs%d" % b])
        quant(T.qx[:, :], T.qxs[:, :], T.xs[:, :], ["xs%d" % b for b in range(4)], ["qx"])
    dmas("do", [("y", T.oc[:, :], T.qx[:, 0:C].bitcast(dt.uint8))] + [("s", T.osc[4 * i:4 * i + 4, :], T.qxs[32 * i:32 * i + 4, 0:C]) for i in range(4)], ["qx"], ["oc"])
    mm(0, C, T.vq[:, :], T.vqs[:, :], T.qx[:, :], T.qxs[:, :], ["vq", "qx"])
    act(T.yo[:, :], T.ps[:, 0:C], AF.Copy, ["ps0"], ["yo"])
    dmas("do", [("y", T.y[:, :], T.yo[:, :])], ["yo"], ["y"])
    for s in SEMAPHORES:
        if seen["y"].get(s, 0) < cnt[s]:
            need("y", ("end", s, cnt[s]))
